import numpy as np
import ml_dtypes


def mxq(x, axis, fmt="e4m3"):
    dtype, down = {"e4m3": (ml_dtypes.float8_e4m3fn, 7), "e5m2": (ml_dtypes.float8_e5m2, 14)}[fmt]
    v = np.moveaxis(np.asarray(x, np.float32).astype(ml_dtypes.bfloat16).astype(np.float64), axis, -1)
    blocks = v.reshape(v.shape[:-1] + (-1, 32))
    amax = np.abs(blocks).max(-1, keepdims=True)
    byte = np.maximum(np.where(amax > 0, np.frexp(amax)[1] - 1 + 127, 0) - down, 1)
    scale = np.exp2(byte - 127.0)
    codes = (blocks / scale).astype(np.float32).astype(dtype).astype(np.float64)
    return np.moveaxis((codes * scale).reshape(v.shape), -1, axis)


WIDE = False


def mx_kscale(k):
    if not WIDE:
        return np.ones(k)
    levels = np.array([10, -10, 5, -5, 0])
    if k % 512:
        return np.exp2(np.random.permutation(np.resize(levels, k // 32))).repeat(32)
    a = np.empty((k // 512, 16))
    for p in range(k // 512):
        a[p, :8] = np.random.permutation(np.resize(levels, 8))
        for g in range(8):
            far = levels[np.abs(levels - a[p, g]) >= 10]
            a[p, g + 8] = far[np.random.randint(len(far))]
    return np.exp2(a.ravel()).repeat(32)


def f64(x):
    return np.asarray(x).astype(np.float64)


def striped(idx):
    return np.tile(idx.reshape(-1, 16).T, (8, 1)).astype(np.uint16)


def unstriped(offs):
    return offs[:16].T.reshape(-1).astype(np.int64)


E2M1 = np.array([0.0, 0.5, 1.0, 1.5, 2.0, 3.0, 4.0, 6.0, -0.0, -0.5, -1.0, -1.5, -2.0, -3.0, -4.0, -6.0])


def pack_weight(w, fmt):
    k, n = w.shape
    w = f64(np.asarray(w, np.float32).astype(ml_dtypes.bfloat16)).reshape(k // 32, 32, n)
    amax = np.abs(w).max(1)
    if fmt == "e4m3":
        byte = np.frexp(amax)[1] - 1 + 127 - 7
    else:
        mant, ex = np.frexp(amax / 6.0)
        byte = np.where(mant > 0.5, ex, ex - 1) + 127
    byte = np.clip(np.where(amax > 0, byte, 1), 1, 254)
    scaled = (w * np.exp2(127.0 - byte)[:, None, :]).reshape(k, n).astype(np.float32)
    by_word = np.ascontiguousarray(scaled.reshape(k // 512, 128, 4, n).transpose(0, 1, 3, 2))
    if fmt == "e4m3":
        words = by_word.astype(ml_dtypes.float8_e4m3fn).view(np.uint8)
    else:
        c = by_word.astype(ml_dtypes.float4_e2m1fn).view(np.uint8) & 0xF
        words = (c[..., 0::2] | (c[..., 1::2] << 4)).reshape(k // 512, 128, 2 * n)
    return np.ascontiguousarray(words), np.ascontiguousarray(byte.astype(np.uint8).reshape(k // 512, 16, n))


def unpack_weight(words, scales, fmt):
    g, _, n = scales.shape
    words = np.ascontiguousarray(words).reshape(g, 128, n, -1)
    if fmt == "e4m3":
        vals = words.view(ml_dtypes.float8_e4m3fn).astype(np.float64)
    else:
        nib = np.empty((g, 128, n, 4), np.uint8)
        nib[..., 0::2] = words & 0xF
        nib[..., 1::2] = words >> 4
        vals = E2M1[nib]
    vals = vals * np.repeat(np.exp2(scales.astype(np.float64) - 127.0), 8, axis=1)[..., None]
    return vals.transpose(0, 1, 3, 2).reshape(g * 512, n)


K, T, E, C, N, TOP = 1024, 768, 12, 256, 128, 4


def by_expert(wq, xq):
    return np.concatenate([wq[e].T @ xq[:, e * C:(e + 1) * C] for e in range(E)], axis=1)


def setup_inputs():
    n = np.random.standard_normal
    s = mx_kscale(K)
    deal = np.repeat(np.arange(E), C).reshape(TOP, T)[:, np.random.permutation(T)]
    deal = np.take_along_axis(deal, np.argsort(np.random.rand(TOP, T), axis=0), axis=0)
    for _ in range(8):
        s_, t_ = np.random.permutation(T).reshape(2, -1); r = np.random.randint(TOP, size=T // 2); x, y = deal[r, s_].copy(), deal[r, t_].copy()
        ok = ~((deal[:, s_] == y).any(0) | (deal[:, t_] == x).any(0)); deal[r[ok], s_[ok]] = y[ok]; deal[r[ok], t_[ok]] = x[ok]
    order = np.lexsort((np.random.rand(TOP * T), deal.reshape(-1)))
    slot_token = order % T; pos = np.empty(TOP * T, np.int64); pos[order] = np.arange(TOP * T); pos = pos.reshape(TOP, T)
    g = np.random.uniform(0.5, 1.5, (TOP, T)); g = g / g.sum(0)
    x = pack_weight(n((K, T)) * s[:, None], "e4m3")
    wq = [pack_weight(m, "e2m1") for m in n((E, K, N)) / np.sqrt(K) / s[None, :, None]]
    wk = [pack_weight(m, "e4m3") for m in n((E, K, N)) / np.sqrt(K) / s[None, :, None]]
    return {
        "x_words": x[0],
        "x_scales": x[1],
        "wq_words": np.stack([m[0] for m in wq]),
        "wq_scales": np.stack([m[1] for m in wq]),
        "wk_words": np.stack([m[0] for m in wk]),
        "wk_scales": np.stack([m[1] for m in wk]),
        "wv": (n((E, K, N)) / np.sqrt(K) / s[None, :, None]).astype(np.float32),
        "bias": (0.3 * n((3 * N, E))).astype(np.float32),
        "gate": np.stack([np.tile(r, (128, 1)) for r in g]).astype(np.float32),
        "offs": striped(slot_token),
        "pos1": striped(pos[0]),
        "pos2": striped(pos[1]),
        "pos3": striped(pos[2]),
        "pos4": striped(pos[3]),
    }


def reference(x_words, x_scales, wq_words, wq_scales, wk_words, wk_scales, wv, bias, gate, offs, pos1, pos2, pos3, pos4):
    wq = np.stack([unpack_weight(wq_words[e], wq_scales[e], "e2m1") for e in range(E)])
    wk = np.stack([unpack_weight(wk_words[e], wk_scales[e], "e4m3") for e in range(E)])
    wvq = mxq(f64(wv), 1, "e4m3")
    idx = unstriped(offs)
    xq = unpack_weight(x_words, x_scales, "e4m3")[:, idx]
    y = np.concatenate([by_expert(w, xq) for w in (wq, wk, wvq)])
    y = y + np.repeat(f64(bias), C, axis=1)
    out = sum(f64(gate[r, :1]) * y[:, unstriped(p)] for r, p in enumerate((pos1, pos2, pos3, pos4)))
    return out

@@ -1,0 +1,215 @@
+from contextlib import ExitStack
+
+import concourse.mybir as mybir
+from concourse.masks import make_identity
+
+K, T, E, C, N, TOP = 1024, 768, 12, 256, 128, 4
+FLOPS = 2 * E * C * K * 3 * N
+
+F32 = mybir.dt.float32
+BF16 = mybir.dt.bfloat16
+I32 = mybir.dt.int32
+U32 = mybir.dt.uint32
+U16 = mybir.dt.uint16
+U8 = mybir.dt.uint8
+FP8X4 = mybir.dt.float8_e4m3fn_x4
+FP4X4 = mybir.dt.float4_e2m1fn_x4
+MULT = mybir.AluOpType.mult
+ADD = mybir.AluOpType.add
+IDENTITY = mybir.ActivationFunctionType.Identity
+
+P = 128
+PACK = 4
+PASSES = K // (P * PACK)
+SLOTS = E * C
+LIST_ROWS = 16
+WORD_WINDOW = 2 * T
+SCALE_WINDOW = 2048
+SCALE_CUTS = (0, 1536, 3072)
+WORD_CUTS = (0, 1024, 2048, 2816, 3072)
+HALF = T // 2
+Q_ROWS, K_ROWS, V_ROWS = 0, 1, 2
+
+
+def tile_moe_qkv_kernel(
+    tc, x_words, x_scales, wq_words, wq_scales, wk_words, wk_scales, wv, bias, gate, offs, pos1, pos2, pos3, pos4, out
+):
+    nc = tc.nc
+    with ExitStack() as ctx:
+        keep = ctx.enter_context(tc.tile_pool(name="keep", bufs=1))
+        stage = ctx.enter_context(tc.tile_pool(name="stage", bufs=2))
+        psum_acc = ctx.enter_context(tc.psum_pool(name="psum_acc", bufs=4))
+        psum = ctx.enter_context(tc.psum_pool(name="psum", bufs=2))
+
+        offs_sb = keep.tile([P, SLOTS // LIST_ROWS], U16, name="offs_sb")
+        pos_sb = [keep.tile([P, T // LIST_ROWS], U16, name="pos_sb%d" % r) for r in range(TOP)]
+        x_scale_sb = keep.tile([P, SCALE_WINDOW], U8, name="x_scale_sb", align_bytes=64)
+        x_word_sb = keep.tile([P, T + WORD_WINDOW], I32, name="x_word_sb", align_bytes=64)
+        slot_words = [keep.tile([P, SLOTS], U32, name="slot_words%d" % s, align_bytes=64) for s in range(PASSES)]
+        slot_scales = keep.tile([P, SLOTS], U8, name="slot_scales", align_bytes=64)
+        slot_scales_low = keep.tile([P, SLOTS], U8, name="slot_scales_low", align_bytes=64)
+        wq_word_sb = keep.tile([P, E * PASSES, 2 * N], U8, name="wq_word_sb", align_bytes=64)
+        wk_word_sb = keep.tile([P, E * PASSES, N], I32, name="wk_word_sb", align_bytes=64)
+        wv_word_sb = keep.tile([P, E * PASSES, N], U32, name="wv_word_sb", align_bytes=64)
+        wq_scale_sb = keep.tile([P, E * PASSES, N], U8, name="wq_scale_sb", align_bytes=64)
+        wk_scale_sb = keep.tile([P, E * PASSES, N], U8, name="wk_scale_sb", align_bytes=64)
+        wv_scale_sb = keep.tile([P, E * PASSES, N], U8, name="wv_scale_sb", align_bytes=64)
+        wv_raw = keep.tile([P, E * PASSES, PACK, N], F32, name="wv_raw")
+        wv_bf = keep.tile([P, E * PASSES, N, PACK], BF16, name="wv_bf", align_bytes=64)
+        bias_sb = keep.tile([P, 3, E], F32, name="bias_sb")
+        gate_sb = keep.tile([P, TOP, T], F32, name="gate_sb")
+        slot_out = [keep.tile([P, SLOTS], F32, name="slot_out%d" % j) for j in range(3)]
+        ident = keep.tile([P, P], F32, name="ident")
+
+        nc.vector.memset(x_scale_sb[:].bitcast(I32), 0)
+        nc.vector.memset(wk_scale_sb[:].rearrange("p g n -> p (g n)").bitcast(I32), 0)
+        nc.vector.memset(wq_scale_sb[:].rearrange("p g n -> p (g n)").bitcast(I32), 0)
+        nc.vector.memset(x_word_sb[:, PASSES * T :], 0)
+        nc.vector.memset(slot_scales_low[:].bitcast(I32), 0)
+        make_identity(nc, ident[:])
+
+        def load_wv(e):
+            nc.sync.dma_start(
+                out=wv_raw[:, PASSES * e : PASSES * (e + 1)].rearrange("p s j n -> p s (j n)"),
+                in_=wv[e].rearrange("(s p j) n -> p s (j n)", s=PASSES, j=PACK),
+            )
+
+        def load_weight_scales(plane, scales):
+            rows = scales.rearrange("e s (q j) n -> q j (e s) n", j=4)
+            for q in range(4):
+                nc.sync.dma_start(out=plane[32 * q : 32 * q + 4].bitcast(I32), in_=rows[q].bitcast(I32))
+
+        wk_rows = wk_words.rearrange("e s p n d -> p (e s) (n d)").bitcast(I32)
+
+        def load_wk(e0, e1):
+            group = slice(PASSES * e0, PASSES * e1)
+            nc.sync.dma_start(out=wk_word_sb[:, group], in_=wk_rows[:, group])
+
+        def load_gate(r0, r1):
+            nc.sync.dma_start(out=gate_sb[:, r0:r1], in_=gate[r0:r1].rearrange("r p t -> p r t"))
+
+        nc.sync.dma_start(offs_sb[:], offs)
+        for q in range(4):
+            nc.sync.dma_start(
+                out=x_scale_sb[32 * q : 32 * q + 8, 0:T].bitcast(I32), in_=x_scales[:, 4 * q : 4 * q + 4].bitcast(I32)
+            )
+        nc.sync.dma_start(
+            out=x_word_sb[:, 0 : PASSES * T].rearrange("p (s t) -> p s t", s=PASSES),
+            in_=x_words.rearrange("s p t d -> p s (t d)").bitcast(I32),
+        )
+        for e in (0, 1, 2):
+            load_wv(e)
+        nc.sync.dma_start(out=bias_sb[:], in_=bias.rearrange("(j p) e -> p j e", p=P))
+        load_weight_scales(wk_scale_sb, wk_scales)
+        load_weight_scales(wq_scale_sb, wq_scales)
+        for third in range(3):
+            load_wk(4 * third, 4 * third + 4)
+            load_wv(3 + 2 * third)
+            load_wv(4 + 2 * third)
+        for r, pos in enumerate((pos1, pos2, pos3, pos4)):
+            nc.sync.dma_start(pos_sb[r][:], pos)
+        load_gate(0, 2)
+        nc.sync.dma_start(out=wq_word_sb[:].bitcast(I32), in_=wq_words.rearrange("e s p b -> p (e s) b").bitcast(I32))
+        load_gate(2, 4)
+        for e in (9, 10, 11):
+            load_wv(e)
+
+        def entries(list_tile, first, last):
+            return list_tile[:, first // LIST_ROWS : last // LIST_ROWS]
+
+        for first, last in zip(SCALE_CUTS, SCALE_CUTS[1:]):
+            nc.vector.tensor_copy(slot_scales[:, first:last], x_scale_sb[:].indirect(entries(offs_sb, first, last)))
+        for q in range(4):
+            nc.gpsimd.dma_start(
+                out=slot_scales_low[32 * q : 32 * q + 4].bitcast(I32),
+                in_=slot_scales[32 * q + 4 : 32 * q + 8].bitcast(I32),
+            )
+        for first, last in zip(WORD_CUTS, WORD_CUTS[1:]):
+            for s in range(PASSES):
+                window = x_word_sb[:, s * T : s * T + WORD_WINDOW].bitcast(U32)
+                nc.vector.tensor_copy(slot_words[s][:, first:last], window.indirect(entries(offs_sb, first, last)))
+
+        def project(j, e, words, scales, dtype, width, token_scales):
+            acc = psum_acc.tile([P, C], F32, name="acc")
+            for u0 in range(0, C, width):
+                slots = slice(e * C + u0, e * C + u0 + width)
+                for s in range(PASSES):
+                    nc.tensor.matmul_mx(
+                        out=acc[:, u0 : u0 + width],
+                        lhsT=words[:, PASSES * e + s].bitcast(dtype),
+                        lhsT_scale=scales[:, PASSES * e + s],
+                        rhs=slot_words[s][:, slots].bitcast(FP8X4),
+                        rhs_scale=token_scales[s][:, slots],
+                        start=(s == 0),
+                        stop=(s == PASSES - 1),
+                    )
+            nc.scalar.activation(slot_out[j][:, e * C : (e + 1) * C], acc[:], IDENTITY, bias=bias_sb[:, j, e : e + 1])
+
+        packed_planes = (slot_scales[:], slot_scales[4:P])
+        low_planes = (slot_scales[:], slot_scales_low[:])
+        for e in range(E):
+            project(K_ROWS, e, wk_word_sb, wk_scale_sb, FP8X4, C, packed_planes)
+        for e in range(E):
+            project(Q_ROWS, e, wq_word_sb, wq_scale_sb, FP4X4, C // 2, low_planes)
+        for g in range(E * PASSES):
+            nc.scalar.copy(
+                wv_bf[:, g].rearrange("p (c i) j -> p c j i", i=4), wv_raw[:, g].rearrange("p j (c i) -> p c j i", i=4)
+            )
+        for e0 in range(0, E, 2):
+            group = slice(PASSES * e0, PASSES * (e0 + 2))
+            nc.vector.quantize_mx(
+                out=wv_word_sb[:, group].rearrange("p g n -> p (g n)").bitcast(FP8X4),
+                scales=wv_scale_sb[:, group].rearrange("p g n -> p (g n)"),
+                in_=wv_bf[:, group].rearrange("p g n j -> p (g n j)"),
+            )
+        for e in range(E):
+            project(V_ROWS, e, wv_word_sb, wv_scale_sb, FP8X4, C, packed_planes)
+
+        def fetch(j, r, t0, t1):
+            nc.vector.tensor_tensor(
+                weighted[j][r][:, t0:t1], slot_out[j][:].indirect(entries(pos_sb[r], t0, t1)), gate_sb[:, r, t0:t1], MULT
+            )
+
+        def add_up(j, t0, terms):
+            turned = psum.tile([P, HALF], F32, name="turned")
+            for b0 in range(0, HALF, P):
+                for r in range(terms):
+                    nc.tensor.matmul(
+                        turned[:, b0 : b0 + P],
+                        weighted[j][r][:, t0 + b0 : t0 + b0 + P],
+                        ident[:],
+                        start=(r == 0),
+                        stop=(r == terms - 1),
+                        is_transpose=True,
+                    )
+            turned_sb = stage.tile([P, HALF], F32, name="turned_sb")
+            nc.scalar.copy(turned_sb[:], turned[:])
+            total = psum.tile([P, HALF], F32, name="total")
+            for b0 in range(0, HALF, P):
+                nc.tensor.transpose(total[:, b0 : b0 + P], turned_sb[:, b0 : b0 + P], ident[:])
+            return total
+
+        def store(j, t0, result):
+            nc.sync.dma_start(out=out[j * N : (j + 1) * N, t0 : t0 + HALF], in_=result[:])
+
+        weighted = {}
+        for j in (K_ROWS, Q_ROWS):
+            weighted[j] = [stage.tile([P, T], F32, name="weighted%d" % r) for r in range(TOP)]
+            for r in range(TOP):
+                fetch(j, r, 0, T)
+            for t0 in (0, HALF):
+                total = add_up(j, t0, TOP)
+                result = stage.tile([P, HALF], F32, name="result")
+                nc.scalar.copy(result[:], total[:])
+                store(j, t0, result)
+        weighted[V_ROWS] = [stage.tile([P, T], F32, name="weighted%d" % r) for r in range(TOP)]
+        partial = []
+        for t0 in (0, HALF):
+            for r in range(TOP - 1):
+                fetch(V_ROWS, r, t0, t0 + HALF)
+            partial.append(add_up(V_ROWS, t0, TOP - 1))
+        for t0, total in zip((0, HALF), partial):
+            fetch(V_ROWS, TOP - 1, t0, t0 + HALF)
+            result = stage.tile([P, HALF], F32, name="result")
+            nc.vector.tensor_tensor(result[:], total[:], weighted[V_ROWS][TOP - 1][:, t0 : t0 + HALF], ADD)
+            store(V_ROWS, t0, result)

@@ -23,11 +23,11 @@ PACK = 4
 PASSES = K // (P * PACK)
 SLOTS = E * C
 LIST_ROWS = 16
-WORD_WINDOW = 2 * T
-SCALE_WINDOW = 2048
-SCALE_CUTS = (0, 1536, 3072)
-WORD_CUTS = (0, 1024, 2048, 2816, 3072)
-HALF = T // 2
+WINDOW = 2048
+HALF_SLOTS = SLOTS // 2
+GATE_SLOT = 6
+EVEN_PIECES = ((0, 384), (384, T))
+LAST_PIECES = ((0, 512), (512, T))
 Q_ROWS, K_ROWS, V_ROWS = 0, 1, 2
 
 
@@ -38,13 +38,14 @@ def tile_moe_qkv_kernel(
     with ExitStack() as ctx:
         keep = ctx.enter_context(tc.tile_pool(name="keep", bufs=1))
         stage = ctx.enter_context(tc.tile_pool(name="stage", bufs=2))
+        terms_pool = ctx.enter_context(tc.tile_pool(name="terms", bufs=3))
         psum_acc = ctx.enter_context(tc.psum_pool(name="psum_acc", bufs=4))
         psum = ctx.enter_context(tc.psum_pool(name="psum", bufs=2))
 
         offs_sb = keep.tile([P, SLOTS // LIST_ROWS], U16, name="offs_sb")
         pos_sb = [keep.tile([P, T // LIST_ROWS], U16, name="pos_sb%d" % r) for r in range(TOP)]
-        x_scale_sb = keep.tile([P, SCALE_WINDOW], U8, name="x_scale_sb", align_bytes=64)
-        x_word_sb = keep.tile([P, T + WORD_WINDOW], I32, name="x_word_sb", align_bytes=64)
+        x_scale_sb = keep.tile([P, WINDOW], U8, name="x_scale_sb", align_bytes=64)
+        x_word_sb = keep.tile([P, T + WINDOW], I32, name="x_word_sb", align_bytes=64)
         slot_words = [keep.tile([P, SLOTS], U32, name="slot_words%d" % s, align_bytes=64) for s in range(PASSES)]
         slot_scales = keep.tile([P, SLOTS], U8, name="slot_scales", align_bytes=64)
         slot_scales_low = keep.tile([P, SLOTS], U8, name="slot_scales_low", align_bytes=64)
@@ -54,23 +55,23 @@ def tile_moe_qkv_kernel(
         wq_scale_sb = keep.tile([P, E * PASSES, N], U8, name="wq_scale_sb", align_bytes=64)
         wk_scale_sb = keep.tile([P, E * PASSES, N], U8, name="wk_scale_sb", align_bytes=64)
         wv_scale_sb = keep.tile([P, E * PASSES, N], U8, name="wv_scale_sb", align_bytes=64)
-        wv_raw = keep.tile([P, E * PASSES, PACK, N], F32, name="wv_raw")
+        wv_raw = [keep.tile([P, PASSES, PACK, N], F32, name="wv_raw%d" % e, tag="stream%d" % e) for e in range(E)]
         wv_bf = keep.tile([P, E * PASSES, N, PACK], BF16, name="wv_bf", align_bytes=64)
         bias_sb = keep.tile([P, 3, E], F32, name="bias_sb")
-        gate_sb = keep.tile([P, TOP, T], F32, name="gate_sb")
         slot_out = [keep.tile([P, SLOTS], F32, name="slot_out%d" % j) for j in range(3)]
         ident = keep.tile([P, P], F32, name="ident")
 
-        nc.vector.memset(x_scale_sb[:].bitcast(I32), 0)
-        nc.vector.memset(wk_scale_sb[:].rearrange("p g n -> p (g n)").bitcast(I32), 0)
-        nc.vector.memset(wq_scale_sb[:].rearrange("p g n -> p (g n)").bitcast(I32), 0)
+        nc.gpsimd.memset(x_scale_sb[:, 0:T].bitcast(I32), 0)
+        nc.gpsimd.memset(wk_scale_sb[:].rearrange("p g n -> p (g n)").bitcast(I32), 0)
+        nc.gpsimd.memset(wq_scale_sb[:].rearrange("p g n -> p (g n)").bitcast(I32), 0)
         nc.vector.memset(x_word_sb[:, PASSES * T :], 0)
-        nc.vector.memset(slot_scales_low[:].bitcast(I32), 0)
+        nc.vector.memset(x_scale_sb[:, T:].bitcast(I32), 0)
+        nc.gpsimd.memset(slot_scales_low[:].bitcast(I32), 0)
         make_identity(nc, ident[:])
 
         def load_wv(e):
             nc.sync.dma_start(
-                out=wv_raw[:, PASSES * e : PASSES * (e + 1)].rearrange("p s j n -> p s (j n)"),
+                out=wv_raw[e][:].rearrange("p s j n -> p s (j n)"),
                 in_=wv[e].rearrange("(s p j) n -> p s (j n)", s=PASSES, j=PACK),
             )
 
@@ -85,49 +86,56 @@ def tile_moe_qkv_kernel(
             group = slice(PASSES * e0, PASSES * e1)
             nc.sync.dma_start(out=wk_word_sb[:, group], in_=wk_rows[:, group])
 
-        def load_gate(r0, r1):
-            nc.sync.dma_start(out=gate_sb[:, r0:r1], in_=gate[r0:r1].rearrange("r p t -> p r t"))
-
+        word_start = (T, 0)
         nc.sync.dma_start(offs_sb[:], offs)
+        for s in range(PASSES):
+            nc.sync.dma_start(
+                out=x_word_sb[:, word_start[s] : word_start[s] + T],
+                in_=x_words[s].rearrange("p t d -> p (t d)").bitcast(I32),
+            )
         for q in range(4):
             nc.sync.dma_start(
                 out=x_scale_sb[32 * q : 32 * q + 8, 0:T].bitcast(I32), in_=x_scales[:, 4 * q : 4 * q + 4].bitcast(I32)
             )
-        nc.sync.dma_start(
-            out=x_word_sb[:, 0 : PASSES * T].rearrange("p (s t) -> p s t", s=PASSES),
-            in_=x_words.rearrange("s p t d -> p s (t d)").bitcast(I32),
-        )
-        for e in (0, 1, 2):
+        for e in range(E):
             load_wv(e)
         nc.sync.dma_start(out=bias_sb[:], in_=bias.rearrange("(j p) e -> p j e", p=P))
         load_weight_scales(wk_scale_sb, wk_scales)
         load_weight_scales(wq_scale_sb, wq_scales)
-        for third in range(3):
-            load_wk(4 * third, 4 * third + 4)
-            load_wv(3 + 2 * third)
-            load_wv(4 + 2 * third)
+        for e0 in (0, E // 2):
+            load_wk(e0, e0 + E // 2)
         for r, pos in enumerate((pos1, pos2, pos3, pos4)):
             nc.sync.dma_start(pos_sb[r][:], pos)
-        load_gate(0, 2)
         nc.sync.dma_start(out=wq_word_sb[:].bitcast(I32), in_=wq_words.rearrange("e s p b -> p (e s) b").bitcast(I32))
-        load_gate(2, 4)
-        for e in (9, 10, 11):
-            load_wv(e)
 
         def entries(list_tile, first, last):
             return list_tile[:, first // LIST_ROWS : last // LIST_ROWS]
 
-        for first, last in zip(SCALE_CUTS, SCALE_CUTS[1:]):
+        def gather_words(first):
+            for s in range(PASSES):
+                window = x_word_sb[:, word_start[s] : word_start[s] + WINDOW].bitcast(U32)
+                last = first + HALF_SLOTS
+                nc.vector.tensor_copy(slot_words[s][:, first:last], window.indirect(entries(offs_sb, first, last)))
+
+        gather_words(0)
+        for first in (0, HALF_SLOTS):
+            last = first + HALF_SLOTS
             nc.vector.tensor_copy(slot_scales[:, first:last], x_scale_sb[:].indirect(entries(offs_sb, first, last)))
+        gather_words(HALF_SLOTS)
         for q in range(4):
-            nc.gpsimd.dma_start(
+            nc.sync.dma_start(
                 out=slot_scales_low[32 * q : 32 * q + 4].bitcast(I32),
                 in_=slot_scales[32 * q + 4 : 32 * q + 8].bitcast(I32),
             )
-        for first, last in zip(WORD_CUTS, WORD_CUTS[1:]):
-            for s in range(PASSES):
-                window = x_word_sb[:, s * T : s * T + WORD_WINDOW].bitcast(U32)
-                nc.vector.tensor_copy(slot_words[s][:, first:last], window.indirect(entries(offs_sb, first, last)))
+
+        for g in range(E * PASSES):
+            nc.scalar.copy(
+                wv_bf[:, g].rearrange("p (c i) j -> p c j i", i=4),
+                wv_raw[g // PASSES][:, g % PASSES].rearrange("p j (c i) -> p c j i", i=4),
+            )
+        gate_sb = [keep.tile([P, T], F32, name="gate_sb%d" % r, tag="stream%d" % (GATE_SLOT + r)) for r in range(TOP)]
+        for r in range(TOP):
+            nc.sync.dma_start(out=gate_sb[r][:], in_=gate[r])
 
         def project(j, e, words, scales, dtype, width, token_scales):
             acc = psum_acc.tile([P, C], F32, name="acc")
@@ -151,10 +159,6 @@ def tile_moe_qkv_kernel(
             project(K_ROWS, e, wk_word_sb, wk_scale_sb, FP8X4, C, packed_planes)
         for e in range(E):
             project(Q_ROWS, e, wq_word_sb, wq_scale_sb, FP4X4, C // 2, low_planes)
-        for g in range(E * PASSES):
-            nc.scalar.copy(
-                wv_bf[:, g].rearrange("p (c i) j -> p c j i", i=4), wv_raw[:, g].rearrange("p j (c i) -> p c j i", i=4)
-            )
         for e0 in range(0, E, 2):
             group = slice(PASSES * e0, PASSES * (e0 + 2))
             nc.vector.quantize_mx(
@@ -167,12 +171,12 @@ def tile_moe_qkv_kernel(
 
         def fetch(j, r, t0, t1):
             nc.vector.tensor_tensor(
-                weighted[j][r][:, t0:t1], slot_out[j][:].indirect(entries(pos_sb[r], t0, t1)), gate_sb[:, r, t0:t1], MULT
+                weighted[j][r][:, t0:t1], slot_out[j][:].indirect(entries(pos_sb[r], t0, t1)), gate_sb[r][:, t0:t1], MULT
             )
 
-        def add_up(j, t0, terms):
-            turned = psum.tile([P, HALF], F32, name="turned")
-            for b0 in range(0, HALF, P):
+        def add_up(j, t0, t1, terms):
+            turned = psum.tile([P, t1 - t0], F32, name="turned")
+            for b0 in range(0, t1 - t0, P):
                 for r in range(terms):
                     nc.tensor.matmul(
                         turned[:, b0 : b0 + P],
@@ -182,34 +186,34 @@ def tile_moe_qkv_kernel(
                         stop=(r == terms - 1),
                         is_transpose=True,
                     )
-            turned_sb = stage.tile([P, HALF], F32, name="turned_sb")
+            turned_sb = stage.tile([P, t1 - t0], F32, name="turned_sb")
             nc.scalar.copy(turned_sb[:], turned[:])
-            total = psum.tile([P, HALF], F32, name="total")
-            for b0 in range(0, HALF, P):
+            total = psum.tile([P, t1 - t0], F32, name="total")
+            for b0 in range(0, t1 - t0, P):
                 nc.tensor.transpose(total[:, b0 : b0 + P], turned_sb[:, b0 : b0 + P], ident[:])
             return total
 
-        def store(j, t0, result):
-            nc.sync.dma_start(out=out[j * N : (j + 1) * N, t0 : t0 + HALF], in_=result[:])
+        def store(j, t0, t1, result):
+            nc.sync.dma_start(out=out[j * N : (j + 1) * N, t0:t1], in_=result[:])
 
         weighted = {}
         for j in (K_ROWS, Q_ROWS):
-            weighted[j] = [stage.tile([P, T], F32, name="weighted%d" % r) for r in range(TOP)]
+            weighted[j] = [terms_pool.tile([P, T], F32, name="weighted%d" % r) for r in range(TOP)]
             for r in range(TOP):
                 fetch(j, r, 0, T)
-            for t0 in (0, HALF):
-                total = add_up(j, t0, TOP)
-                result = stage.tile([P, HALF], F32, name="result")
+            for t0, t1 in EVEN_PIECES:
+                total = add_up(j, t0, t1, TOP)
+                result = stage.tile([P, t1 - t0], F32, name="result")
                 nc.scalar.copy(result[:], total[:])
-                store(j, t0, result)
-        weighted[V_ROWS] = [stage.tile([P, T], F32, name="weighted%d" % r) for r in range(TOP)]
+                store(j, t0, t1, result)
+        weighted[V_ROWS] = [terms_pool.tile([P, T], F32, name="weighted%d" % r) for r in range(TOP)]
         partial = []
-        for t0 in (0, HALF):
+        for t0, t1 in LAST_PIECES:
             for r in range(TOP - 1):
-                fetch(V_ROWS, r, t0, t0 + HALF)
-            partial.append(add_up(V_ROWS, t0, TOP - 1))
-        for t0, total in zip((0, HALF), partial):
-            fetch(V_ROWS, TOP - 1, t0, t0 + HALF)
-            result = stage.tile([P, HALF], F32, name="result")
-            nc.vector.tensor_tensor(result[:], total[:], weighted[V_ROWS][TOP - 1][:, t0 : t0 + HALF], ADD)
-            store(V_ROWS, t0, result)
+                fetch(V_ROWS, r, t0, t1)
+            partial.append(add_up(V_ROWS, t0, t1, TOP - 1))
+        for (t0, t1), total in zip(LAST_PIECES, partial):
+            fetch(V_ROWS, TOP - 1, t0, t1)
+            result = stage.tile([P, t1 - t0], F32, name="result")
+            nc.vector.tensor_tensor(result[:], total[:], weighted[V_ROWS][TOP - 1][:, t0:t1], ADD)
+            store(V_ROWS, t0, t1, result)

@@ -25,7 +25,9 @@ SLOTS = E * C
 LIST_ROWS = 16
 WINDOW = 2048
 HALF_SLOTS = SLOTS // 2
-GATE_SLOT = 6
+BANKS = 8
+EARLY = 9
+W_ROW = PASSES * PACK * N
 EVEN_PIECES = ((0, 384), (384, T))
 LAST_PIECES = ((0, 512), (512, T))
 Q_ROWS, K_ROWS, V_ROWS = 0, 1, 2
@@ -39,24 +41,24 @@ def tile_moe_qkv_kernel(
         keep = ctx.enter_context(tc.tile_pool(name="keep", bufs=1))
         stage = ctx.enter_context(tc.tile_pool(name="stage", bufs=2))
         terms_pool = ctx.enter_context(tc.tile_pool(name="terms", bufs=3))
-        psum_acc = ctx.enter_context(tc.psum_pool(name="psum_acc", bufs=4))
-        psum = ctx.enter_context(tc.psum_pool(name="psum", bufs=2))
+        psum = ctx.enter_context(tc.psum_pool(name="psum", bufs=1))
 
         offs_sb = keep.tile([P, SLOTS // LIST_ROWS], U16, name="offs_sb")
         pos_sb = [keep.tile([P, T // LIST_ROWS], U16, name="pos_sb%d" % r) for r in range(TOP)]
-        x_scale_sb = keep.tile([P, WINDOW], U8, name="x_scale_sb", align_bytes=64)
+        x_scale_sb = keep.tile([P, WINDOW], U8, name="x_scale_sb", tag="x_scales_then_late", align_bytes=64)
         x_word_sb = keep.tile([P, T + WINDOW], I32, name="x_word_sb", align_bytes=64)
         slot_words = [keep.tile([P, SLOTS], U32, name="slot_words%d" % s, align_bytes=64) for s in range(PASSES)]
         slot_scales = keep.tile([P, SLOTS], U8, name="slot_scales", align_bytes=64)
         slot_scales_low = keep.tile([P, SLOTS], U8, name="slot_scales_low", align_bytes=64)
-        wq_word_sb = keep.tile([P, E * PASSES, 2 * N], U8, name="wq_word_sb", align_bytes=64)
+        wq_word_sb = keep.tile([P, E * PASSES, 2 * N], U8, name="wq_word_sb", tag="wq_then_late", align_bytes=64)
         wk_word_sb = keep.tile([P, E * PASSES, N], I32, name="wk_word_sb", align_bytes=64)
         wv_word_sb = keep.tile([P, E * PASSES, N], U32, name="wv_word_sb", align_bytes=64)
         wq_scale_sb = keep.tile([P, E * PASSES, N], U8, name="wq_scale_sb", align_bytes=64)
         wk_scale_sb = keep.tile([P, E * PASSES, N], U8, name="wk_scale_sb", align_bytes=64)
         wv_scale_sb = keep.tile([P, E * PASSES, N], U8, name="wv_scale_sb", align_bytes=64)
-        wv_raw = [keep.tile([P, PASSES, PACK, N], F32, name="wv_raw%d" % e, tag="stream%d" % e) for e in range(E)]
-        wv_bf = keep.tile([P, E * PASSES, N, PACK], BF16, name="wv_bf", align_bytes=64)
+        early_raw = keep.tile([P, EARLY, W_ROW], F32, name="early_raw")
+        early_bf = keep.tile([P, EARLY, W_ROW], BF16, name="early_bf", align_bytes=64)
+        early_gates = keep.tile([P, 2, T], F32, name="early_gates")
         bias_sb = keep.tile([P, 3, E], F32, name="bias_sb")
         slot_out = [keep.tile([P, SLOTS], F32, name="slot_out%d" % j) for j in range(3)]
         ident = keep.tile([P, P], F32, name="ident")
@@ -69,9 +71,9 @@ def tile_moe_qkv_kernel(
         nc.gpsimd.memset(slot_scales_low[:].bitcast(I32), 0)
         make_identity(nc, ident[:])
 
-        def load_wv(e):
+        def load_wv(e, raw):
             nc.sync.dma_start(
-                out=wv_raw[e][:].rearrange("p s j n -> p s (j n)"),
+                out=raw.rearrange("p (s c) -> p s c", s=PASSES),
                 in_=wv[e].rearrange("(s p j) n -> p s (j n)", s=PASSES, j=PACK),
             )
 
@@ -80,11 +82,9 @@ def tile_moe_qkv_kernel(
             for q in range(4):
                 nc.sync.dma_start(out=plane[32 * q : 32 * q + 4].bitcast(I32), in_=rows[q].bitcast(I32))
 
-        wk_rows = wk_words.rearrange("e s p n d -> p (e s) (n d)").bitcast(I32)
-
-        def load_wk(e0, e1):
-            group = slice(PASSES * e0, PASSES * e1)
-            nc.sync.dma_start(out=wk_word_sb[:, group], in_=wk_rows[:, group])
+        def load_wk(h):
+            rows = wk_words.rearrange("e s p n d -> p (e s) (n d)").bitcast(I32)
+            nc.sync.dma_start(out=wk_word_sb[:, E * h : E * (h + 1)], in_=rows[:, E * h : E * (h + 1)])
 
         word_start = (T, 0)
         nc.sync.dma_start(offs_sb[:], offs)
@@ -97,24 +97,27 @@ def tile_moe_qkv_kernel(
             nc.sync.dma_start(
                 out=x_scale_sb[32 * q : 32 * q + 8, 0:T].bitcast(I32), in_=x_scales[:, 4 * q : 4 * q + 4].bitcast(I32)
             )
-        for e in range(E):
-            load_wv(e)
+        for e in range(EARLY - 1):
+            load_wv(e, early_raw[:, e])
         nc.sync.dma_start(out=bias_sb[:], in_=bias.rearrange("(j p) e -> p j e", p=P))
         load_weight_scales(wk_scale_sb, wk_scales)
-        load_weight_scales(wq_scale_sb, wq_scales)
-        for e0 in (0, E // 2):
-            load_wk(e0, e0 + E // 2)
+        load_wk(0)
+        load_wv(EARLY - 1, early_raw[:, EARLY - 1])
+        load_wk(1)
         for r, pos in enumerate((pos1, pos2, pos3, pos4)):
             nc.sync.dma_start(pos_sb[r][:], pos)
+        for r in range(2):
+            nc.sync.dma_start(out=early_gates[:, r], in_=gate[r])
+        load_weight_scales(wq_scale_sb, wq_scales)
         nc.sync.dma_start(out=wq_word_sb[:].bitcast(I32), in_=wq_words.rearrange("e s p b -> p (e s) b").bitcast(I32))
 
         def entries(list_tile, first, last):
             return list_tile[:, first // LIST_ROWS : last // LIST_ROWS]
 
         def gather_words(first):
+            last = first + HALF_SLOTS
             for s in range(PASSES):
                 window = x_word_sb[:, word_start[s] : word_start[s] + WINDOW].bitcast(U32)
-                last = first + HALF_SLOTS
                 nc.vector.tensor_copy(slot_words[s][:, first:last], window.indirect(entries(offs_sb, first, last)))
 
         gather_words(0)
@@ -128,17 +131,42 @@ def tile_moe_qkv_kernel(
                 in_=slot_scales[32 * q + 4 : 32 * q + 8].bitcast(I32),
             )
 
-        for g in range(E * PASSES):
+        late = keep.tile([P, 2 * T + (E - EARLY) * W_ROW], F32, name="late", tag="x_scales_then_late", align_bytes=64)
+        gate_sb = [early_gates[:, 0], early_gates[:, 1], late[:, 0:T], late[:, T : 2 * T]]
+        late_raw = late[:, 2 * T :].rearrange("p (e c) -> p e c", c=W_ROW)
+        for r in (2, 3):
+            nc.sync.dma_start(out=gate_sb[r], in_=gate[r])
+        for e in range(EARLY, E):
+            load_wv(e, late_raw[:, e - EARLY])
+
+        def round_wv(raw, rounded):
             nc.scalar.copy(
-                wv_bf[:, g].rearrange("p (c i) j -> p c j i", i=4),
-                wv_raw[g // PASSES][:, g % PASSES].rearrange("p j (c i) -> p c j i", i=4),
+                rounded.rearrange("p (s n j) -> p s n j", s=PASSES, j=PACK),
+                raw.rearrange("p (s j n) -> p s n j", s=PASSES, j=PACK),
             )
-        gate_sb = [keep.tile([P, T], F32, name="gate_sb%d" % r, tag="stream%d" % (GATE_SLOT + r)) for r in range(TOP)]
-        for r in range(TOP):
-            nc.sync.dma_start(out=gate_sb[r][:], in_=gate[r])
+
+        def quantize_wv(e0, e1, rounded):
+            group = slice(PASSES * e0, PASSES * e1)
+            nc.vector.quantize_mx(
+                out=wv_word_sb[:, group].rearrange("p g n -> p (g n)").bitcast(FP8X4),
+                scales=wv_scale_sb[:, group].rearrange("p g n -> p (g n)"),
+                in_=rounded.rearrange("p e c -> p (e c)"),
+            )
+
+        for e in range(EARLY):
+            round_wv(early_raw[:, e], early_bf[:, e])
+        for e0 in range(0, EARLY, 2):
+            e1 = min(e0 + 2, EARLY)
+            quantize_wv(e0, e1, early_bf[:, e0:e1])
+
+        tenants = []
+
+        def next_bank(width):
+            tenants.append(psum.tile([P, width], F32, name="bank%d" % (len(tenants) % BANKS)))
+            return tenants[-1]
 
         def project(j, e, words, scales, dtype, width, token_scales):
-            acc = psum_acc.tile([P, C], F32, name="acc")
+            acc = next_bank(C)
             for u0 in range(0, C, width):
                 slots = slice(e * C + u0, e * C + u0 + width)
                 for s in range(PASSES):
@@ -157,17 +185,25 @@ def tile_moe_qkv_kernel(
         low_planes = (slot_scales[:], slot_scales_low[:])
         for e in range(E):
             project(K_ROWS, e, wk_word_sb, wk_scale_sb, FP8X4, C, packed_planes)
+        for e in range(EARLY):
+            project(V_ROWS, e, wv_word_sb, wv_scale_sb, FP8X4, C, packed_planes)
         for e in range(E):
             project(Q_ROWS, e, wq_word_sb, wq_scale_sb, FP4X4, C // 2, low_planes)
-        for e0 in range(0, E, 2):
-            group = slice(PASSES * e0, PASSES * (e0 + 2))
-            nc.vector.quantize_mx(
-                out=wv_word_sb[:, group].rearrange("p g n -> p (g n)").bitcast(FP8X4),
-                scales=wv_scale_sb[:, group].rearrange("p g n -> p (g n)"),
-                in_=wv_bf[:, group].rearrange("p g n j -> p (g n j)"),
-            )
-        for e in range(E):
+        late_bf = keep.tile([P, E - EARLY, W_ROW], BF16, name="late_bf", tag="wq_then_late", align_bytes=64)
+        for e in range(EARLY, E):
+            round_wv(late_raw[:, e - EARLY], late_bf[:, e - EARLY])
+        quantize_wv(EARLY, EARLY + 1, late_bf[:, 0:1])
+        quantize_wv(EARLY + 1, E, late_bf[:, 1:])
+        for e in range(EARLY, E):
             project(V_ROWS, e, wv_word_sb, wv_scale_sb, FP8X4, C, packed_planes)
+
+        weighted = {
+            j: [terms_pool.tile([P, T], F32, name="weighted%d" % r) for r in range(TOP - 1)]
+            for j in (K_ROWS, Q_ROWS, V_ROWS)
+        }
+        weighted[K_ROWS].append(keep.tile([P, T], F32, name="last_k_term"))
+        weighted[Q_ROWS].append(keep.tile([P, T], F32, name="last_q_term", tag="wq_then_late", align_bytes=64))
+        weighted[V_ROWS].append(keep.tile([P, T], F32, name="last_v_term"))
 
         def fetch(j, r, t0, t1):
             nc.vector.tensor_tensor(
@@ -175,7 +211,7 @@ def tile_moe_qkv_kernel(
             )
 
         def add_up(j, t0, t1, terms):
-            turned = psum.tile([P, t1 - t0], F32, name="turned")
+            turned = next_bank(t1 - t0)
             for b0 in range(0, t1 - t0, P):
                 for r in range(terms):
                     nc.tensor.matmul(
@@ -188,25 +224,22 @@ def tile_moe_qkv_kernel(
                     )
             turned_sb = stage.tile([P, t1 - t0], F32, name="turned_sb")
             nc.scalar.copy(turned_sb[:], turned[:])
-            total = psum.tile([P, t1 - t0], F32, name="total")
+            total = next_bank(t1 - t0)
             for b0 in range(0, t1 - t0, P):
                 nc.tensor.transpose(total[:, b0 : b0 + P], turned_sb[:, b0 : b0 + P], ident[:])
             return total
 
         def store(j, t0, t1, result):
-            nc.sync.dma_start(out=out[j * N : (j + 1) * N, t0:t1], in_=result[:])
+            nc.sync.dma_start(out=out[j * N : (j + 1) * N, t0:t1], in_=result)
 
-        weighted = {}
         for j in (K_ROWS, Q_ROWS):
-            weighted[j] = [terms_pool.tile([P, T], F32, name="weighted%d" % r) for r in range(TOP)]
             for r in range(TOP):
                 fetch(j, r, 0, T)
             for t0, t1 in EVEN_PIECES:
                 total = add_up(j, t0, t1, TOP)
                 result = stage.tile([P, t1 - t0], F32, name="result")
                 nc.scalar.copy(result[:], total[:])
-                store(j, t0, t1, result)
-        weighted[V_ROWS] = [terms_pool.tile([P, T], F32, name="weighted%d" % r) for r in range(TOP)]
+                store(j, t0, t1, result[:])
         partial = []
         for t0, t1 in LAST_PIECES:
             for r in range(TOP - 1):
@@ -214,6 +247,6 @@ def tile_moe_qkv_kernel(
             partial.append(add_up(V_ROWS, t0, t1, TOP - 1))
         for (t0, t1), total in zip(LAST_PIECES, partial):
             fetch(V_ROWS, TOP - 1, t0, t1)
-            result = stage.tile([P, t1 - t0], F32, name="result")
-            nc.vector.tensor_tensor(result[:], total[:], weighted[V_ROWS][TOP - 1][:, t0:t1], ADD)
-            store(V_ROWS, t0, t1, result)
+            last_term = weighted[V_ROWS][TOP - 1][:, t0:t1]
+            nc.vector.tensor_tensor(last_term, total[:], last_term, ADD)
+            store(V_ROWS, t0, t1, last_term)

@@ -24,10 +24,16 @@ PASSES = K // (P * PACK)
 SLOTS = E * C
 LIST_ROWS = 16
 WINDOW = 2048
-HALF_SLOTS = SLOTS // 2
 BANKS = 8
-EARLY = 9
+BANK = 512
 W_ROW = PASSES * PACK * N
+GATE_COLS = TOP * T // P
+SCALE_CHUNKS = ((0, 6), (6, 12))
+WORD_CHUNKS = ((0, 6), (6, 10), (10, 12))
+EARLY_LOADS = ((0, 2), (2, 4), (4, 6), (6, 8), (8, 9))
+EARLY_QUANT = ((0, 4), (4, 8), (8, 9))
+LATE_LOADS = ((9, 10), (10, 12))
+EARLY = EARLY_LOADS[-1][1]
 EVEN_PIECES = ((0, 384), (384, T))
 LAST_PIECES = ((0, 512), (512, T))
 Q_ROWS, K_ROWS, V_ROWS = 0, 1, 2
@@ -40,41 +46,46 @@ def tile_moe_qkv_kernel(
     with ExitStack() as ctx:
         keep = ctx.enter_context(tc.tile_pool(name="keep", bufs=1))
         stage = ctx.enter_context(tc.tile_pool(name="stage", bufs=2))
-        terms_pool = ctx.enter_context(tc.tile_pool(name="terms", bufs=3))
         psum = ctx.enter_context(tc.psum_pool(name="psum", bufs=1))
 
         offs_sb = keep.tile([P, SLOTS // LIST_ROWS], U16, name="offs_sb")
         pos_sb = [keep.tile([P, T // LIST_ROWS], U16, name="pos_sb%d" % r) for r in range(TOP)]
-        x_scale_sb = keep.tile([P, WINDOW], U8, name="x_scale_sb", tag="x_scales_then_late", align_bytes=64)
+        x_scale_sb = keep.tile([P, WINDOW], U8, name="x_scale_sb", align_bytes=64)
         x_word_sb = keep.tile([P, T + WINDOW], I32, name="x_word_sb", align_bytes=64)
         slot_words = [keep.tile([P, SLOTS], U32, name="slot_words%d" % s, align_bytes=64) for s in range(PASSES)]
         slot_scales = keep.tile([P, SLOTS], U8, name="slot_scales", align_bytes=64)
         slot_scales_low = keep.tile([P, SLOTS], U8, name="slot_scales_low", align_bytes=64)
-        wq_word_sb = keep.tile([P, E * PASSES, 2 * N], U8, name="wq_word_sb", tag="wq_then_late", align_bytes=64)
+        wq_word_sb = keep.tile([P, E * PASSES, 2 * N], U8, name="wq_word_sb", align_bytes=64)
         wk_word_sb = keep.tile([P, E * PASSES, N], I32, name="wk_word_sb", align_bytes=64)
         wv_word_sb = keep.tile([P, E * PASSES, N], U32, name="wv_word_sb", align_bytes=64)
         wq_scale_sb = keep.tile([P, E * PASSES, N], U8, name="wq_scale_sb", align_bytes=64)
         wk_scale_sb = keep.tile([P, E * PASSES, N], U8, name="wk_scale_sb", align_bytes=64)
         wv_scale_sb = keep.tile([P, E * PASSES, N], U8, name="wv_scale_sb", align_bytes=64)
-        early_raw = keep.tile([P, EARLY, W_ROW], F32, name="early_raw")
-        early_bf = keep.tile([P, EARLY, W_ROW], BF16, name="early_bf", align_bytes=64)
-        early_gates = keep.tile([P, 2, T], F32, name="early_gates")
+        raw = {
+            (e0, e1): keep.tile([P, (e1 - e0) * W_ROW], F32, name="raw%d" % e0, tag="raw%d" % e0)
+            for e0, e1 in EARLY_LOADS + LATE_LOADS
+        }
+        early_bf = keep.tile([P, EARLY * W_ROW], BF16, name="early_bf", align_bytes=64)
+        late_bf = keep.tile([P, (E - EARLY) * W_ROW], BF16, name="late_bf", tag="late_bf", align_bytes=64)
+        gate_cols = keep.tile([P, GATE_COLS], F32, name="gate_cols")
+        gates = keep.tile([P, TOP * T], F32, name="gates")
         bias_sb = keep.tile([P, 3, E], F32, name="bias_sb")
         slot_out = [keep.tile([P, SLOTS], F32, name="slot_out%d" % j) for j in range(3)]
         ident = keep.tile([P, P], F32, name="ident")
 
         nc.gpsimd.memset(x_scale_sb[:, 0:T].bitcast(I32), 0)
-        nc.gpsimd.memset(wk_scale_sb[:].rearrange("p g n -> p (g n)").bitcast(I32), 0)
-        nc.gpsimd.memset(wq_scale_sb[:].rearrange("p g n -> p (g n)").bitcast(I32), 0)
-        nc.vector.memset(x_word_sb[:, PASSES * T :], 0)
-        nc.vector.memset(x_scale_sb[:, T:].bitcast(I32), 0)
-        nc.gpsimd.memset(slot_scales_low[:].bitcast(I32), 0)
         make_identity(nc, ident[:])
+        nc.gpsimd.memset(wk_scale_sb[:].rearrange("p g n -> p (g n)").bitcast(I32), 0)
+        nc.gpsimd.memset(slot_scales_low[:].bitcast(I32), 0)
+        nc.gpsimd.memset(wq_scale_sb[:].rearrange("p g n -> p (g n)").bitcast(I32), 0)
+        nc.vector.memset(x_scale_sb[:, T:].bitcast(I32), 0)
+        nc.vector.memset(x_word_sb[:, PASSES * T :], 0)
 
-        def load_wv(e, raw):
+        def load_wv(group):
+            rows = wv.rearrange("e (s p j) n -> p (e s) (j n)", s=PASSES, j=PACK)
             nc.sync.dma_start(
-                out=raw.rearrange("p (s c) -> p s c", s=PASSES),
-                in_=wv[e].rearrange("(s p j) n -> p s (j n)", s=PASSES, j=PACK),
+                out=raw[group][:].rearrange("p (g c) -> p g c", c=PACK * N),
+                in_=rows[:, PASSES * group[0] : PASSES * group[1]],
             )
 
         def load_weight_scales(plane, scales):
@@ -86,63 +97,76 @@ def tile_moe_qkv_kernel(
             rows = wk_words.rearrange("e s p n d -> p (e s) (n d)").bitcast(I32)
             nc.sync.dma_start(out=wk_word_sb[:, E * h : E * (h + 1)], in_=rows[:, E * h : E * (h + 1)])
 
+        def load_wq(h):
+            rows = wq_words.rearrange("e s p b -> p (e s) b").bitcast(I32)
+            nc.sync.dma_start(out=wq_word_sb[:, E * h : E * (h + 1)].bitcast(I32), in_=rows[:, E * h : E * (h + 1)])
+
         word_start = (T, 0)
         nc.sync.dma_start(offs_sb[:], offs)
+        for q in range(4):
+            nc.sync.dma_start(
+                out=x_scale_sb[32 * q : 32 * q + 8, 0:T].bitcast(I32), in_=x_scales[:, 4 * q : 4 * q + 4].bitcast(I32)
+            )
+        nc.sync.dma_start(out=gate_cols[:], in_=gate[:, 0].rearrange("r (c i) -> r c i", i=GATE_COLS))
         for s in range(PASSES):
             nc.sync.dma_start(
                 out=x_word_sb[:, word_start[s] : word_start[s] + T],
                 in_=x_words[s].rearrange("p t d -> p (t d)").bitcast(I32),
             )
-        for q in range(4):
-            nc.sync.dma_start(
-                out=x_scale_sb[32 * q : 32 * q + 8, 0:T].bitcast(I32), in_=x_scales[:, 4 * q : 4 * q + 4].bitcast(I32)
-            )
-        for e in range(EARLY - 1):
-            load_wv(e, early_raw[:, e])
+        for group in EARLY_LOADS:
+            load_wv(group)
         nc.sync.dma_start(out=bias_sb[:], in_=bias.rearrange("(j p) e -> p j e", p=P))
         load_weight_scales(wk_scale_sb, wk_scales)
         load_wk(0)
-        load_wv(EARLY - 1, early_raw[:, EARLY - 1])
         load_wk(1)
         for r, pos in enumerate((pos1, pos2, pos3, pos4)):
             nc.sync.dma_start(pos_sb[r][:], pos)
-        for r in range(2):
-            nc.sync.dma_start(out=early_gates[:, r], in_=gate[r])
-        load_weight_scales(wq_scale_sb, wq_scales)
-        nc.sync.dma_start(out=wq_word_sb[:].bitcast(I32), in_=wq_words.rearrange("e s p b -> p (e s) b").bitcast(I32))
 
         def entries(list_tile, first, last):
             return list_tile[:, first // LIST_ROWS : last // LIST_ROWS]
 
-        def gather_words(first):
-            last = first + HALF_SLOTS
+        for e0, e1 in SCALE_CHUNKS:
+            nc.vector.tensor_copy(
+                slot_scales[:, e0 * C : e1 * C], x_scale_sb[:].indirect(entries(offs_sb, e0 * C, e1 * C))
+            )
+        for e0, e1 in WORD_CHUNKS:
             for s in range(PASSES):
                 window = x_word_sb[:, word_start[s] : word_start[s] + WINDOW].bitcast(U32)
-                nc.vector.tensor_copy(slot_words[s][:, first:last], window.indirect(entries(offs_sb, first, last)))
-
-        gather_words(0)
-        for first in (0, HALF_SLOTS):
-            last = first + HALF_SLOTS
-            nc.vector.tensor_copy(slot_scales[:, first:last], x_scale_sb[:].indirect(entries(offs_sb, first, last)))
-        gather_words(HALF_SLOTS)
+                nc.vector.tensor_copy(
+                    slot_words[s][:, e0 * C : e1 * C], window.indirect(entries(offs_sb, e0 * C, e1 * C))
+                )
         for q in range(4):
             nc.sync.dma_start(
                 out=slot_scales_low[32 * q : 32 * q + 4].bitcast(I32),
                 in_=slot_scales[32 * q + 4 : 32 * q + 8].bitcast(I32),
             )
+        load_weight_scales(wq_scale_sb, wq_scales)
+        load_wq(0)
+        load_wq(1)
+        for group in LATE_LOADS:
+            load_wv(group)
 
-        late = keep.tile([P, 2 * T + (E - EARLY) * W_ROW], F32, name="late", tag="x_scales_then_late", align_bytes=64)
-        gate_sb = [early_gates[:, 0], early_gates[:, 1], late[:, 0:T], late[:, T : 2 * T]]
-        late_raw = late[:, 2 * T :].rearrange("p (e c) -> p e c", c=W_ROW)
-        for r in (2, 3):
-            nc.sync.dma_start(out=gate_sb[r], in_=gate[r])
-        for e in range(EARLY, E):
-            load_wv(e, late_raw[:, e - EARLY])
+        tenants = []
 
-        def round_wv(raw, rounded):
+        def next_bank(width):
+            tenants.append(psum.tile([P, width], F32, name="bank%d" % (len(tenants) % BANKS)))
+            return tenants[-1]
+
+        per_bank = BANK // P
+        for i0 in range(0, GATE_COLS, per_bank):
+            spread = next_bank(BANK)
+            for i in range(per_bank):
+                column = gate_cols[:, i0 + i : i0 + i + 1].to_broadcast([P, P])
+                nc.tensor.transpose(spread[:, i * P : (i + 1) * P], column, ident[:])
             nc.scalar.copy(
-                rounded.rearrange("p (s n j) -> p s n j", s=PASSES, j=PACK),
-                raw.rearrange("p (s j n) -> p s n j", s=PASSES, j=PACK),
+                gates[:].rearrange("p (m i) -> p m i", i=GATE_COLS)[:, :, i0 : i0 + per_bank],
+                spread[:].rearrange("p (i m) -> p m i", i=per_bank),
+            )
+
+        def round_wv(group, rounded):
+            nc.scalar.copy(
+                rounded.rearrange("p (g c i j) -> p g c j i", c=N // 4, i=4, j=PACK),
+                raw[group][:].rearrange("p (g j c i) -> p g c j i", c=N // 4, i=4, j=PACK),
             )
 
         def quantize_wv(e0, e1, rounded):
@@ -150,20 +174,13 @@ def tile_moe_qkv_kernel(
             nc.vector.quantize_mx(
                 out=wv_word_sb[:, group].rearrange("p g n -> p (g n)").bitcast(FP8X4),
                 scales=wv_scale_sb[:, group].rearrange("p g n -> p (g n)"),
-                in_=rounded.rearrange("p e c -> p (e c)"),
+                in_=rounded,
             )
 
-        for e in range(EARLY):
-            round_wv(early_raw[:, e], early_bf[:, e])
-        for e0 in range(0, EARLY, 2):
-            e1 = min(e0 + 2, EARLY)
-            quantize_wv(e0, e1, early_bf[:, e0:e1])
-
-        tenants = []
-
-        def next_bank(width):
-            tenants.append(psum.tile([P, width], F32, name="bank%d" % (len(tenants) % BANKS)))
-            return tenants[-1]
+        for e0, e1 in EARLY_LOADS:
+            round_wv((e0, e1), early_bf[:, e0 * W_ROW : e1 * W_ROW])
+        for e0, e1 in EARLY_QUANT:
+            quantize_wv(e0, e1, early_bf[:, e0 * W_ROW : e1 * W_ROW])
 
         def project(j, e, words, scales, dtype, width, token_scales):
             acc = next_bank(C)
@@ -189,64 +206,77 @@ def tile_moe_qkv_kernel(
             project(V_ROWS, e, wv_word_sb, wv_scale_sb, FP8X4, C, packed_planes)
         for e in range(E):
             project(Q_ROWS, e, wq_word_sb, wq_scale_sb, FP4X4, C // 2, low_planes)
-        late_bf = keep.tile([P, E - EARLY, W_ROW], BF16, name="late_bf", tag="wq_then_late", align_bytes=64)
-        for e in range(EARLY, E):
-            round_wv(late_raw[:, e - EARLY], late_bf[:, e - EARLY])
-        quantize_wv(EARLY, EARLY + 1, late_bf[:, 0:1])
-        quantize_wv(EARLY + 1, E, late_bf[:, 1:])
+        for e0, e1 in LATE_LOADS:
+            round_wv((e0, e1), late_bf[:, (e0 - EARLY) * W_ROW : (e1 - EARLY) * W_ROW])
+        for e0, e1 in LATE_LOADS:
+            quantize_wv(e0, e1, late_bf[:, (e0 - EARLY) * W_ROW : (e1 - EARLY) * W_ROW])
         for e in range(EARLY, E):
             project(V_ROWS, e, wv_word_sb, wv_scale_sb, FP8X4, C, packed_planes)
 
-        weighted = {
-            j: [terms_pool.tile([P, T], F32, name="weighted%d" % r) for r in range(TOP - 1)]
-            for j in (K_ROWS, Q_ROWS, V_ROWS)
-        }
-        weighted[K_ROWS].append(keep.tile([P, T], F32, name="last_k_term"))
-        weighted[Q_ROWS].append(keep.tile([P, T], F32, name="last_q_term", tag="wq_then_late", align_bytes=64))
-        weighted[V_ROWS].append(keep.tile([P, T], F32, name="last_v_term"))
-
-        def fetch(j, r, t0, t1):
+        def fetch(j, r, t0, t1, term):
             nc.vector.tensor_tensor(
-                weighted[j][r][:, t0:t1], slot_out[j][:].indirect(entries(pos_sb[r], t0, t1)), gate_sb[r][:, t0:t1], MULT
+                term, slot_out[j][:].indirect(entries(pos_sb[r], t0, t1)), gates[:, r * T + t0 : r * T + t1], MULT
             )
 
-        def add_up(j, t0, t1, terms):
-            turned = next_bank(t1 - t0)
-            for b0 in range(0, t1 - t0, P):
-                for r in range(terms):
+        def add_up(terms, turned_sb):
+            width = terms[0].shape[1]
+            turned = next_bank(width)
+            for b0 in range(0, width, P):
+                for r, term in enumerate(terms):
                     nc.tensor.matmul(
                         turned[:, b0 : b0 + P],
-                        weighted[j][r][:, t0 + b0 : t0 + b0 + P],
+                        term[:, b0 : b0 + P],
                         ident[:],
                         start=(r == 0),
-                        stop=(r == terms - 1),
+                        stop=(r == len(terms) - 1),
                         is_transpose=True,
                     )
-            turned_sb = stage.tile([P, t1 - t0], F32, name="turned_sb")
-            nc.scalar.copy(turned_sb[:], turned[:])
-            total = next_bank(t1 - t0)
-            for b0 in range(0, t1 - t0, P):
+            nc.scalar.copy(turned_sb, turned[:])
+            total = next_bank(width)
+            for b0 in range(0, width, P):
                 nc.tensor.transpose(total[:, b0 : b0 + P], turned_sb[:, b0 : b0 + P], ident[:])
             return total
 
         def store(j, t0, t1, result):
             nc.sync.dma_start(out=out[j * N : (j + 1) * N, t0:t1], in_=result)
 
-        for j in (K_ROWS, Q_ROWS):
+        def finish(j, t0, t1, terms, turned_sb):
+            total = add_up(terms, turned_sb)
+            result = keep.tile([P, t1 - t0], F32, name="result%d_%d" % (j, t0))
+            nc.scalar.copy(result[:], total[:])
+            store(j, t0, t1, result[:])
+
+        k_pairs = [keep.tile([P, 2 * T], F32, name="k_terms%d" % h, tag="raw%d" % EARLY_LOADS[h][0]) for h in range(2)]
+        k_terms = [k_pairs[r // 2][:, (r % 2) * T : (r % 2 + 1) * T] for r in range(TOP)]
+        for r in range(TOP):
+            fetch(K_ROWS, r, 0, T, k_terms[r])
+        for (t0, t1), late in zip(EVEN_PIECES, LATE_LOADS):
+            turned_sb = keep.tile([P, t1 - t0], F32, name="k_turned%d" % t0, tag="raw%d" % late[0])
+            finish(K_ROWS, t0, t1, [term[:, t0:t1] for term in k_terms], turned_sb[:])
+
+        half = T // 2
+        q_first = keep.tile([P, TOP * half], F32, name="q_first", tag="raw%d" % EARLY_LOADS[2][0])
+        q_second = keep.tile([P, 2 * half], F32, name="q_second", tag="raw%d" % EARLY_LOADS[3][0])
+        q_last = keep.tile([P, 2 * half], F32, name="q_last", tag="late_bf", align_bytes=64)
+        q_terms = [
+            [q_first[:, r * half : (r + 1) * half] for r in range(TOP)],
+            [pair[:, r * half : (r + 1) * half] for pair in (q_second, q_last) for r in range(2)],
+        ]
+        for (t0, t1), terms in zip(EVEN_PIECES, q_terms):
             for r in range(TOP):
-                fetch(j, r, 0, T)
-            for t0, t1 in EVEN_PIECES:
-                total = add_up(j, t0, t1, TOP)
-                result = stage.tile([P, t1 - t0], F32, name="result")
-                nc.scalar.copy(result[:], total[:])
-                store(j, t0, t1, result[:])
+                fetch(Q_ROWS, r, t0, t1, terms[r])
+            turned_sb = stage.tile([P, t1 - t0], F32, name="turned_sb")
+            finish(Q_ROWS, t0, t1, terms, turned_sb[:])
+
+        v_terms = [keep.tile([P, T], F32, name="v_term%d" % r) for r in range(TOP)]
         partial = []
         for t0, t1 in LAST_PIECES:
             for r in range(TOP - 1):
-                fetch(V_ROWS, r, t0, t1)
-            partial.append(add_up(V_ROWS, t0, t1, TOP - 1))
+                fetch(V_ROWS, r, t0, t1, v_terms[r][:, t0:t1])
+            turned_sb = stage.tile([P, t1 - t0], F32, name="turned_sb")
+            partial.append(add_up([term[:, t0:t1] for term in v_terms[: TOP - 1]], turned_sb[:]))
         for (t0, t1), total in zip(LAST_PIECES, partial):
-            fetch(V_ROWS, TOP - 1, t0, t1)
-            last_term = weighted[V_ROWS][TOP - 1][:, t0:t1]
+            last_term = v_terms[TOP - 1][:, t0:t1]
+            fetch(V_ROWS, TOP - 1, t0, t1, last_term)
             nc.vector.tensor_tensor(last_term, total[:], last_term, ADD)
             store(V_ROWS, t0, t1, last_term)

@@ -17,6 +17,7 @@ FP4X4 = mybir.dt.float4_e2m1fn_x4
 MULT = mybir.AluOpType.mult
 ADD = mybir.AluOpType.add
 IDENTITY = mybir.ActivationFunctionType.Identity
+COPY = mybir.ActivationFunctionType.Copy
 
 P = 128
 PACK = 4
@@ -27,16 +28,15 @@ WINDOW = 2048
 BANKS = 8
 BANK = 512
 W_ROW = PASSES * PACK * N
-GATE_COLS = TOP * T // P
+BLOCKS = T // P
+HALF = T // 2
 SCALE_CHUNKS = ((0, 6), (6, 12))
-WORD_CHUNKS = ((0, 6), (6, 10), (10, 12))
-EARLY_LOADS = ((0, 2), (2, 4), (4, 6), (6, 8), (8, 9))
-EARLY_QUANT = ((0, 4), (4, 8), (8, 9))
-LATE_LOADS = ((9, 10), (10, 12))
-EARLY = EARLY_LOADS[-1][1]
-EVEN_PIECES = ((0, 384), (384, T))
+WORD_CHUNKS = ((0, 6), (6, 9), (9, 11), (11, 12))
+PAIRS = tuple((e, e + 2) for e in range(0, E, 2))
+QUANT = ((0, 4), (4, 8), (8, 10), (10, 12))
 LAST_PIECES = ((0, 512), (512, T))
 Q_ROWS, K_ROWS, V_ROWS = 0, 1, 2
+PLAIN_TERMS = 2
 
 
 def tile_moe_qkv_kernel(
@@ -45,7 +45,6 @@ def tile_moe_qkv_kernel(
     nc = tc.nc
     with ExitStack() as ctx:
         keep = ctx.enter_context(tc.tile_pool(name="keep", bufs=1))
-        stage = ctx.enter_context(tc.tile_pool(name="stage", bufs=2))
         psum = ctx.enter_context(tc.psum_pool(name="psum", bufs=1))
 
         offs_sb = keep.tile([P, SLOTS // LIST_ROWS], U16, name="offs_sb")
@@ -61,66 +60,55 @@ def tile_moe_qkv_kernel(
         wq_scale_sb = keep.tile([P, E * PASSES, N], U8, name="wq_scale_sb", align_bytes=64)
         wk_scale_sb = keep.tile([P, E * PASSES, N], U8, name="wk_scale_sb", align_bytes=64)
         wv_scale_sb = keep.tile([P, E * PASSES, N], U8, name="wv_scale_sb", align_bytes=64)
-        raw = {
-            (e0, e1): keep.tile([P, (e1 - e0) * W_ROW], F32, name="raw%d" % e0, tag="raw%d" % e0)
-            for e0, e1 in EARLY_LOADS + LATE_LOADS
+        raw = {e0: keep.tile([P, 2 * W_ROW], F32, name="raw%d" % e0, tag="raw%d" % e0) for e0, e1 in PAIRS}
+        rounded = {
+            e0: keep.tile([P, (e1 - e0) * W_ROW], BF16, name="rounded%d" % e0, align_bytes=64) for e0, e1 in QUANT
         }
-        early_bf = keep.tile([P, EARLY * W_ROW], BF16, name="early_bf", align_bytes=64)
-        late_bf = keep.tile([P, (E - EARLY) * W_ROW], BF16, name="late_bf", tag="late_bf", align_bytes=64)
-        gate_cols = keep.tile([P, GATE_COLS], F32, name="gate_cols")
+        gate_rows = keep.tile([P, P], F32, name="gate_rows")
+        gate_cols = keep.tile([P, TOP * BLOCKS], F32, name="gate_cols")
         gates = keep.tile([P, TOP * T], F32, name="gates")
         bias_sb = keep.tile([P, 3, E], F32, name="bias_sb")
-        slot_out = [keep.tile([P, SLOTS], F32, name="slot_out%d" % j) for j in range(3)]
         ident = keep.tile([P, P], F32, name="ident")
 
         nc.gpsimd.memset(x_scale_sb[:, 0:T].bitcast(I32), 0)
+        nc.gpsimd.memset(gate_rows[:], 0.0)
         make_identity(nc, ident[:])
-        nc.gpsimd.memset(wk_scale_sb[:].rearrange("p g n -> p (g n)").bitcast(I32), 0)
-        nc.gpsimd.memset(slot_scales_low[:].bitcast(I32), 0)
         nc.gpsimd.memset(wq_scale_sb[:].rearrange("p g n -> p (g n)").bitcast(I32), 0)
+        nc.gpsimd.memset(slot_scales_low[:].bitcast(I32), 0)
+        nc.gpsimd.memset(wk_scale_sb[:].rearrange("p g n -> p (g n)").bitcast(I32), 0)
         nc.vector.memset(x_scale_sb[:, T:].bitcast(I32), 0)
         nc.vector.memset(x_word_sb[:, PASSES * T :], 0)
 
-        def load_wv(group):
+        def load_wv(e0):
             rows = wv.rearrange("e (s p j) n -> p (e s) (j n)", s=PASSES, j=PACK)
             nc.sync.dma_start(
-                out=raw[group][:].rearrange("p (g c) -> p g c", c=PACK * N),
-                in_=rows[:, PASSES * group[0] : PASSES * group[1]],
+                out=raw[e0][:].rearrange("p (g c) -> p g c", c=PACK * N),
+                in_=rows[:, PASSES * e0 : PASSES * (e0 + 2)],
             )
 
-        def load_weight_scales(plane, scales):
+        def load_weight_scales(plane, scales, quadrants):
             rows = scales.rearrange("e s (q j) n -> q j (e s) n", j=4)
-            for q in range(4):
+            for q in quadrants:
                 nc.sync.dma_start(out=plane[32 * q : 32 * q + 4].bitcast(I32), in_=rows[q].bitcast(I32))
 
-        def load_wk(h):
-            rows = wk_words.rearrange("e s p n d -> p (e s) (n d)").bitcast(I32)
-            nc.sync.dma_start(out=wk_word_sb[:, E * h : E * (h + 1)], in_=rows[:, E * h : E * (h + 1)])
+        def load_pos(r):
+            nc.sync.dma_start(pos_sb[r][:], (pos1, pos2, pos3, pos4)[r])
 
-        def load_wq(h):
-            rows = wq_words.rearrange("e s p b -> p (e s) b").bitcast(I32)
-            nc.sync.dma_start(out=wq_word_sb[:, E * h : E * (h + 1)].bitcast(I32), in_=rows[:, E * h : E * (h + 1)])
-
-        word_start = (T, 0)
         nc.sync.dma_start(offs_sb[:], offs)
         for q in range(4):
             nc.sync.dma_start(
                 out=x_scale_sb[32 * q : 32 * q + 8, 0:T].bitcast(I32), in_=x_scales[:, 4 * q : 4 * q + 4].bitcast(I32)
             )
-        nc.sync.dma_start(out=gate_cols[:], in_=gate[:, 0].rearrange("r (c i) -> r c i", i=GATE_COLS))
-        for s in range(PASSES):
-            nc.sync.dma_start(
-                out=x_word_sb[:, word_start[s] : word_start[s] + T],
-                in_=x_words[s].rearrange("p t d -> p (t d)").bitcast(I32),
-            )
-        for group in EARLY_LOADS:
-            load_wv(group)
+        nc.sync.dma_start(
+            out=x_word_sb[:, 0 : PASSES * T].rearrange("p (s t) -> p s t", s=PASSES),
+            in_=x_words.rearrange("s p t d -> p s (t d)").bitcast(I32),
+        )
+        nc.sync.dma_start(out=gate_rows[0 : TOP * BLOCKS], in_=gate[:, 0].rearrange("r (b m) -> r b m", m=P))
+        for e0 in (0, 2, 4, 6):
+            load_wv(e0)
         nc.sync.dma_start(out=bias_sb[:], in_=bias.rearrange("(j p) e -> p j e", p=P))
-        load_weight_scales(wk_scale_sb, wk_scales)
-        load_wk(0)
-        load_wk(1)
-        for r, pos in enumerate((pos1, pos2, pos3, pos4)):
-            nc.sync.dma_start(pos_sb[r][:], pos)
+        load_weight_scales(wq_scale_sb, wq_scales, range(4))
+        nc.sync.dma_start(out=wq_word_sb[:].bitcast(I32), in_=wq_words.rearrange("e s p b -> p (e s) b").bitcast(I32))
 
         def entries(list_tile, first, last):
             return list_tile[:, first // LIST_ROWS : last // LIST_ROWS]
@@ -131,7 +119,7 @@ def tile_moe_qkv_kernel(
             )
         for e0, e1 in WORD_CHUNKS:
             for s in range(PASSES):
-                window = x_word_sb[:, word_start[s] : word_start[s] + WINDOW].bitcast(U32)
+                window = x_word_sb[:, s * T : s * T + WINDOW].bitcast(U32)
                 nc.vector.tensor_copy(
                     slot_words[s][:, e0 * C : e1 * C], window.indirect(entries(offs_sb, e0 * C, e1 * C))
                 )
@@ -140,50 +128,62 @@ def tile_moe_qkv_kernel(
                 out=slot_scales_low[32 * q : 32 * q + 4].bitcast(I32),
                 in_=slot_scales[32 * q + 4 : 32 * q + 8].bitcast(I32),
             )
-        load_weight_scales(wq_scale_sb, wq_scales)
-        load_wq(0)
-        load_wq(1)
-        for group in LATE_LOADS:
-            load_wv(group)
+        load_wv(8)
+        load_pos(0)
+        load_pos(1)
+        load_wv(10)
+        load_pos(2)
+        load_weight_scales(wk_scale_sb, wk_scales, (0, 1))
+        load_pos(3)
+        load_weight_scales(wk_scale_sb, wk_scales, (2, 3))
+        nc.sync.dma_start(out=wk_word_sb[:], in_=wk_words.rearrange("e s p n d -> p (e s) (n d)").bitcast(I32))
 
-        tenants = []
+        def bank(b, width):
+            return psum.tile([P, width], F32, name="bank%d" % (b % BANKS))
 
-        def next_bank(width):
-            tenants.append(psum.tile([P, width], F32, name="bank%d" % (len(tenants) % BANKS)))
-            return tenants[-1]
-
+        turned_gates = bank(0, P)
+        nc.tensor.transpose(turned_gates[:], gate_rows[:], ident[:])
+        nc.scalar.copy(gate_cols[:], turned_gates[:, 0 : TOP * BLOCKS])
         per_bank = BANK // P
-        for i0 in range(0, GATE_COLS, per_bank):
-            spread = next_bank(BANK)
+        for i0 in range(0, TOP * BLOCKS, per_bank):
+            spread = bank(1 + i0 // per_bank, BANK)
             for i in range(per_bank):
                 column = gate_cols[:, i0 + i : i0 + i + 1].to_broadcast([P, P])
                 nc.tensor.transpose(spread[:, i * P : (i + 1) * P], column, ident[:])
+            nc.scalar.copy(gates[:, i0 * P : (i0 + per_bank) * P], spread[:])
+
+        def rounded_part(e0, e1):
+            g0 = max(g for g, g1 in QUANT if g <= e0)
+            return rounded[g0][:, (e0 - g0) * W_ROW : (e1 - g0) * W_ROW]
+
+        def round_wv(e0):
             nc.scalar.copy(
-                gates[:].rearrange("p (m i) -> p m i", i=GATE_COLS)[:, :, i0 : i0 + per_bank],
-                spread[:].rearrange("p (i m) -> p m i", i=per_bank),
+                rounded_part(e0, e0 + 2).rearrange("p (g c i j) -> p g c j i", c=N // 4, i=4, j=PACK),
+                raw[e0][:].rearrange("p (g j c i) -> p g c j i", c=N // 4, i=4, j=PACK),
             )
 
-        def round_wv(group, rounded):
-            nc.scalar.copy(
-                rounded.rearrange("p (g c i j) -> p g c j i", c=N // 4, i=4, j=PACK),
-                raw[group][:].rearrange("p (g j c i) -> p g c j i", c=N // 4, i=4, j=PACK),
-            )
+        def round_wv_gpsimd(e0):
+            for g in range(2 * PASSES):
+                cols = slice(g * PACK * N, (g + 1) * PACK * N)
+                nc.gpsimd.tensor_scalar(
+                    rounded_part(e0, e0 + 2)[:, cols].rearrange("p (n j) -> p n j", j=PACK),
+                    raw[e0][:, cols].rearrange("p (j n) -> p n j", j=PACK),
+                    1.0,
+                    0.0,
+                    MULT,
+                    ADD,
+                )
 
-        def quantize_wv(e0, e1, rounded):
+        def quantize_wv(e0, e1):
             group = slice(PASSES * e0, PASSES * e1)
             nc.vector.quantize_mx(
                 out=wv_word_sb[:, group].rearrange("p g n -> p (g n)").bitcast(FP8X4),
                 scales=wv_scale_sb[:, group].rearrange("p g n -> p (g n)"),
-                in_=rounded,
+                in_=rounded[e0][:],
             )
 
-        for e0, e1 in EARLY_LOADS:
-            round_wv((e0, e1), early_bf[:, e0 * W_ROW : e1 * W_ROW])
-        for e0, e1 in EARLY_QUANT:
-            quantize_wv(e0, e1, early_bf[:, e0 * W_ROW : e1 * W_ROW])
-
-        def project(j, e, words, scales, dtype, width, token_scales):
-            acc = next_bank(C)
+        def project(results, j, e, b, words, scales, dtype, width, token_scales):
+            acc = bank(b, C)
             for u0 in range(0, C, width):
                 slots = slice(e * C + u0, e * C + u0 + width)
                 for s in range(PASSES):
@@ -196,87 +196,105 @@ def tile_moe_qkv_kernel(
                         start=(s == 0),
                         stop=(s == PASSES - 1),
                     )
-            nc.scalar.activation(slot_out[j][:, e * C : (e + 1) * C], acc[:], IDENTITY, bias=bias_sb[:, j, e : e + 1])
+            nc.scalar.activation(results[:, e * C : (e + 1) * C], acc[:], IDENTITY, bias=bias_sb[:, j, e : e + 1])
 
         packed_planes = (slot_scales[:], slot_scales[4:P])
         low_planes = (slot_scales[:], slot_scales_low[:])
-        for e in range(E):
-            project(K_ROWS, e, wk_word_sb, wk_scale_sb, FP8X4, C, packed_planes)
-        for e in range(EARLY):
-            project(V_ROWS, e, wv_word_sb, wv_scale_sb, FP8X4, C, packed_planes)
-        for e in range(E):
-            project(Q_ROWS, e, wq_word_sb, wq_scale_sb, FP4X4, C // 2, low_planes)
-        for e0, e1 in LATE_LOADS:
-            round_wv((e0, e1), late_bf[:, (e0 - EARLY) * W_ROW : (e1 - EARLY) * W_ROW])
-        for e0, e1 in LATE_LOADS:
-            quantize_wv(e0, e1, late_bf[:, (e0 - EARLY) * W_ROW : (e1 - EARLY) * W_ROW])
-        for e in range(EARLY, E):
-            project(V_ROWS, e, wv_word_sb, wv_scale_sb, FP8X4, C, packed_planes)
 
-        def fetch(j, r, t0, t1, term):
+        for e0 in (0, 2, 4, 6):
+            round_wv(e0)
+        round_wv_gpsimd(8)
+        q_slots = keep.tile([P, SLOTS], F32, name="q_slots")
+        for e in range(E):
+            project(q_slots, Q_ROWS, e, e, wq_word_sb, wq_scale_sb, FP4X4, C // 2, low_planes)
+        round_wv(10)
+        for e0, e1 in QUANT:
+            quantize_wv(e0, e1)
+        v_slots = keep.tile([P, SLOTS], F32, name="v_slots", tag="raw10")
+        for e in range(E):
+            project(v_slots, V_ROWS, e, E + e, wv_word_sb, wv_scale_sb, FP8X4, C, packed_planes)
+
+        def fetch_gated(results, r, t0, t1, term):
             nc.vector.tensor_tensor(
-                term, slot_out[j][:].indirect(entries(pos_sb[r], t0, t1)), gates[:, r * T + t0 : r * T + t1], MULT
+                term, results[:].indirect(entries(pos_sb[r], t0, t1)), gates[:, r * T + t0 : r * T + t1], MULT
             )
 
-        def add_up(terms, turned_sb):
-            width = terms[0].shape[1]
-            turned = next_bank(width)
-            for b0 in range(0, width, P):
-                for r, term in enumerate(terms):
+        def turn_and_add(b, sources):
+            width = sources[0].shape[1]
+            turned = bank(b, width)
+            for i, source in enumerate(sources):
+                for c0 in range(0, width, P):
                     nc.tensor.matmul(
-                        turned[:, b0 : b0 + P],
-                        term[:, b0 : b0 + P],
+                        turned[:, c0 : c0 + P],
+                        source[:, c0 : c0 + P],
                         ident[:],
-                        start=(r == 0),
-                        stop=(r == len(terms) - 1),
+                        start=(i == 0 and c0 == 0),
+                        stop=(i == len(sources) - 1 and c0 == width - P),
                         is_transpose=True,
                     )
-            nc.scalar.copy(turned_sb, turned[:])
-            total = next_bank(width)
-            for b0 in range(0, width, P):
-                nc.tensor.transpose(total[:, b0 : b0 + P], turned_sb[:, b0 : b0 + P], ident[:])
-            return total
+            return turned
 
         def store(j, t0, t1, result):
             nc.sync.dma_start(out=out[j * N : (j + 1) * N, t0:t1], in_=result)
 
-        def finish(j, t0, t1, terms, turned_sb):
-            total = add_up(terms, turned_sb)
-            result = keep.tile([P, t1 - t0], F32, name="result%d_%d" % (j, t0))
-            nc.scalar.copy(result[:], total[:])
-            store(j, t0, t1, result[:])
+        def fetch_terms(results, name, tags):
+            pairs = [keep.tile([P, 2 * T], F32, name="%s_terms%d" % (name, h), tag=tags[h]) for h in range(2)]
+            terms = [pairs[r // 2][:, (r % 2) * T : (r % 2 + 1) * T] for r in range(TOP)]
+            for r in range(PLAIN_TERMS):
+                nc.vector.tensor_copy(terms[r], results[:].indirect(pos_sb[r][:]))
+            for r in range(PLAIN_TERMS, TOP):
+                fetch_gated(results, r, 0, T, terms[r])
+            return terms
 
-        k_pairs = [keep.tile([P, 2 * T], F32, name="k_terms%d" % h, tag="raw%d" % EARLY_LOADS[h][0]) for h in range(2)]
-        k_terms = [k_pairs[r // 2][:, (r % 2) * T : (r % 2 + 1) * T] for r in range(TOP)]
-        for r in range(TOP):
-            fetch(K_ROWS, r, 0, T, k_terms[r])
-        for (t0, t1), late in zip(EVEN_PIECES, LATE_LOADS):
-            turned_sb = keep.tile([P, t1 - t0], F32, name="k_turned%d" % t0, tag="raw%d" % late[0])
-            finish(K_ROWS, t0, t1, [term[:, t0:t1] for term in k_terms], turned_sb[:])
+        def gate_plain_terms(name, terms, first_bank):
+            parts = []
+            for h in range(2):
+                t0 = h * HALF
+                parts.append([])
+                for r in range(PLAIN_TERMS):
+                    turned = turn_and_add(first_bank + 2 * h + r, [terms[r][:, t0 : t0 + HALF]])
+                    part = keep.tile([P, HALF], F32, name="%s_part%d_%d" % (name, h, r))
+                    for c0 in range(0, HALF, P):
+                        column = r * BLOCKS + (t0 + c0) // P
+                        nc.scalar.activation(
+                            part[:, c0 : c0 + P], turned[:, c0 : c0 + P], COPY, scale=gate_cols[:, column : column + 1]
+                        )
+                    parts[h].append(part[:])
+            return parts
 
-        half = T // 2
-        q_first = keep.tile([P, TOP * half], F32, name="q_first", tag="raw%d" % EARLY_LOADS[2][0])
-        q_second = keep.tile([P, 2 * half], F32, name="q_second", tag="raw%d" % EARLY_LOADS[3][0])
-        q_last = keep.tile([P, 2 * half], F32, name="q_last", tag="late_bf", align_bytes=64)
-        q_terms = [
-            [q_first[:, r * half : (r + 1) * half] for r in range(TOP)],
-            [pair[:, r * half : (r + 1) * half] for pair in (q_second, q_last) for r in range(2)],
-        ]
-        for (t0, t1), terms in zip(EVEN_PIECES, q_terms):
-            for r in range(TOP):
-                fetch(Q_ROWS, r, t0, t1, terms[r])
-            turned_sb = stage.tile([P, t1 - t0], F32, name="turned_sb")
-            finish(Q_ROWS, t0, t1, terms, turned_sb[:])
+        def combine(j, name, terms, parts):
+            for h in range(2):
+                t0 = h * HALF
+                turned = turn_and_add(4 + 2 * h, [term[:, t0 : t0 + HALF] for term in terms[PLAIN_TERMS:]])
+                rest = keep.tile([P, HALF], F32, name="%s_rest%d" % (name, h))
+                nc.scalar.copy(rest[:], turned[:])
+                total = turn_and_add(5 + 2 * h, parts[h] + [rest[:]])
+                result = keep.tile([P, HALF], F32, name="%s_result%d" % (name, h))
+                nc.scalar.copy(result[:], total[:])
+                store(j, t0, t0 + HALF, result[:])
 
-        v_terms = [keep.tile([P, T], F32, name="v_term%d" % r) for r in range(TOP)]
+        q_terms = fetch_terms(q_slots, "q", ("raw0", "raw2"))
+        q_parts = gate_plain_terms("q", q_terms, 4)
+        k_slots = keep.tile([P, SLOTS], F32, name="k_slots")
+        for e in range(E):
+            project(k_slots, K_ROWS, e, e, wk_word_sb, wk_scale_sb, FP8X4, C, packed_planes)
+        combine(Q_ROWS, "q", q_terms, q_parts)
+        v_terms = fetch_terms(v_slots, "v", ("raw4", "raw6"))
+        combine(V_ROWS, "v", v_terms, gate_plain_terms("v", v_terms, 0))
+
+        k_terms = [keep.tile([P, T], F32, name="k_term%d" % r) for r in range(2)]
+        k_pair = keep.tile([P, 2 * T], F32, name="k_pair", tag="raw8")
+        k_terms = [k_terms[0][:], k_terms[1][:], k_pair[:, 0:T], k_pair[:, T:]]
         partial = []
-        for t0, t1 in LAST_PIECES:
+        for h, (t0, t1) in enumerate(LAST_PIECES):
             for r in range(TOP - 1):
-                fetch(V_ROWS, r, t0, t1, v_terms[r][:, t0:t1])
-            turned_sb = stage.tile([P, t1 - t0], F32, name="turned_sb")
-            partial.append(add_up([term[:, t0:t1] for term in v_terms[: TOP - 1]], turned_sb[:]))
+                fetch_gated(k_slots, r, t0, t1, k_terms[r][:, t0:t1])
+            turned = turn_and_add(5 + 2 * h, [term[:, t0:t1] for term in k_terms[: TOP - 1]])
+            part = keep.tile([P, t1 - t0], F32, name="k_part%d" % h)
+            nc.scalar.copy(part[:], turned[:])
+            partial.append(turn_and_add(4 + 2 * h, [part[:]]))
         for (t0, t1), total in zip(LAST_PIECES, partial):
-            last_term = v_terms[TOP - 1][:, t0:t1]
-            fetch(V_ROWS, TOP - 1, t0, t1, last_term)
+            last_term = k_terms[TOP - 1][:, t0:t1]
+            fetch_gated(k_slots, TOP - 1, t0, t1, last_term)
             nc.vector.tensor_tensor(last_term, total[:], last_term, ADD)
-            store(V_ROWS, t0, t1, last_term)
+            store(K_ROWS, t0, t1, last_term)

@@ -17,26 +17,26 @@ FP4X4 = mybir.dt.float4_e2m1fn_x4
 MULT = mybir.AluOpType.mult
 ADD = mybir.AluOpType.add
 IDENTITY = mybir.ActivationFunctionType.Identity
-COPY = mybir.ActivationFunctionType.Copy
 
 P = 128
 PACK = 4
 PASSES = K // (P * PACK)
 SLOTS = E * C
 LIST_ROWS = 16
-WINDOW = 2048
+SCALE_WINDOW = 2048
+WORD_WINDOW = 1408
 BANKS = 8
 BANK = 512
 W_ROW = PASSES * PACK * N
-BLOCKS = T // P
+GATE_COLS = TOP * T // P
 HALF = T // 2
 SCALE_CHUNKS = ((0, 6), (6, 12))
-WORD_CHUNKS = ((0, 6), (6, 9), (9, 11), (11, 12))
+WORD_CHUNKS = ((0, 4), (4, 8), (8, 11), (11, 12))
 PAIRS = tuple((e, e + 2) for e in range(0, E, 2))
 QUANT = ((0, 4), (4, 8), (8, 10), (10, 12))
+WQ_LOADS = ((0, 4), (4, 12))
 LAST_PIECES = ((0, 512), (512, T))
 Q_ROWS, K_ROWS, V_ROWS = 0, 1, 2
-PLAIN_TERMS = 2
 
 
 def tile_moe_qkv_kernel(
@@ -49,35 +49,36 @@ def tile_moe_qkv_kernel(
 
         offs_sb = keep.tile([P, SLOTS // LIST_ROWS], U16, name="offs_sb")
         pos_sb = [keep.tile([P, T // LIST_ROWS], U16, name="pos_sb%d" % r) for r in range(TOP)]
-        x_scale_sb = keep.tile([P, WINDOW], U8, name="x_scale_sb", align_bytes=64)
-        x_word_sb = keep.tile([P, T + WINDOW], I32, name="x_word_sb", align_bytes=64)
+        x_scale_sb = keep.tile([P, SCALE_WINDOW], U8, name="x_scale_sb", align_bytes=64)
+        x_word_sb = keep.tile([P, T + WORD_WINDOW], I32, name="x_word_sb", align_bytes=64)
         slot_words = [keep.tile([P, SLOTS], U32, name="slot_words%d" % s, align_bytes=64) for s in range(PASSES)]
         slot_scales = keep.tile([P, SLOTS], U8, name="slot_scales", align_bytes=64)
         slot_scales_low = keep.tile([P, SLOTS], U8, name="slot_scales_low", align_bytes=64)
-        wq_word_sb = keep.tile([P, E * PASSES, 2 * N], U8, name="wq_word_sb", align_bytes=64)
+        wq_word_sb = {
+            e0: keep.tile([P, PASSES * (e1 - e0), 2 * N], U8, name="wq_word_sb%d" % e0, align_bytes=64)
+            for e0, e1 in WQ_LOADS
+        }
         wk_word_sb = keep.tile([P, E * PASSES, N], I32, name="wk_word_sb", align_bytes=64)
         wv_word_sb = keep.tile([P, E * PASSES, N], U32, name="wv_word_sb", align_bytes=64)
         wq_scale_sb = keep.tile([P, E * PASSES, N], U8, name="wq_scale_sb", align_bytes=64)
         wk_scale_sb = keep.tile([P, E * PASSES, N], U8, name="wk_scale_sb", align_bytes=64)
         wv_scale_sb = keep.tile([P, E * PASSES, N], U8, name="wv_scale_sb", align_bytes=64)
-        raw = {e0: keep.tile([P, 2 * W_ROW], F32, name="raw%d" % e0, tag="raw%d" % e0) for e0, e1 in PAIRS}
+        raw = {e0: keep.tile([P, 2 * W_ROW], F32, name="raw%d" % e0, tag="raw%d" % e0, align_bytes=64) for e0, e1 in PAIRS}
         rounded = {
-            e0: keep.tile([P, (e1 - e0) * W_ROW], BF16, name="rounded%d" % e0, align_bytes=64) for e0, e1 in QUANT
+            e0: keep.tile([P, (e1 - e0) * W_ROW], BF16, name="rounded%d" % e0, tag="rounded%d" % e0, align_bytes=64) for e0, e1 in QUANT
         }
-        gate_rows = keep.tile([P, P], F32, name="gate_rows")
-        gate_cols = keep.tile([P, TOP * BLOCKS], F32, name="gate_cols")
+        gate_cols = keep.tile([P, GATE_COLS], F32, name="gate_cols")
         gates = keep.tile([P, TOP * T], F32, name="gates")
         bias_sb = keep.tile([P, 3, E], F32, name="bias_sb")
         ident = keep.tile([P, P], F32, name="ident")
 
         nc.gpsimd.memset(x_scale_sb[:, 0:T].bitcast(I32), 0)
-        nc.gpsimd.memset(gate_rows[:], 0.0)
         make_identity(nc, ident[:])
-        nc.gpsimd.memset(wq_scale_sb[:].rearrange("p g n -> p (g n)").bitcast(I32), 0)
-        nc.gpsimd.memset(slot_scales_low[:].bitcast(I32), 0)
-        nc.gpsimd.memset(wk_scale_sb[:].rearrange("p g n -> p (g n)").bitcast(I32), 0)
         nc.vector.memset(x_scale_sb[:, T:].bitcast(I32), 0)
+        nc.vector.memset(wq_scale_sb[:].rearrange("p g n -> p (g n)").bitcast(I32), 0)
         nc.vector.memset(x_word_sb[:, PASSES * T :], 0)
+        nc.vector.memset(slot_scales_low[:].bitcast(I32), 0)
+        nc.vector.memset(wk_scale_sb[:].rearrange("p g n -> p (g n)").bitcast(I32), 0)
 
         def load_wv(e0):
             rows = wv.rearrange("e (s p j) n -> p (e s) (j n)", s=PASSES, j=PACK)
@@ -91,6 +92,10 @@ def tile_moe_qkv_kernel(
             for q in quadrants:
                 nc.sync.dma_start(out=plane[32 * q : 32 * q + 4].bitcast(I32), in_=rows[q].bitcast(I32))
 
+        def load_wq(e0, e1):
+            rows = wq_words.rearrange("e s p b -> p (e s) b").bitcast(I32)
+            nc.sync.dma_start(out=wq_word_sb[e0][:].bitcast(I32), in_=rows[:, PASSES * e0 : PASSES * e1])
+
         def load_pos(r):
             nc.sync.dma_start(pos_sb[r][:], (pos1, pos2, pos3, pos4)[r])
 
@@ -99,16 +104,17 @@ def tile_moe_qkv_kernel(
             nc.sync.dma_start(
                 out=x_scale_sb[32 * q : 32 * q + 8, 0:T].bitcast(I32), in_=x_scales[:, 4 * q : 4 * q + 4].bitcast(I32)
             )
+        nc.sync.dma_start(out=gate_cols[:], in_=gate[:, 0].rearrange("r (c i) -> r c i", i=GATE_COLS))
+        load_wv(0)
         nc.sync.dma_start(
             out=x_word_sb[:, 0 : PASSES * T].rearrange("p (s t) -> p s t", s=PASSES),
             in_=x_words.rearrange("s p t d -> p s (t d)").bitcast(I32),
         )
-        nc.sync.dma_start(out=gate_rows[0 : TOP * BLOCKS], in_=gate[:, 0].rearrange("r (b m) -> r b m", m=P))
-        for e0 in (0, 2, 4, 6):
+        for e0 in (2, 4, 6):
             load_wv(e0)
         nc.sync.dma_start(out=bias_sb[:], in_=bias.rearrange("(j p) e -> p j e", p=P))
         load_weight_scales(wq_scale_sb, wq_scales, range(4))
-        nc.sync.dma_start(out=wq_word_sb[:].bitcast(I32), in_=wq_words.rearrange("e s p b -> p (e s) b").bitcast(I32))
+        load_wq(*WQ_LOADS[0])
 
         def entries(list_tile, first, last):
             return list_tile[:, first // LIST_ROWS : last // LIST_ROWS]
@@ -119,7 +125,7 @@ def tile_moe_qkv_kernel(
             )
         for e0, e1 in WORD_CHUNKS:
             for s in range(PASSES):
-                window = x_word_sb[:, s * T : s * T + WINDOW].bitcast(U32)
+                window = x_word_sb[:, s * T : s * T + WORD_WINDOW].bitcast(U32)
                 nc.vector.tensor_copy(
                     slot_words[s][:, e0 * C : e1 * C], window.indirect(entries(offs_sb, e0 * C, e1 * C))
                 )
@@ -129,28 +135,26 @@ def tile_moe_qkv_kernel(
                 in_=slot_scales[32 * q + 4 : 32 * q + 8].bitcast(I32),
             )
         load_wv(8)
-        load_pos(0)
-        load_pos(1)
+        load_wq(*WQ_LOADS[1])
+        for r in range(TOP):
+            load_pos(r)
         load_wv(10)
-        load_pos(2)
-        load_weight_scales(wk_scale_sb, wk_scales, (0, 1))
-        load_pos(3)
-        load_weight_scales(wk_scale_sb, wk_scales, (2, 3))
+        load_weight_scales(wk_scale_sb, wk_scales, range(4))
         nc.sync.dma_start(out=wk_word_sb[:], in_=wk_words.rearrange("e s p n d -> p (e s) (n d)").bitcast(I32))
 
         def bank(b, width):
             return psum.tile([P, width], F32, name="bank%d" % (b % BANKS))
 
-        turned_gates = bank(0, P)
-        nc.tensor.transpose(turned_gates[:], gate_rows[:], ident[:])
-        nc.scalar.copy(gate_cols[:], turned_gates[:, 0 : TOP * BLOCKS])
         per_bank = BANK // P
-        for i0 in range(0, TOP * BLOCKS, per_bank):
-            spread = bank(1 + i0 // per_bank, BANK)
+        for i0 in range(0, GATE_COLS, per_bank):
+            spread = bank(i0 // per_bank, BANK)
             for i in range(per_bank):
                 column = gate_cols[:, i0 + i : i0 + i + 1].to_broadcast([P, P])
                 nc.tensor.transpose(spread[:, i * P : (i + 1) * P], column, ident[:])
-            nc.scalar.copy(gates[:, i0 * P : (i0 + per_bank) * P], spread[:])
+            nc.scalar.copy(
+                gates[:].rearrange("p (m i) -> p m i", i=GATE_COLS)[:, :, i0 : i0 + per_bank],
+                spread[:].rearrange("p (i m) -> p m i", i=per_bank),
+            )
 
         def rounded_part(e0, e1):
             g0 = max(g for g, g1 in QUANT if g <= e0)
@@ -161,18 +165,6 @@ def tile_moe_qkv_kernel(
                 rounded_part(e0, e0 + 2).rearrange("p (g c i j) -> p g c j i", c=N // 4, i=4, j=PACK),
                 raw[e0][:].rearrange("p (g j c i) -> p g c j i", c=N // 4, i=4, j=PACK),
             )
-
-        def round_wv_gpsimd(e0):
-            for g in range(2 * PASSES):
-                cols = slice(g * PACK * N, (g + 1) * PACK * N)
-                nc.gpsimd.tensor_scalar(
-                    rounded_part(e0, e0 + 2)[:, cols].rearrange("p (n j) -> p n j", j=PACK),
-                    raw[e0][:, cols].rearrange("p (j n) -> p n j", j=PACK),
-                    1.0,
-                    0.0,
-                    MULT,
-                    ADD,
-                )
 
         def quantize_wv(e0, e1):
             group = slice(PASSES * e0, PASSES * e1)
@@ -189,7 +181,7 @@ def tile_moe_qkv_kernel(
                 for s in range(PASSES):
                     nc.tensor.matmul_mx(
                         out=acc[:, u0 : u0 + width],
-                        lhsT=words[:, PASSES * e + s].bitcast(dtype),
+                        lhsT=words[:, s].bitcast(dtype),
                         lhsT_scale=scales[:, PASSES * e + s],
                         rhs=slot_words[s][:, slots].bitcast(FP8X4),
                         rhs_scale=token_scales[s][:, slots],
@@ -198,21 +190,24 @@ def tile_moe_qkv_kernel(
                     )
             nc.scalar.activation(results[:, e * C : (e + 1) * C], acc[:], IDENTITY, bias=bias_sb[:, j, e : e + 1])
 
+        def expert(words, i):
+            return words[:, PASSES * i : PASSES * (i + 1)]
+
         packed_planes = (slot_scales[:], slot_scales[4:P])
         low_planes = (slot_scales[:], slot_scales_low[:])
 
-        for e0 in (0, 2, 4, 6):
+        for e0 in (0, 2, 4, 6, 8):
             round_wv(e0)
-        round_wv_gpsimd(8)
         q_slots = keep.tile([P, SLOTS], F32, name="q_slots")
-        for e in range(E):
-            project(q_slots, Q_ROWS, e, e, wq_word_sb, wq_scale_sb, FP4X4, C // 2, low_planes)
+        for e0, e1 in WQ_LOADS:
+            for e in range(e0, e1):
+                project(q_slots, Q_ROWS, e, e, expert(wq_word_sb[e0], e - e0), wq_scale_sb, FP4X4, C // 2, low_planes)
         round_wv(10)
         for e0, e1 in QUANT:
             quantize_wv(e0, e1)
-        v_slots = keep.tile([P, SLOTS], F32, name="v_slots", tag="raw10")
+        v_slots = keep.tile([P, SLOTS], F32, name="v_slots", tag="raw10", align_bytes=64)
         for e in range(E):
-            project(v_slots, V_ROWS, e, E + e, wv_word_sb, wv_scale_sb, FP8X4, C, packed_planes)
+            project(v_slots, V_ROWS, e, e % 4, expert(wv_word_sb, e), wv_scale_sb, FP8X4, C, packed_planes)
 
         def fetch_gated(results, r, t0, t1, term):
             nc.vector.tensor_tensor(
@@ -238,61 +233,41 @@ def tile_moe_qkv_kernel(
             nc.sync.dma_start(out=out[j * N : (j + 1) * N, t0:t1], in_=result)
 
         def fetch_terms(results, name, tags):
-            pairs = [keep.tile([P, 2 * T], F32, name="%s_terms%d" % (name, h), tag=tags[h]) for h in range(2)]
+            pairs = [keep.tile([P, 2 * T], F32, name="%s_terms%d" % (name, h), tag=tags[h], align_bytes=64) for h in range(2)]
             terms = [pairs[r // 2][:, (r % 2) * T : (r % 2 + 1) * T] for r in range(TOP)]
-            for r in range(PLAIN_TERMS):
-                nc.vector.tensor_copy(terms[r], results[:].indirect(pos_sb[r][:]))
-            for r in range(PLAIN_TERMS, TOP):
+            for r in range(TOP):
                 fetch_gated(results, r, 0, T, terms[r])
             return terms
 
-        def gate_plain_terms(name, terms, first_bank):
-            parts = []
+        def combine(j, name, terms):
             for h in range(2):
                 t0 = h * HALF
-                parts.append([])
-                for r in range(PLAIN_TERMS):
-                    turned = turn_and_add(first_bank + 2 * h + r, [terms[r][:, t0 : t0 + HALF]])
-                    part = keep.tile([P, HALF], F32, name="%s_part%d_%d" % (name, h, r))
-                    for c0 in range(0, HALF, P):
-                        column = r * BLOCKS + (t0 + c0) // P
-                        nc.scalar.activation(
-                            part[:, c0 : c0 + P], turned[:, c0 : c0 + P], COPY, scale=gate_cols[:, column : column + 1]
-                        )
-                    parts[h].append(part[:])
-            return parts
-
-        def combine(j, name, terms, parts):
-            for h in range(2):
-                t0 = h * HALF
-                turned = turn_and_add(4 + 2 * h, [term[:, t0 : t0 + HALF] for term in terms[PLAIN_TERMS:]])
-                rest = keep.tile([P, HALF], F32, name="%s_rest%d" % (name, h))
-                nc.scalar.copy(rest[:], turned[:])
-                total = turn_and_add(5 + 2 * h, parts[h] + [rest[:]])
+                turned = turn_and_add(4 + h, [term[:, t0 : t0 + HALF] for term in terms])
+                summed = keep.tile([P, HALF], F32, name="%s_summed%d" % (name, h))
+                nc.scalar.copy(summed[:], turned[:])
+                total = turn_and_add(6 + h, [summed[:]])
                 result = keep.tile([P, HALF], F32, name="%s_result%d" % (name, h))
                 nc.scalar.copy(result[:], total[:])
                 store(j, t0, t0 + HALF, result[:])
 
-        q_terms = fetch_terms(q_slots, "q", ("raw0", "raw2"))
-        q_parts = gate_plain_terms("q", q_terms, 4)
+        q_terms = fetch_terms(q_slots, "q", ("raw0", "rounded10"))
         k_slots = keep.tile([P, SLOTS], F32, name="k_slots")
         for e in range(E):
-            project(k_slots, K_ROWS, e, e, wk_word_sb, wk_scale_sb, FP8X4, C, packed_planes)
-        combine(Q_ROWS, "q", q_terms, q_parts)
-        v_terms = fetch_terms(v_slots, "v", ("raw4", "raw6"))
-        combine(V_ROWS, "v", v_terms, gate_plain_terms("v", v_terms, 0))
+            project(k_slots, K_ROWS, e, 4 + e % 4, expert(wk_word_sb, e), wk_scale_sb, FP8X4, C, packed_planes)
+        combine(Q_ROWS, "q", q_terms)
+        combine(V_ROWS, "v", fetch_terms(v_slots, "v", ("raw4", "raw6")))
 
         k_terms = [keep.tile([P, T], F32, name="k_term%d" % r) for r in range(2)]
-        k_pair = keep.tile([P, 2 * T], F32, name="k_pair", tag="raw8")
+        k_pair = keep.tile([P, 2 * T], F32, name="k_pair", tag="raw8", align_bytes=64)
         k_terms = [k_terms[0][:], k_terms[1][:], k_pair[:, 0:T], k_pair[:, T:]]
         partial = []
         for h, (t0, t1) in enumerate(LAST_PIECES):
             for r in range(TOP - 1):
                 fetch_gated(k_slots, r, t0, t1, k_terms[r][:, t0:t1])
-            turned = turn_and_add(5 + 2 * h, [term[:, t0:t1] for term in k_terms[: TOP - 1]])
+            turned = turn_and_add(4 + h, [term[:, t0:t1] for term in k_terms[: TOP - 1]])
             part = keep.tile([P, t1 - t0], F32, name="k_part%d" % h)
             nc.scalar.copy(part[:], turned[:])
-            partial.append(turn_and_add(4 + 2 * h, [part[:]]))
+            partial.append(turn_and_add(6 + h, [part[:]]))
         for (t0, t1), total in zip(LAST_PIECES, partial):
             last_term = k_terms[TOP - 1][:, t0:t1]
             fetch_gated(k_slots, TOP - 1, t0, t1, last_term)

@@ -35,6 +35,8 @@ WORD_CHUNKS = ((0, 4), (4, 8), (8, 11), (11, 12))
 PAIRS = tuple((e, e + 2) for e in range(0, E, 2))
 QUANT = ((0, 4), (4, 8), (8, 10), (10, 12))
 WQ_LOADS = ((0, 4), (4, 12))
+WK_LOADS = ((0, 6), (6, 10), (10, 12))
+K_BANKS = (4, 5, 6, 7, 0, 1, 4, 5, 6, 7, 4, 5)
 LAST_PIECES = ((0, 512), (512, T))
 Q_ROWS, K_ROWS, V_ROWS = 0, 1, 2
 
@@ -58,7 +60,10 @@ def tile_moe_qkv_kernel(
             e0: keep.tile([P, PASSES * (e1 - e0), 2 * N], U8, name="wq_word_sb%d" % e0, align_bytes=64)
             for e0, e1 in WQ_LOADS
         }
-        wk_word_sb = keep.tile([P, E * PASSES, N], I32, name="wk_word_sb", align_bytes=64)
+        wk_word_sb = {
+            e0: keep.tile([P, PASSES * (e1 - e0), N], I32, name="wk_word_sb%d" % e0, align_bytes=64)
+            for e0, e1 in WK_LOADS
+        }
         wv_word_sb = keep.tile([P, E * PASSES, N], U32, name="wv_word_sb", align_bytes=64)
         wq_scale_sb = keep.tile([P, E * PASSES, N], U8, name="wq_scale_sb", align_bytes=64)
         wk_scale_sb = keep.tile([P, E * PASSES, N], U8, name="wk_scale_sb", align_bytes=64)
@@ -87,10 +92,10 @@ def tile_moe_qkv_kernel(
                 in_=rows[:, PASSES * e0 : PASSES * (e0 + 2)],
             )
 
-        def load_weight_scales(plane, scales, quadrants):
-            rows = scales.rearrange("e s (q j) n -> q j (e s) n", j=4)
-            for q in quadrants:
-                nc.sync.dma_start(out=plane[32 * q : 32 * q + 4].bitcast(I32), in_=rows[q].bitcast(I32))
+        def load_weight_scales(plane, scales):
+            rows = scales.rearrange("e s (q j) n -> j q (e s) n", j=4)
+            for j in range(4):
+                nc.sync.dma_start(out=plane[j:P:32].bitcast(I32), in_=rows[j].bitcast(I32))
 
         def load_wq(e0, e1):
             rows = wq_words.rearrange("e s p b -> p (e s) b").bitcast(I32)
@@ -113,7 +118,7 @@ def tile_moe_qkv_kernel(
         for e0 in (2, 4, 6):
             load_wv(e0)
         nc.sync.dma_start(out=bias_sb[:], in_=bias.rearrange("(j p) e -> p j e", p=P))
-        load_weight_scales(wq_scale_sb, wq_scales, range(4))
+        load_weight_scales(wq_scale_sb, wq_scales)
         load_wq(*WQ_LOADS[0])
 
         def entries(list_tile, first, last):
@@ -129,18 +134,17 @@ def tile_moe_qkv_kernel(
                 nc.vector.tensor_copy(
                     slot_words[s][:, e0 * C : e1 * C], window.indirect(entries(offs_sb, e0 * C, e1 * C))
                 )
-        for q in range(4):
-            nc.sync.dma_start(
-                out=slot_scales_low[32 * q : 32 * q + 4].bitcast(I32),
-                in_=slot_scales[32 * q + 4 : 32 * q + 8].bitcast(I32),
-            )
+        for j in range(4):
+            nc.sync.dma_start(out=slot_scales_low[j:P:32].bitcast(I32), in_=slot_scales[4 + j : P : 32].bitcast(I32))
         load_wv(8)
         load_wq(*WQ_LOADS[1])
         for r in range(TOP):
             load_pos(r)
         load_wv(10)
-        load_weight_scales(wk_scale_sb, wk_scales, range(4))
-        nc.sync.dma_start(out=wk_word_sb[:], in_=wk_words.rearrange("e s p n d -> p (e s) (n d)").bitcast(I32))
+        load_weight_scales(wk_scale_sb, wk_scales)
+        for e0, e1 in WK_LOADS:
+            rows = wk_words.rearrange("e s p n d -> p (e s) (n d)").bitcast(I32)
+            nc.sync.dma_start(out=wk_word_sb[e0][:], in_=rows[:, PASSES * e0 : PASSES * e1])
 
         def bank(b, width):
             return psum.tile([P, width], F32, name="bank%d" % (b % BANKS))
@@ -214,19 +218,22 @@ def tile_moe_qkv_kernel(
                 term, results[:].indirect(entries(pos_sb[r], t0, t1)), gates[:, r * T + t0 : r * T + t1], MULT
             )
 
+        def turn_into(turned, source, first, last):
+            width = source.shape[1]
+            for c0 in range(0, width, P):
+                nc.tensor.matmul(
+                    turned[:, c0 : c0 + P],
+                    source[:, c0 : c0 + P],
+                    ident[:],
+                    start=(first and c0 == 0),
+                    stop=(last and c0 == width - P),
+                    is_transpose=True,
+                )
+
         def turn_and_add(b, sources):
-            width = sources[0].shape[1]
-            turned = bank(b, width)
+            turned = bank(b, sources[0].shape[1])
             for i, source in enumerate(sources):
-                for c0 in range(0, width, P):
-                    nc.tensor.matmul(
-                        turned[:, c0 : c0 + P],
-                        source[:, c0 : c0 + P],
-                        ident[:],
-                        start=(i == 0 and c0 == 0),
-                        stop=(i == len(sources) - 1 and c0 == width - P),
-                        is_transpose=True,
-                    )
+                turn_into(turned, source, i == 0, i == len(sources) - 1)
             return turned
 
         def store(j, t0, t1, result):
@@ -239,23 +246,28 @@ def tile_moe_qkv_kernel(
                 fetch_gated(results, r, 0, T, terms[r])
             return terms
 
-        def combine(j, name, terms):
+        def combine(j, name, terms, turn_bank, total_bank):
+            turned = [bank(turn_bank + h, HALF) for h in range(2)]
+            for r, term in enumerate(terms):
+                for h in range(2):
+                    turn_into(turned[h], term[:, h * HALF : (h + 1) * HALF], r == 0, r == TOP - 1)
             for h in range(2):
-                t0 = h * HALF
-                turned = turn_and_add(4 + h, [term[:, t0 : t0 + HALF] for term in terms])
                 summed = keep.tile([P, HALF], F32, name="%s_summed%d" % (name, h))
-                nc.scalar.copy(summed[:], turned[:])
-                total = turn_and_add(6 + h, [summed[:]])
+                nc.scalar.copy(summed[:], turned[h][:])
+                total = turn_and_add(total_bank + h, [summed[:]])
                 result = keep.tile([P, HALF], F32, name="%s_result%d" % (name, h))
                 nc.scalar.copy(result[:], total[:])
-                store(j, t0, t0 + HALF, result[:])
+                store(j, h * HALF, (h + 1) * HALF, result[:])
 
         q_terms = fetch_terms(q_slots, "q", ("raw0", "rounded10"))
+        combine(Q_ROWS, "q", q_terms, 0, 2)
         k_slots = keep.tile([P, SLOTS], F32, name="k_slots")
-        for e in range(E):
-            project(k_slots, K_ROWS, e, 4 + e % 4, expert(wk_word_sb, e), wk_scale_sb, FP8X4, C, packed_planes)
-        combine(Q_ROWS, "q", q_terms)
-        combine(V_ROWS, "v", fetch_terms(v_slots, "v", ("raw4", "raw6")))
+        for e0, e1 in WK_LOADS:
+            for e in range(e0, e1):
+                project(
+                    k_slots, K_ROWS, e, K_BANKS[e], expert(wk_word_sb[e0], e - e0), wk_scale_sb, FP8X4, C, packed_planes
+                )
+        combine(V_ROWS, "v", fetch_terms(v_slots, "v", ("raw4", "raw6")), 0, 2)
 
         k_terms = [keep.tile([P, T], F32, name="k_term%d" % r) for r in range(2)]
         k_pair = keep.tile([P, 2 * T], F32, name="k_pair", tag="raw8", align_bytes=64)

@@ -33,10 +33,10 @@ HALF = T // 2
 SCALE_CHUNKS = ((0, 6), (6, 12))
 WORD_CHUNKS = ((0, 4), (4, 8), (8, 11), (11, 12))
 PAIRS = tuple((e, e + 2) for e in range(0, E, 2))
-QUANT = ((0, 4), (4, 8), (8, 10), (10, 12))
+QUANT = ((0, 4), (4, 8), (8, 12))
 WQ_LOADS = ((0, 4), (4, 12))
 WK_LOADS = ((0, 6), (6, 10), (10, 12))
-K_BANKS = (4, 5, 6, 7, 0, 1, 4, 5, 6, 7, 4, 5)
+K_BANKS = (4, 5, 6, 7, 4, 5, 6, 7, 4, 5, 0, 1)
 LAST_PIECES = ((0, 512), (512, T))
 Q_ROWS, K_ROWS, V_ROWS = 0, 1, 2
 
@@ -57,7 +57,7 @@ def tile_moe_qkv_kernel(
         slot_scales = keep.tile([P, SLOTS], U8, name="slot_scales", align_bytes=64)
         slot_scales_low = keep.tile([P, SLOTS], U8, name="slot_scales_low", align_bytes=64)
         wq_word_sb = {
-            e0: keep.tile([P, PASSES * (e1 - e0), 2 * N], U8, name="wq_word_sb%d" % e0, align_bytes=64)
+            e0: keep.tile([P, PASSES * (e1 - e0), 2 * N], U8, name="wq_word_sb%d" % e0, tag="wq%d" % e0, align_bytes=64)
             for e0, e1 in WQ_LOADS
         }
         wk_word_sb = {
@@ -70,7 +70,7 @@ def tile_moe_qkv_kernel(
         wv_scale_sb = keep.tile([P, E * PASSES, N], U8, name="wv_scale_sb", align_bytes=64)
         raw = {e0: keep.tile([P, 2 * W_ROW], F32, name="raw%d" % e0, tag="raw%d" % e0, align_bytes=64) for e0, e1 in PAIRS}
         rounded = {
-            e0: keep.tile([P, (e1 - e0) * W_ROW], BF16, name="rounded%d" % e0, tag="rounded%d" % e0, align_bytes=64) for e0, e1 in QUANT
+            e0: keep.tile([P, (e1 - e0) * W_ROW], BF16, name="rounded%d" % e0, align_bytes=64) for e0, e1 in QUANT[:2]
         }
         gate_cols = keep.tile([P, GATE_COLS], F32, name="gate_cols")
         gates = keep.tile([P, TOP * T], F32, name="gates")
@@ -79,11 +79,11 @@ def tile_moe_qkv_kernel(
 
         nc.gpsimd.memset(x_scale_sb[:, 0:T].bitcast(I32), 0)
         make_identity(nc, ident[:])
+        nc.vector.memset(wk_scale_sb[:].rearrange("p g n -> p (g n)").bitcast(I32), 0)
         nc.vector.memset(x_scale_sb[:, T:].bitcast(I32), 0)
         nc.vector.memset(wq_scale_sb[:].rearrange("p g n -> p (g n)").bitcast(I32), 0)
         nc.vector.memset(x_word_sb[:, PASSES * T :], 0)
         nc.vector.memset(slot_scales_low[:].bitcast(I32), 0)
-        nc.vector.memset(wk_scale_sb[:].rearrange("p g n -> p (g n)").bitcast(I32), 0)
 
         def load_wv(e0):
             rows = wv.rearrange("e (s p j) n -> p (e s) (j n)", s=PASSES, j=PACK)
@@ -109,17 +109,20 @@ def tile_moe_qkv_kernel(
             nc.sync.dma_start(
                 out=x_scale_sb[32 * q : 32 * q + 8, 0:T].bitcast(I32), in_=x_scales[:, 4 * q : 4 * q + 4].bitcast(I32)
             )
-        nc.sync.dma_start(out=gate_cols[:], in_=gate[:, 0].rearrange("r (c i) -> r c i", i=GATE_COLS))
-        load_wv(0)
+        load_weight_scales(wk_scale_sb, wk_scales)
+        load_weight_scales(wq_scale_sb, wq_scales)
         nc.sync.dma_start(
             out=x_word_sb[:, 0 : PASSES * T].rearrange("p (s t) -> p s t", s=PASSES),
             in_=x_words.rearrange("s p t d -> p s (t d)").bitcast(I32),
         )
-        for e0 in (2, 4, 6):
-            load_wv(e0)
+        nc.sync.dma_start(out=gate_cols[:], in_=gate[:, 0].rearrange("r (c i) -> r c i", i=GATE_COLS))
         nc.sync.dma_start(out=bias_sb[:], in_=bias.rearrange("(j p) e -> p j e", p=P))
-        load_weight_scales(wq_scale_sb, wq_scales)
+        for r in range(TOP):
+            load_pos(r)
+        for e0 in (0, 2, 4):
+            load_wv(e0)
         load_wq(*WQ_LOADS[0])
+        load_wv(6)
 
         def entries(list_tile, first, last):
             return list_tile[:, first // LIST_ROWS : last // LIST_ROWS]
@@ -136,12 +139,9 @@ def tile_moe_qkv_kernel(
                 )
         for j in range(4):
             nc.sync.dma_start(out=slot_scales_low[j:P:32].bitcast(I32), in_=slot_scales[4 + j : P : 32].bitcast(I32))
-        load_wv(8)
         load_wq(*WQ_LOADS[1])
-        for r in range(TOP):
-            load_pos(r)
+        load_wv(8)
         load_wv(10)
-        load_weight_scales(wk_scale_sb, wk_scales)
         for e0, e1 in WK_LOADS:
             rows = wk_words.rearrange("e s p n d -> p (e s) (n d)").bitcast(I32)
             nc.sync.dma_start(out=wk_word_sb[e0][:], in_=rows[:, PASSES * e0 : PASSES * e1])
@@ -200,12 +200,14 @@ def tile_moe_qkv_kernel(
         packed_planes = (slot_scales[:], slot_scales[4:P])
         low_planes = (slot_scales[:], slot_scales_low[:])
 
-        for e0 in (0, 2, 4, 6, 8):
+        for e0 in (0, 2, 4, 6):
             round_wv(e0)
         q_slots = keep.tile([P, SLOTS], F32, name="q_slots")
         for e0, e1 in WQ_LOADS:
             for e in range(e0, e1):
                 project(q_slots, Q_ROWS, e, e, expert(wq_word_sb[e0], e - e0), wq_scale_sb, FP4X4, C // 2, low_planes)
+        rounded[8] = keep.tile([P, 4 * W_ROW], BF16, name="rounded8", tag="wq4", align_bytes=64)
+        round_wv(8)
         round_wv(10)
         for e0, e1 in QUANT:
             quantize_wv(e0, e1)
@@ -259,7 +261,7 @@ def tile_moe_qkv_kernel(
                 nc.scalar.copy(result[:], total[:])
                 store(j, h * HALF, (h + 1) * HALF, result[:])
 
-        q_terms = fetch_terms(q_slots, "q", ("raw0", "rounded10"))
+        q_terms = fetch_terms(q_slots, "q", ("raw0", "wq4"))
         combine(Q_ROWS, "q", q_terms, 0, 2)
         k_slots = keep.tile([P, SLOTS], F32, name="k_slots")
         for e0, e1 in WK_LOADS:

@@ -33,10 +33,10 @@ HALF = T // 2
 SCALE_CHUNKS = ((0, 6), (6, 12))
 WORD_CHUNKS = ((0, 4), (4, 8), (8, 11), (11, 12))
 PAIRS = tuple((e, e + 2) for e in range(0, E, 2))
-QUANT = ((0, 4), (4, 8), (8, 12))
-WQ_LOADS = ((0, 4), (4, 12))
+ROUNDED = ((0, 4), (4, 8), (8, 12))
+QUANT = ((0, 4), (4, 8), (8, 10), (10, 12))
 WK_LOADS = ((0, 6), (6, 10), (10, 12))
-K_BANKS = (4, 5, 6, 7, 4, 5, 6, 7, 4, 5, 0, 1)
+K_BANKS = (0, 1, 2, 3, 4, 5, 0, 1, 2, 3, 6, 7)
 LAST_PIECES = ((0, 512), (512, T))
 Q_ROWS, K_ROWS, V_ROWS = 0, 1, 2
 
@@ -56,10 +56,7 @@ def tile_moe_qkv_kernel(
         slot_words = [keep.tile([P, SLOTS], U32, name="slot_words%d" % s, align_bytes=64) for s in range(PASSES)]
         slot_scales = keep.tile([P, SLOTS], U8, name="slot_scales", align_bytes=64)
         slot_scales_low = keep.tile([P, SLOTS], U8, name="slot_scales_low", align_bytes=64)
-        wq_word_sb = {
-            e0: keep.tile([P, PASSES * (e1 - e0), 2 * N], U8, name="wq_word_sb%d" % e0, tag="wq%d" % e0, align_bytes=64)
-            for e0, e1 in WQ_LOADS
-        }
+        wq_word_sb = keep.tile([P, E * PASSES, 2 * N], U8, name="wq_word_sb", tag="wq", align_bytes=64)
         wk_word_sb = {
             e0: keep.tile([P, PASSES * (e1 - e0), N], I32, name="wk_word_sb%d" % e0, align_bytes=64)
             for e0, e1 in WK_LOADS
@@ -70,7 +67,7 @@ def tile_moe_qkv_kernel(
         wv_scale_sb = keep.tile([P, E * PASSES, N], U8, name="wv_scale_sb", align_bytes=64)
         raw = {e0: keep.tile([P, 2 * W_ROW], F32, name="raw%d" % e0, tag="raw%d" % e0, align_bytes=64) for e0, e1 in PAIRS}
         rounded = {
-            e0: keep.tile([P, (e1 - e0) * W_ROW], BF16, name="rounded%d" % e0, align_bytes=64) for e0, e1 in QUANT[:2]
+            e0: keep.tile([P, (e1 - e0) * W_ROW], BF16, name="rounded%d" % e0, align_bytes=64) for e0, e1 in ROUNDED[:2]
         }
         gate_cols = keep.tile([P, GATE_COLS], F32, name="gate_cols")
         gates = keep.tile([P, TOP * T], F32, name="gates")
@@ -79,11 +76,11 @@ def tile_moe_qkv_kernel(
 
         nc.gpsimd.memset(x_scale_sb[:, 0:T].bitcast(I32), 0)
         make_identity(nc, ident[:])
-        nc.vector.memset(wk_scale_sb[:].rearrange("p g n -> p (g n)").bitcast(I32), 0)
         nc.vector.memset(x_scale_sb[:, T:].bitcast(I32), 0)
         nc.vector.memset(wq_scale_sb[:].rearrange("p g n -> p (g n)").bitcast(I32), 0)
         nc.vector.memset(x_word_sb[:, PASSES * T :], 0)
         nc.vector.memset(slot_scales_low[:].bitcast(I32), 0)
+        nc.vector.memset(wk_scale_sb[:].rearrange("p g n -> p (g n)").bitcast(I32), 0)
 
         def load_wv(e0):
             rows = wv.rearrange("e (s p j) n -> p (e s) (j n)", s=PASSES, j=PACK)
@@ -97,10 +94,6 @@ def tile_moe_qkv_kernel(
             for j in range(4):
                 nc.sync.dma_start(out=plane[j:P:32].bitcast(I32), in_=rows[j].bitcast(I32))
 
-        def load_wq(e0, e1):
-            rows = wq_words.rearrange("e s p b -> p (e s) b").bitcast(I32)
-            nc.sync.dma_start(out=wq_word_sb[e0][:].bitcast(I32), in_=rows[:, PASSES * e0 : PASSES * e1])
-
         def load_pos(r):
             nc.sync.dma_start(pos_sb[r][:], (pos1, pos2, pos3, pos4)[r])
 
@@ -109,20 +102,18 @@ def tile_moe_qkv_kernel(
             nc.sync.dma_start(
                 out=x_scale_sb[32 * q : 32 * q + 8, 0:T].bitcast(I32), in_=x_scales[:, 4 * q : 4 * q + 4].bitcast(I32)
             )
-        load_weight_scales(wk_scale_sb, wk_scales)
-        load_weight_scales(wq_scale_sb, wq_scales)
+        load_wv(0)
         nc.sync.dma_start(
             out=x_word_sb[:, 0 : PASSES * T].rearrange("p (s t) -> p s t", s=PASSES),
             in_=x_words.rearrange("s p t d -> p s (t d)").bitcast(I32),
         )
+        load_weight_scales(wq_scale_sb, wq_scales)
         nc.sync.dma_start(out=gate_cols[:], in_=gate[:, 0].rearrange("r (c i) -> r c i", i=GATE_COLS))
         nc.sync.dma_start(out=bias_sb[:], in_=bias.rearrange("(j p) e -> p j e", p=P))
         for r in range(TOP):
             load_pos(r)
-        for e0 in (0, 2, 4):
-            load_wv(e0)
-        load_wq(*WQ_LOADS[0])
-        load_wv(6)
+        load_wv(2)
+        load_wv(4)
 
         def entries(list_tile, first, last):
             return list_tile[:, first // LIST_ROWS : last // LIST_ROWS]
@@ -139,9 +130,11 @@ def tile_moe_qkv_kernel(
                 )
         for j in range(4):
             nc.sync.dma_start(out=slot_scales_low[j:P:32].bitcast(I32), in_=slot_scales[4 + j : P : 32].bitcast(I32))
-        load_wq(*WQ_LOADS[1])
+        nc.sync.dma_start(out=wq_word_sb[:].bitcast(I32), in_=wq_words.rearrange("e s p b -> p (e s) b").bitcast(I32))
+        load_wv(6)
         load_wv(8)
         load_wv(10)
+        load_weight_scales(wk_scale_sb, wk_scales)
         for e0, e1 in WK_LOADS:
             rows = wk_words.rearrange("e s p n d -> p (e s) (n d)").bitcast(I32)
             nc.sync.dma_start(out=wk_word_sb[e0][:], in_=rows[:, PASSES * e0 : PASSES * e1])
@@ -161,7 +154,7 @@ def tile_moe_qkv_kernel(
             )
 
         def rounded_part(e0, e1):
-            g0 = max(g for g, g1 in QUANT if g <= e0)
+            g0 = max(g for g, g1 in ROUNDED if g <= e0)
             return rounded[g0][:, (e0 - g0) * W_ROW : (e1 - g0) * W_ROW]
 
         def round_wv(e0):
@@ -175,7 +168,7 @@ def tile_moe_qkv_kernel(
             nc.vector.quantize_mx(
                 out=wv_word_sb[:, group].rearrange("p g n -> p (g n)").bitcast(FP8X4),
                 scales=wv_scale_sb[:, group].rearrange("p g n -> p (g n)"),
-                in_=rounded[e0][:],
+                in_=rounded_part(e0, e1),
             )
 
         def project(results, j, e, b, words, scales, dtype, width, token_scales):
@@ -203,17 +196,16 @@ def tile_moe_qkv_kernel(
         for e0 in (0, 2, 4, 6):
             round_wv(e0)
         q_slots = keep.tile([P, SLOTS], F32, name="q_slots")
-        for e0, e1 in WQ_LOADS:
-            for e in range(e0, e1):
-                project(q_slots, Q_ROWS, e, e, expert(wq_word_sb[e0], e - e0), wq_scale_sb, FP4X4, C // 2, low_planes)
-        rounded[8] = keep.tile([P, 4 * W_ROW], BF16, name="rounded8", tag="wq4", align_bytes=64)
+        for e in range(E):
+            project(q_slots, Q_ROWS, e, e, expert(wq_word_sb, e), wq_scale_sb, FP4X4, C // 2, low_planes)
+        rounded[8] = keep.tile([P, 4 * W_ROW], BF16, name="rounded8", tag="wq", align_bytes=64)
         round_wv(8)
         round_wv(10)
         for e0, e1 in QUANT:
             quantize_wv(e0, e1)
         v_slots = keep.tile([P, SLOTS], F32, name="v_slots", tag="raw10", align_bytes=64)
         for e in range(E):
-            project(v_slots, V_ROWS, e, e % 4, expert(wv_word_sb, e), wv_scale_sb, FP8X4, C, packed_planes)
+            project(v_slots, V_ROWS, e, E + e, expert(wv_word_sb, e), wv_scale_sb, FP8X4, C, packed_planes)
 
         def fetch_gated(results, r, t0, t1, term):
             nc.vector.tensor_tensor(
@@ -242,7 +234,9 @@ def tile_moe_qkv_kernel(
             nc.sync.dma_start(out=out[j * N : (j + 1) * N, t0:t1], in_=result)
 
         def fetch_terms(results, name, tags):
-            pairs = [keep.tile([P, 2 * T], F32, name="%s_terms%d" % (name, h), tag=tags[h], align_bytes=64) for h in range(2)]
+            pairs = [
+                keep.tile([P, 2 * T], F32, name="%s_terms%d" % (name, h), tag=tags[h], align_bytes=64) for h in range(2)
+            ]
             terms = [pairs[r // 2][:, (r % 2) * T : (r % 2 + 1) * T] for r in range(TOP)]
             for r in range(TOP):
                 fetch_gated(results, r, 0, T, terms[r])
@@ -261,15 +255,15 @@ def tile_moe_qkv_kernel(
                 nc.scalar.copy(result[:], total[:])
                 store(j, h * HALF, (h + 1) * HALF, result[:])
 
-        q_terms = fetch_terms(q_slots, "q", ("raw0", "wq4"))
-        combine(Q_ROWS, "q", q_terms, 0, 2)
+        q_terms = fetch_terms(q_slots, "q", ("raw0", "wq"))
         k_slots = keep.tile([P, SLOTS], F32, name="k_slots")
         for e0, e1 in WK_LOADS:
             for e in range(e0, e1):
                 project(
                     k_slots, K_ROWS, e, K_BANKS[e], expert(wk_word_sb[e0], e - e0), wk_scale_sb, FP8X4, C, packed_planes
                 )
-        combine(V_ROWS, "v", fetch_terms(v_slots, "v", ("raw4", "raw6")), 0, 2)
+        combine(Q_ROWS, "q", q_terms, 4, 0)
+        combine(V_ROWS, "v", fetch_terms(v_slots, "v", ("raw4", "raw6")), 6, 2)
 
         k_terms = [keep.tile([P, T], F32, name="k_term%d" % r) for r in range(2)]
         k_pair = keep.tile([P, 2 * T], F32, name="k_pair", tag="raw8", align_bytes=64)
@@ -281,7 +275,7 @@ def tile_moe_qkv_kernel(
             turned = turn_and_add(4 + h, [term[:, t0:t1] for term in k_terms[: TOP - 1]])
             part = keep.tile([P, t1 - t0], F32, name="k_part%d" % h)
             nc.scalar.copy(part[:], turned[:])
-            partial.append(turn_and_add(6 + h, [part[:]]))
+            partial.append(turn_and_add(h, [part[:]]))
         for (t0, t1), total in zip(LAST_PIECES, partial):
             last_term = k_terms[TOP - 1][:, t0:t1]
             fetch_gated(k_slots, TOP - 1, t0, t1, last_term)

@@ -32,13 +32,12 @@ GATE_COLS = TOP * T // P
 HALF = T // 2
 SCALE_CHUNKS = ((0, 6), (6, 12))
 WORD_CHUNKS = ((0, 4), (4, 8), (8, 11), (11, 12))
-PAIRS = tuple((e, e + 2) for e in range(0, E, 2))
-ROUNDED = ((0, 4), (4, 8), (8, 12))
-QUANT = ((0, 4), (4, 8), (8, 10), (10, 12))
-WK_LOADS = ((0, 6), (6, 10), (10, 12))
-K_BANKS = (0, 1, 2, 3, 4, 5, 0, 1, 2, 3, 6, 7)
+QUANT = ((0, 4), (4, 8), (8, 12))
+WQ_LOADS = ((0, 4), (4, 8), (8, 12))
+WK_LOADS = ((0, 12),)
 LAST_PIECES = ((0, 512), (512, T))
 Q_ROWS, K_ROWS, V_ROWS = 0, 1, 2
+COPY = mybir.ActivationFunctionType.Copy
 
 
 def tile_moe_qkv_kernel(
@@ -49,30 +48,28 @@ def tile_moe_qkv_kernel(
         keep = ctx.enter_context(tc.tile_pool(name="keep", bufs=1))
         psum = ctx.enter_context(tc.psum_pool(name="psum", bufs=1))
 
+        def tile(shape, dtype, name, tag=None):
+            return keep.tile(shape, dtype, name=name, tag=tag or name, align_bytes=64)
+
         offs_sb = keep.tile([P, SLOTS // LIST_ROWS], U16, name="offs_sb")
         pos_sb = [keep.tile([P, T // LIST_ROWS], U16, name="pos_sb%d" % r) for r in range(TOP)]
-        x_scale_sb = keep.tile([P, SCALE_WINDOW], U8, name="x_scale_sb", align_bytes=64)
-        x_word_sb = keep.tile([P, T + WORD_WINDOW], I32, name="x_word_sb", align_bytes=64)
-        slot_words = [keep.tile([P, SLOTS], U32, name="slot_words%d" % s, align_bytes=64) for s in range(PASSES)]
-        slot_scales = keep.tile([P, SLOTS], U8, name="slot_scales", align_bytes=64)
-        slot_scales_low = keep.tile([P, SLOTS], U8, name="slot_scales_low", align_bytes=64)
-        wq_word_sb = keep.tile([P, E * PASSES, 2 * N], U8, name="wq_word_sb", tag="wq", align_bytes=64)
-        wk_word_sb = {
-            e0: keep.tile([P, PASSES * (e1 - e0), N], I32, name="wk_word_sb%d" % e0, align_bytes=64)
-            for e0, e1 in WK_LOADS
-        }
-        wv_word_sb = keep.tile([P, E * PASSES, N], U32, name="wv_word_sb", align_bytes=64)
-        wq_scale_sb = keep.tile([P, E * PASSES, N], U8, name="wq_scale_sb", align_bytes=64)
-        wk_scale_sb = keep.tile([P, E * PASSES, N], U8, name="wk_scale_sb", align_bytes=64)
-        wv_scale_sb = keep.tile([P, E * PASSES, N], U8, name="wv_scale_sb", align_bytes=64)
-        raw = {e0: keep.tile([P, 2 * W_ROW], F32, name="raw%d" % e0, tag="raw%d" % e0, align_bytes=64) for e0, e1 in PAIRS}
-        rounded = {
-            e0: keep.tile([P, (e1 - e0) * W_ROW], BF16, name="rounded%d" % e0, align_bytes=64) for e0, e1 in ROUNDED[:2]
-        }
-        gate_cols = keep.tile([P, GATE_COLS], F32, name="gate_cols")
-        gates = keep.tile([P, TOP * T], F32, name="gates")
-        bias_sb = keep.tile([P, 3, E], F32, name="bias_sb")
-        ident = keep.tile([P, P], F32, name="ident")
+        x_scale_sb = tile([P, SCALE_WINDOW], U8, "x_scale_sb")
+        x_word_sb = tile([P, T + WORD_WINDOW], I32, "x_word_sb")
+        slot_words = [tile([P, SLOTS], U32, "slot_words%d" % s) for s in range(PASSES)]
+        slot_scales = tile([P, SLOTS], U8, "slot_scales")
+        slot_scales_low = tile([P, SLOTS], U8, "slot_scales_low")
+        wq_word_sb = {e0: tile([P, PASSES * (e1 - e0), 2 * N], U8, "wq_word_sb%d" % e0) for e0, e1 in WQ_LOADS}
+        wk_word_sb = {e0: tile([P, PASSES * (e1 - e0), N], I32, "wk_word_sb%d" % e0) for e0, e1 in WK_LOADS}
+        wv_word_sb = tile([P, E * PASSES, N], U32, "wv_word_sb")
+        wq_scale_sb = tile([P, E * PASSES, N], U8, "wq_scale_sb")
+        wk_scale_sb = tile([P, E * PASSES, N], U8, "wk_scale_sb")
+        wv_scale_sb = tile([P, E * PASSES, N], U8, "wv_scale_sb")
+        raw = {e0: tile([P, 2 * W_ROW], F32, "raw%d" % e0) for e0 in range(0, E, 2)}
+        rounded = {e0: tile([P, (e1 - e0) * W_ROW], BF16, "rounded%d" % e0) for e0, e1 in QUANT}
+        gate_cols = tile([P, GATE_COLS], F32, "gate_cols")
+        gates = tile([P, TOP * T], F32, "gates")
+        bias_sb = tile([P, 3, E], F32, "bias_sb")
+        ident = tile([P, P], F32, "ident")
 
         nc.gpsimd.memset(x_scale_sb[:, 0:T].bitcast(I32), 0)
         make_identity(nc, ident[:])
@@ -94,24 +91,19 @@ def tile_moe_qkv_kernel(
             for j in range(4):
                 nc.sync.dma_start(out=plane[j:P:32].bitcast(I32), in_=rows[j].bitcast(I32))
 
-        def load_pos(r):
-            nc.sync.dma_start(pos_sb[r][:], (pos1, pos2, pos3, pos4)[r])
-
         nc.sync.dma_start(offs_sb[:], offs)
         for q in range(4):
             nc.sync.dma_start(
                 out=x_scale_sb[32 * q : 32 * q + 8, 0:T].bitcast(I32), in_=x_scales[:, 4 * q : 4 * q + 4].bitcast(I32)
             )
+        nc.sync.dma_start(out=gate_cols[:], in_=gate[:, 0].rearrange("r (c i) -> r c i", i=GATE_COLS))
         load_wv(0)
         nc.sync.dma_start(
             out=x_word_sb[:, 0 : PASSES * T].rearrange("p (s t) -> p s t", s=PASSES),
             in_=x_words.rearrange("s p t d -> p s (t d)").bitcast(I32),
         )
         load_weight_scales(wq_scale_sb, wq_scales)
-        nc.sync.dma_start(out=gate_cols[:], in_=gate[:, 0].rearrange("r (c i) -> r c i", i=GATE_COLS))
         nc.sync.dma_start(out=bias_sb[:], in_=bias.rearrange("(j p) e -> p j e", p=P))
-        for r in range(TOP):
-            load_pos(r)
         load_wv(2)
         load_wv(4)
 
@@ -130,10 +122,19 @@ def tile_moe_qkv_kernel(
                 )
         for j in range(4):
             nc.sync.dma_start(out=slot_scales_low[j:P:32].bitcast(I32), in_=slot_scales[4 + j : P : 32].bitcast(I32))
-        nc.sync.dma_start(out=wq_word_sb[:].bitcast(I32), in_=wq_words.rearrange("e s p b -> p (e s) b").bitcast(I32))
+
+        def load_wq(e0, e1):
+            rows = wq_words.rearrange("e s p b -> p (e s) b").bitcast(I32)
+            nc.sync.dma_start(out=wq_word_sb[e0][:].bitcast(I32), in_=rows[:, PASSES * e0 : PASSES * e1])
+
+        load_wq(*WQ_LOADS[0])
         load_wv(6)
         load_wv(8)
+        load_wq(*WQ_LOADS[1])
         load_wv(10)
+        load_wq(*WQ_LOADS[2])
+        for r in range(TOP):
+            nc.sync.dma_start(pos_sb[r][:], (pos1, pos2, pos3, pos4)[r])
         load_weight_scales(wk_scale_sb, wk_scales)
         for e0, e1 in WK_LOADS:
             rows = wk_words.rearrange("e s p n d -> p (e s) (n d)").bitcast(I32)
@@ -153,13 +154,11 @@ def tile_moe_qkv_kernel(
                 spread[:].rearrange("p (i m) -> p m i", i=per_bank),
             )
 
-        def rounded_part(e0, e1):
-            g0 = max(g for g, g1 in ROUNDED if g <= e0)
-            return rounded[g0][:, (e0 - g0) * W_ROW : (e1 - g0) * W_ROW]
-
         def round_wv(e0):
+            g0 = max(g for g, g1 in QUANT if g <= e0)
+            part = rounded[g0][:, (e0 - g0) * W_ROW : (e0 + 2 - g0) * W_ROW]
             nc.scalar.copy(
-                rounded_part(e0, e0 + 2).rearrange("p (g c i j) -> p g c j i", c=N // 4, i=4, j=PACK),
+                part.rearrange("p (g c i j) -> p g c j i", c=N // 4, i=4, j=PACK),
                 raw[e0][:].rearrange("p (g j c i) -> p g c j i", c=N // 4, i=4, j=PACK),
             )
 
@@ -168,49 +167,52 @@ def tile_moe_qkv_kernel(
             nc.vector.quantize_mx(
                 out=wv_word_sb[:, group].rearrange("p g n -> p (g n)").bitcast(FP8X4),
                 scales=wv_scale_sb[:, group].rearrange("p g n -> p (g n)"),
-                in_=rounded_part(e0, e1),
+                in_=rounded[e0][:],
             )
 
-        def project(results, j, e, b, words, scales, dtype, width, token_scales):
-            acc = bank(b, C)
-            for u0 in range(0, C, width):
-                slots = slice(e * C + u0, e * C + u0 + width)
+        def project(results, j, experts, b, words, scales, dtype, token_scales):
+            acc = bank(b, len(experts) * C)
+            for i, e in enumerate(experts):
+                slots = slice(e * C, (e + 1) * C)
                 for s in range(PASSES):
                     nc.tensor.matmul_mx(
-                        out=acc[:, u0 : u0 + width],
-                        lhsT=words[:, s].bitcast(dtype),
+                        out=acc[:, i * C : (i + 1) * C],
+                        lhsT=words(e)[:, s].bitcast(dtype),
                         lhsT_scale=scales[:, PASSES * e + s],
                         rhs=slot_words[s][:, slots].bitcast(FP8X4),
                         rhs_scale=token_scales[s][:, slots],
                         start=(s == 0),
                         stop=(s == PASSES - 1),
                     )
-            nc.scalar.activation(results[:, e * C : (e + 1) * C], acc[:], IDENTITY, bias=bias_sb[:, j, e : e + 1])
+            for i, e in enumerate(experts):
+                nc.scalar.activation(
+                    results[:, e * C : (e + 1) * C], acc[:, i * C : (i + 1) * C], IDENTITY, bias=bias_sb[:, j, e : e + 1]
+                )
 
-        def expert(words, i):
-            return words[:, PASSES * i : PASSES * (i + 1)]
+        def words_of(pieces):
+            def words(e):
+                e0 = max(g for g in pieces if g <= e)
+                return pieces[e0][:, PASSES * (e - e0) : PASSES * (e - e0 + 1)]
+
+            return words
 
         packed_planes = (slot_scales[:], slot_scales[4:P])
         low_planes = (slot_scales[:], slot_scales_low[:])
 
-        for e0 in (0, 2, 4, 6):
-            round_wv(e0)
-        q_slots = keep.tile([P, SLOTS], F32, name="q_slots")
-        for e in range(E):
-            project(q_slots, Q_ROWS, e, e, expert(wq_word_sb, e), wq_scale_sb, FP4X4, C // 2, low_planes)
-        rounded[8] = keep.tile([P, 4 * W_ROW], BF16, name="rounded8", tag="wq", align_bytes=64)
-        round_wv(8)
-        round_wv(10)
-        for e0, e1 in QUANT:
-            quantize_wv(e0, e1)
-        v_slots = keep.tile([P, SLOTS], F32, name="v_slots", tag="raw10", align_bytes=64)
-        for e in range(E):
-            project(v_slots, V_ROWS, e, E + e, expert(wv_word_sb, e), wv_scale_sb, FP8X4, C, packed_planes)
+        def term_tiles(name, tags):
+            pairs = [tile([P, 2 * T], F32, "%s_terms%d" % (name, h), tags[h]) for h in range(2)]
+            return [pairs[r // 2][:, (r % 2) * T : (r % 2 + 1) * T] for r in range(TOP)]
 
-        def fetch_gated(results, r, t0, t1, term):
+        def fetch_gated(results, r, term, t0=0, t1=T):
             nc.vector.tensor_tensor(
-                term, results[:].indirect(entries(pos_sb[r], t0, t1)), gates[:, r * T + t0 : r * T + t1], MULT
+                term[:, t0:t1], results[:].indirect(entries(pos_sb[r], t0, t1)), gates[:, r * T + t0 : r * T + t1], MULT
             )
+
+        def fetch_plain(results, r, term, t0=0, t1=T):
+            nc.scalar.activation(term[:, t0:t1], results[:].indirect(entries(pos_sb[r], t0, t1)), COPY)
+
+        def gate_term(r, term, t0=0, t1=T):
+            nc.vector.tensor_tensor(term[:, t0:t1], term[:, t0:t1], gates[:, r * T + t0 : r * T + t1], MULT)
 
         def turn_into(turned, source, first, last):
             width = source.shape[1]
@@ -224,60 +226,87 @@ def tile_moe_qkv_kernel(
                     is_transpose=True,
                 )
 
-        def turn_and_add(b, sources):
-            turned = bank(b, sources[0].shape[1])
-            for i, source in enumerate(sources):
-                turn_into(turned, source, i == 0, i == len(sources) - 1)
+        def turn_terms(b, terms):
+            turned = [bank(b + h, HALF) for h in range(2)]
+            for i, term in enumerate(terms):
+                for h in range(2):
+                    turn_into(turned[h], term[:, h * HALF : (h + 1) * HALF], i == 0, i == len(terms) - 1)
             return turned
+
+        def turn_back(name, turned, b, tag=None):
+            totals = []
+            summed = tile([P, T], F32, "%s_summed" % name, tag)
+            for h in range(2):
+                half = summed[:, h * HALF : (h + 1) * HALF]
+                nc.scalar.copy(half, turned[h][:])
+                total = bank(b + h, HALF)
+                turn_into(total, half, True, True)
+                totals.append(total)
+            return totals
 
         def store(j, t0, t1, result):
             nc.sync.dma_start(out=out[j * N : (j + 1) * N, t0:t1], in_=result)
 
-        def fetch_terms(results, name, tags):
-            pairs = [
-                keep.tile([P, 2 * T], F32, name="%s_terms%d" % (name, h), tag=tags[h], align_bytes=64) for h in range(2)
-            ]
-            terms = [pairs[r // 2][:, (r % 2) * T : (r % 2 + 1) * T] for r in range(TOP)]
-            for r in range(TOP):
-                fetch_gated(results, r, 0, T, terms[r])
-            return terms
-
-        def combine(j, name, terms, turn_bank, total_bank):
-            turned = [bank(turn_bank + h, HALF) for h in range(2)]
-            for r, term in enumerate(terms):
-                for h in range(2):
-                    turn_into(turned[h], term[:, h * HALF : (h + 1) * HALF], r == 0, r == TOP - 1)
+        def finish(j, name, totals):
             for h in range(2):
-                summed = keep.tile([P, HALF], F32, name="%s_summed%d" % (name, h))
-                nc.scalar.copy(summed[:], turned[h][:])
-                total = turn_and_add(total_bank + h, [summed[:]])
-                result = keep.tile([P, HALF], F32, name="%s_result%d" % (name, h))
-                nc.scalar.copy(result[:], total[:])
+                result = tile([P, HALF], F32, "%s_result%d" % (name, h))
+                nc.scalar.copy(result[:], totals[h][:])
                 store(j, h * HALF, (h + 1) * HALF, result[:])
 
-        q_terms = fetch_terms(q_slots, "q", ("raw0", "wq"))
-        k_slots = keep.tile([P, SLOTS], F32, name="k_slots")
-        for e0, e1 in WK_LOADS:
+        q_slots = tile([P, SLOTS], F32, "q_slots")
+        for pairs, (e0, e1) in zip(((0, 2, 4), (6, 8), (10,)), WQ_LOADS):
+            for pair in pairs:
+                round_wv(pair)
             for e in range(e0, e1):
-                project(
-                    k_slots, K_ROWS, e, K_BANKS[e], expert(wk_word_sb[e0], e - e0), wk_scale_sb, FP8X4, C, packed_planes
-                )
-        combine(Q_ROWS, "q", q_terms, 4, 0)
-        combine(V_ROWS, "v", fetch_terms(v_slots, "v", ("raw4", "raw6")), 6, 2)
+                project(q_slots, Q_ROWS, [e], e + 4, words_of(wq_word_sb), wq_scale_sb, FP4X4, low_planes)
+        for e0, e1 in QUANT:
+            quantize_wv(e0, e1)
+        q_terms = term_tiles("q", ("raw0", "raw2"))
+        for r in (0, 1):
+            fetch_plain(q_slots, r, q_terms[r])
+        for r in (2, 3):
+            fetch_gated(q_slots, r, q_terms[r])
+        for r in (0, 1):
+            gate_term(r, q_terms[r])
+        v_slots = tile([P, SLOTS], F32, "v_slots")
+        for e in range(0, E, 2):
+            project(v_slots, V_ROWS, [e, e + 1], 4 + e // 2, words_of({0: wv_word_sb}), wv_scale_sb, FP8X4, packed_planes)
+        k_slots = tile([P, SLOTS], F32, "k_slots")
+        for e in range(0, E, 2):
+            project(k_slots, K_ROWS, [e, e + 1], 2 + e // 2, words_of(wk_word_sb), wk_scale_sb, FP8X4, packed_planes)
+        v_terms = term_tiles("v", ("wk_word_sb0", "raw6"))
+        fetch_plain(v_slots, 0, v_terms[0])
+        fetch_plain(v_slots, 1, v_terms[1], 0, HALF)
+        for r in (2, 3):
+            fetch_gated(v_slots, r, v_terms[r])
+        fetch_gated(v_slots, 1, v_terms[1], HALF, T)
+        q_turned = turn_terms(2, [q_terms[r] for r in (2, 3, 0, 1)])
+        q_totals = turn_back("q", q_turned, 0)
+        k_gated = tile([P, 2 * T], F32, "k_gated", "raw10")
+        k_terms = [
+            tile([P, T], F32, "k_plain0", "raw0")[:],
+            tile([P, T], F32, "k_plain1", "q_summed")[:],
+            k_gated[:, 0:T],
+            k_gated[:, T:],
+        ]
+        fetch_plain(k_slots, 0, k_terms[0])
+        finish(Q_ROWS, "q", q_totals)
+        fetch_plain(k_slots, 1, k_terms[1])
+        gate_term(0, v_terms[0])
+        fetch_gated(k_slots, 2, k_terms[2])
+        gate_term(1, v_terms[1], 0, HALF)
+        fetch_gated(k_slots, 3, k_terms[3])
+        v_turned = turn_terms(4, [v_terms[r] for r in (2, 3, 0, 1)])
+        finish(V_ROWS, "v", turn_back("v", v_turned, 6))
 
-        k_terms = [keep.tile([P, T], F32, name="k_term%d" % r) for r in range(2)]
-        k_pair = keep.tile([P, 2 * T], F32, name="k_pair", tag="raw8", align_bytes=64)
-        k_terms = [k_terms[0][:], k_terms[1][:], k_pair[:, 0:T], k_pair[:, T:]]
-        partial = []
-        for h, (t0, t1) in enumerate(LAST_PIECES):
-            for r in range(TOP - 1):
-                fetch_gated(k_slots, r, t0, t1, k_terms[r][:, t0:t1])
-            turned = turn_and_add(4 + h, [term[:, t0:t1] for term in k_terms[: TOP - 1]])
-            part = keep.tile([P, t1 - t0], F32, name="k_part%d" % h)
-            nc.scalar.copy(part[:], turned[:])
-            partial.append(turn_and_add(h, [part[:]]))
-        for (t0, t1), total in zip(LAST_PIECES, partial):
-            last_term = k_terms[TOP - 1][:, t0:t1]
-            fetch_gated(k_slots, TOP - 1, t0, t1, last_term)
-            nc.vector.tensor_tensor(last_term, total[:], last_term, ADD)
-            store(K_ROWS, t0, t1, last_term)
+        def add_into(total, term):
+            nc.vector.tensor_tensor(total, total, term, ADD)
+
+        gate_term(0, k_terms[0])
+        add_into(k_terms[2], k_terms[3])
+        gate_term(1, k_terms[1], *LAST_PIECES[0])
+        add_into(k_terms[2], k_terms[0])
+        gate_term(1, k_terms[1], *LAST_PIECES[1])
+        for t0, t1 in LAST_PIECES:
+            add_into(k_terms[1][:, t0:t1], k_terms[2][:, t0:t1])
+            store(K_ROWS, t0, t1, k_terms[1][:, t0:t1])

@@ -32,9 +32,11 @@ GATE_COLS = TOP * T // P
 HALF = T // 2
 SCALE_CHUNKS = ((0, 6), (6, 12))
 WORD_CHUNKS = ((0, 4), (4, 8), (8, 11), (11, 12))
-QUANT = ((0, 4), (4, 8), (8, 12))
+QUANT = ((0, 4), (4, 8), (8, 10), (10, 12))
 WQ_LOADS = ((0, 4), (4, 8), (8, 12))
-WK_LOADS = ((0, 12),)
+EARLY = 8
+WV_LOADS = ((0, 2), (2, 4), (4, 6), (6, 8), (8, 10), (10, 11), (11, 12))
+WK_LOADS = ((0, 6), (6, 10), (10, 12))
 LAST_PIECES = ((0, 512), (512, T))
 Q_ROWS, K_ROWS, V_ROWS = 0, 1, 2
 COPY = mybir.ActivationFunctionType.Copy
@@ -55,16 +57,16 @@ def tile_moe_qkv_kernel(
         pos_sb = [keep.tile([P, T // LIST_ROWS], U16, name="pos_sb%d" % r) for r in range(TOP)]
         x_scale_sb = tile([P, SCALE_WINDOW], U8, "x_scale_sb")
         x_word_sb = tile([P, T + WORD_WINDOW], I32, "x_word_sb")
-        slot_words = [tile([P, SLOTS], U32, "slot_words%d" % s) for s in range(PASSES)]
+        slot_words = {}
         slot_scales = tile([P, SLOTS], U8, "slot_scales")
         slot_scales_low = tile([P, SLOTS], U8, "slot_scales_low")
         wq_word_sb = {e0: tile([P, PASSES * (e1 - e0), 2 * N], U8, "wq_word_sb%d" % e0) for e0, e1 in WQ_LOADS}
         wk_word_sb = {e0: tile([P, PASSES * (e1 - e0), N], I32, "wk_word_sb%d" % e0) for e0, e1 in WK_LOADS}
-        wv_word_sb = tile([P, E * PASSES, N], U32, "wv_word_sb")
+        wv_word_sb = {e0: tile([P, PASSES * (e1 - e0), N], U32, "wv_word_sb%d" % e0) for e0, e1 in QUANT}
         wq_scale_sb = tile([P, E * PASSES, N], U8, "wq_scale_sb")
         wk_scale_sb = tile([P, E * PASSES, N], U8, "wk_scale_sb")
-        wv_scale_sb = tile([P, E * PASSES, N], U8, "wv_scale_sb")
-        raw = {e0: tile([P, 2 * W_ROW], F32, "raw%d" % e0) for e0 in range(0, E, 2)}
+        wv_scale_sb = {e0: tile([P, PASSES * (e1 - e0), N], U8, "wv_scale_sb%d" % e0) for e0, e1 in QUANT}
+        raw = {e0: tile([P, (e1 - e0) * W_ROW], F32, "raw%d" % e0) for e0, e1 in WV_LOADS}
         rounded = {e0: tile([P, (e1 - e0) * W_ROW], BF16, "rounded%d" % e0) for e0, e1 in QUANT}
         gate_cols = tile([P, GATE_COLS], F32, "gate_cols")
         gates = tile([P, TOP * T], F32, "gates")
@@ -77,13 +79,13 @@ def tile_moe_qkv_kernel(
         nc.vector.memset(wq_scale_sb[:].rearrange("p g n -> p (g n)").bitcast(I32), 0)
         nc.vector.memset(x_word_sb[:, PASSES * T :], 0)
         nc.vector.memset(slot_scales_low[:].bitcast(I32), 0)
-        nc.vector.memset(wk_scale_sb[:].rearrange("p g n -> p (g n)").bitcast(I32), 0)
+        nc.gpsimd.memset(wk_scale_sb[:].rearrange("p g n -> p (g n)").bitcast(I32), 0)
 
-        def load_wv(e0):
+        def load_wv(e0, e1):
             rows = wv.rearrange("e (s p j) n -> p (e s) (j n)", s=PASSES, j=PACK)
             nc.sync.dma_start(
                 out=raw[e0][:].rearrange("p (g c) -> p g c", c=PACK * N),
-                in_=rows[:, PASSES * e0 : PASSES * (e0 + 2)],
+                in_=rows[:, PASSES * e0 : PASSES * e1],
             )
 
         def load_weight_scales(plane, scales):
@@ -97,15 +99,15 @@ def tile_moe_qkv_kernel(
                 out=x_scale_sb[32 * q : 32 * q + 8, 0:T].bitcast(I32), in_=x_scales[:, 4 * q : 4 * q + 4].bitcast(I32)
             )
         nc.sync.dma_start(out=gate_cols[:], in_=gate[:, 0].rearrange("r (c i) -> r c i", i=GATE_COLS))
-        load_wv(0)
+        load_wv(*WV_LOADS[0])
         nc.sync.dma_start(
             out=x_word_sb[:, 0 : PASSES * T].rearrange("p (s t) -> p s t", s=PASSES),
             in_=x_words.rearrange("s p t d -> p s (t d)").bitcast(I32),
         )
+        for e0, e1 in WV_LOADS[1:-1]:
+            load_wv(e0, e1)
         load_weight_scales(wq_scale_sb, wq_scales)
         nc.sync.dma_start(out=bias_sb[:], in_=bias.rearrange("(j p) e -> p j e", p=P))
-        load_wv(2)
-        load_wv(4)
 
         def entries(list_tile, first, last):
             return list_tile[:, first // LIST_ROWS : last // LIST_ROWS]
@@ -114,12 +116,23 @@ def tile_moe_qkv_kernel(
             nc.vector.tensor_copy(
                 slot_scales[:, e0 * C : e1 * C], x_scale_sb[:].indirect(entries(offs_sb, e0 * C, e1 * C))
             )
-        for e0, e1 in WORD_CHUNKS:
-            for s in range(PASSES):
-                window = x_word_sb[:, s * T : s * T + WORD_WINDOW].bitcast(U32)
-                nc.vector.tensor_copy(
-                    slot_words[s][:, e0 * C : e1 * C], window.indirect(entries(offs_sb, e0 * C, e1 * C))
-                )
+
+        def words_at(e0, e1, s):
+            first = max(g for g in slot_words if g <= e0)
+            width = slot_words[first].shape[1] // PASSES
+            return slot_words[first][:, s * width + (e0 - first) * C : s * width + (e1 - first) * C]
+
+        def gather_words(e0, e1, s):
+            window = x_word_sb[:, s * T : s * T + WORD_WINDOW].bitcast(U32)
+            nc.vector.tensor_copy(words_at(e0, e1, s), window.indirect(entries(offs_sb, e0 * C, e1 * C)))
+
+        def gather_group(first, chunks, tag=None):
+            slot_words[first] = tile([P, PASSES * 4 * C], U32, "slot_words%d" % first, tag)
+            for e0, e1 in chunks:
+                for s in range(PASSES):
+                    gather_words(e0, e1, s)
+
+        gather_group(0, WORD_CHUNKS[:1])
         for j in range(4):
             nc.sync.dma_start(out=slot_scales_low[j:P:32].bitcast(I32), in_=slot_scales[4 + j : P : 32].bitcast(I32))
 
@@ -127,14 +140,11 @@ def tile_moe_qkv_kernel(
             rows = wq_words.rearrange("e s p b -> p (e s) b").bitcast(I32)
             nc.sync.dma_start(out=wq_word_sb[e0][:].bitcast(I32), in_=rows[:, PASSES * e0 : PASSES * e1])
 
-        load_wq(*WQ_LOADS[0])
-        load_wv(6)
-        load_wv(8)
-        load_wq(*WQ_LOADS[1])
-        load_wv(10)
-        load_wq(*WQ_LOADS[2])
+        for e0, e1 in WQ_LOADS:
+            load_wq(e0, e1)
         for r in range(TOP):
             nc.sync.dma_start(pos_sb[r][:], (pos1, pos2, pos3, pos4)[r])
+        load_wv(*WV_LOADS[-1])
         load_weight_scales(wk_scale_sb, wk_scales)
         for e0, e1 in WK_LOADS:
             rows = wk_words.rearrange("e s p n d -> p (e s) (n d)").bitcast(I32)
@@ -154,19 +164,18 @@ def tile_moe_qkv_kernel(
                 spread[:].rearrange("p (i m) -> p m i", i=per_bank),
             )
 
-        def round_wv(e0):
+        def round_wv(e0, e1, copy):
             g0 = max(g for g, g1 in QUANT if g <= e0)
-            part = rounded[g0][:, (e0 - g0) * W_ROW : (e0 + 2 - g0) * W_ROW]
-            nc.scalar.copy(
+            part = rounded[g0][:, (e0 - g0) * W_ROW : (e1 - g0) * W_ROW]
+            copy(
                 part.rearrange("p (g c i j) -> p g c j i", c=N // 4, i=4, j=PACK),
                 raw[e0][:].rearrange("p (g j c i) -> p g c j i", c=N // 4, i=4, j=PACK),
             )
 
-        def quantize_wv(e0, e1):
-            group = slice(PASSES * e0, PASSES * e1)
+        def quantize_wv(e0):
             nc.vector.quantize_mx(
-                out=wv_word_sb[:, group].rearrange("p g n -> p (g n)").bitcast(FP8X4),
-                scales=wv_scale_sb[:, group].rearrange("p g n -> p (g n)"),
+                out=wv_word_sb[e0][:].rearrange("p g n -> p (g n)").bitcast(FP8X4),
+                scales=wv_scale_sb[e0][:].rearrange("p g n -> p (g n)"),
                 in_=rounded[e0][:],
             )
 
@@ -178,8 +187,8 @@ def tile_moe_qkv_kernel(
                     nc.tensor.matmul_mx(
                         out=acc[:, i * C : (i + 1) * C],
                         lhsT=words(e)[:, s].bitcast(dtype),
-                        lhsT_scale=scales[:, PASSES * e + s],
-                        rhs=slot_words[s][:, slots].bitcast(FP8X4),
+                        lhsT_scale=scales(e)[:, s],
+                        rhs=words_at(e, e + 1, s).bitcast(FP8X4),
                         rhs_scale=token_scales[s][:, slots],
                         start=(s == 0),
                         stop=(s == PASSES - 1),
@@ -196,6 +205,9 @@ def tile_moe_qkv_kernel(
 
             return words
 
+        def scales_of(plane):
+            return words_of({0: plane})
+
         packed_planes = (slot_scales[:], slot_scales[4:P])
         low_planes = (slot_scales[:], slot_scales_low[:])
 
@@ -211,8 +223,9 @@ def tile_moe_qkv_kernel(
         def fetch_plain(results, r, term, t0=0, t1=T):
             nc.scalar.activation(term[:, t0:t1], results[:].indirect(entries(pos_sb[r], t0, t1)), COPY)
 
-        def gate_term(r, term, t0=0, t1=T):
-            nc.vector.tensor_tensor(term[:, t0:t1], term[:, t0:t1], gates[:, r * T + t0 : r * T + t1], MULT)
+        def gate_term(r, term, t0=0, t1=T, plain=None):
+            source = term if plain is None else plain
+            nc.vector.tensor_tensor(term[:, t0:t1], source[:, t0:t1], gates[:, r * T + t0 : r * T + t1], MULT)
 
         def turn_into(turned, source, first, last):
             width = source.shape[1]
@@ -226,12 +239,11 @@ def tile_moe_qkv_kernel(
                     is_transpose=True,
                 )
 
-        def turn_terms(b, terms):
-            turned = [bank(b + h, HALF) for h in range(2)]
+        def turn_terms(turned, terms, opens, closes):
             for i, term in enumerate(terms):
                 for h in range(2):
-                    turn_into(turned[h], term[:, h * HALF : (h + 1) * HALF], i == 0, i == len(terms) - 1)
-            return turned
+                    half = term[:, h * HALF : (h + 1) * HALF]
+                    turn_into(turned[h], half, opens and i == 0, closes and i == len(terms) - 1)
 
         def turn_back(name, turned, b, tag=None):
             totals = []
@@ -253,60 +265,76 @@ def tile_moe_qkv_kernel(
                 nc.scalar.copy(result[:], totals[h][:])
                 store(j, h * HALF, (h + 1) * HALF, result[:])
 
-        q_slots = tile([P, SLOTS], F32, "q_slots")
-        for pairs, (e0, e1) in zip(((0, 2, 4), (6, 8), (10,)), WQ_LOADS):
-            for pair in pairs:
-                round_wv(pair)
+        def project_q(e0, e1, b):
             for e in range(e0, e1):
-                project(q_slots, Q_ROWS, [e], e + 4, words_of(wq_word_sb), wq_scale_sb, FP4X4, low_planes)
-        for e0, e1 in QUANT:
-            quantize_wv(e0, e1)
-        q_terms = term_tiles("q", ("raw0", "raw2"))
-        for r in (0, 1):
-            fetch_plain(q_slots, r, q_terms[r])
+                project(q_slots, Q_ROWS, [e], b + e - e0, words_of(wq_word_sb), scales_of(wq_scale_sb), FP4X4, low_planes)
+
+        def project_v(e0, e1, b):
+            for e in range(e0, e1, 2):
+                words, scales = words_of(wv_word_sb), words_of(wv_scale_sb)
+                project(v_slots, V_ROWS, [e, e + 1], b + (e - e0) // 2, words, scales, FP8X4, packed_planes)
+
+        q_slots = tile([P, SLOTS], F32, "q_slots")
+        for e0, e1 in WV_LOADS[:-1]:
+            round_wv(e0, e1, nc.scalar.copy)
+        quantize_wv(0)
+        gather_group(4, WORD_CHUNKS[1:2], "rounded0")
+        quantize_wv(4)
+        gather_group(8, WORD_CHUNKS[2:], "rounded4")
+        v_slots = tile([P, SLOTS], F32, "v_slots", "raw10")
+        project_v(0, EARLY, 0)
+        project_q(*WQ_LOADS[0], 4)
+        project_q(*WQ_LOADS[1], 0)
+        project_q(*WQ_LOADS[2], 4)
+        quantize_wv(QUANT[2][0])
+        round_wv(*WV_LOADS[-1], nc.vector.tensor_copy)
+        quantize_wv(QUANT[3][0])
+        q_plain = [tile([P, T], F32, "q_plain0", "raw2")[:], None]
+        q_gated = tile([P, 2 * T], F32, "q_gated", "rounded10")
+        q_terms = [None, None, q_gated[:, 0:T], q_gated[:, T:]]
+        fetch_plain(q_slots, 0, q_plain[0])
         for r in (2, 3):
             fetch_gated(q_slots, r, q_terms[r])
-        for r in (0, 1):
-            gate_term(r, q_terms[r])
-        v_slots = tile([P, SLOTS], F32, "v_slots")
-        for e in range(0, E, 2):
-            project(v_slots, V_ROWS, [e, e + 1], 4 + e // 2, words_of({0: wv_word_sb}), wv_scale_sb, FP8X4, packed_planes)
+        project_v(EARLY, E, 4)
+        q_plain[1] = tile([P, T], F32, "q_plain1", "wv_word_sb%d" % QUANT[-1][0])[:]
+        fetch_plain(q_slots, 1, q_plain[1])
+        v_terms = term_tiles("v", ("raw4", "raw6"))
+        fetch_plain(v_slots, 0, v_terms[0])
+        for r in (1, 2, 3):
+            fetch_gated(v_slots, r, v_terms[r])
+        gate_term(0, v_terms[0])
+        q_turned = [bank(6 + h, HALF) for h in range(2)]
+        turn_terms(q_turned, q_terms[2:], True, False)
         k_slots = tile([P, SLOTS], F32, "k_slots")
         for e in range(0, E, 2):
-            project(k_slots, K_ROWS, [e, e + 1], 2 + e // 2, words_of(wk_word_sb), wk_scale_sb, FP8X4, packed_planes)
-        v_terms = term_tiles("v", ("wk_word_sb0", "raw6"))
-        fetch_plain(v_slots, 0, v_terms[0])
-        fetch_plain(v_slots, 1, v_terms[1], 0, HALF)
-        for r in (2, 3):
-            fetch_gated(v_slots, r, v_terms[r])
-        fetch_gated(v_slots, 1, v_terms[1], HALF, T)
-        q_turned = turn_terms(2, [q_terms[r] for r in (2, 3, 0, 1)])
-        q_totals = turn_back("q", q_turned, 0)
-        k_gated = tile([P, 2 * T], F32, "k_gated", "raw10")
-        k_terms = [
-            tile([P, T], F32, "k_plain0", "raw0")[:],
-            tile([P, T], F32, "k_plain1", "q_summed")[:],
-            k_gated[:, 0:T],
-            k_gated[:, T:],
-        ]
+            project(k_slots, K_ROWS, [e, e + 1], e // 2, words_of(wk_word_sb), scales_of(wk_scale_sb), FP8X4, packed_planes)
+        q_late = tile([P, 2 * T], F32, "q_late", "wk_word_sb%d" % WK_LOADS[-1][0])
+        q_terms[:2] = [q_late[:, 0:T], q_late[:, T:]]
+        for r in (0, 1):
+            gate_term(r, q_terms[r], plain=q_plain[r])
+        turn_terms(q_turned, q_terms[:2], False, True)
+        k_terms = term_tiles("k", ("raw0", "raw8"))
         fetch_plain(k_slots, 0, k_terms[0])
-        finish(Q_ROWS, "q", q_totals)
+        fetch_plain(k_slots, 2, k_terms[2], 0, HALF)
         fetch_plain(k_slots, 1, k_terms[1])
-        gate_term(0, v_terms[0])
-        fetch_gated(k_slots, 2, k_terms[2])
-        gate_term(1, v_terms[1], 0, HALF)
         fetch_gated(k_slots, 3, k_terms[3])
-        v_turned = turn_terms(4, [v_terms[r] for r in (2, 3, 0, 1)])
-        finish(V_ROWS, "v", turn_back("v", v_turned, 6))
+        fetch_gated(k_slots, 2, k_terms[2], HALF, T)
+        v_turned = [bank(4 + h, HALF) for h in range(2)]
+        turn_terms(v_turned, [v_terms[r] for r in (1, 2, 3, 0)], True, True)
+        q_totals = turn_back("q", q_turned, 6)
+        v_totals = turn_back("v", v_turned, 0)
+        finish(Q_ROWS, "q", q_totals)
+        finish(V_ROWS, "v", v_totals)
 
         def add_into(total, term):
             nc.vector.tensor_tensor(total, total, term, ADD)
 
         gate_term(0, k_terms[0])
-        add_into(k_terms[2], k_terms[3])
+        gate_term(2, k_terms[2], 0, HALF)
+        add_into(k_terms[0], k_terms[3])
         gate_term(1, k_terms[1], *LAST_PIECES[0])
-        add_into(k_terms[2], k_terms[0])
+        add_into(k_terms[0], k_terms[2])
         gate_term(1, k_terms[1], *LAST_PIECES[1])
         for t0, t1 in LAST_PIECES:
-            add_into(k_terms[1][:, t0:t1], k_terms[2][:, t0:t1])
+            add_into(k_terms[1][:, t0:t1], k_terms[0][:, t0:t1])
             store(K_ROWS, t0, t1, k_terms[1][:, t0:t1])

@@ -17,6 +17,7 @@ FP4X4 = mybir.dt.float4_e2m1fn_x4
 MULT = mybir.AluOpType.mult
 ADD = mybir.AluOpType.add
 IDENTITY = mybir.ActivationFunctionType.Identity
+COPY = mybir.ActivationFunctionType.Copy
 
 P = 128
 PACK = 4
@@ -30,16 +31,13 @@ BANK = 512
 W_ROW = PASSES * PACK * N
 GATE_COLS = TOP * T // P
 HALF = T // 2
+HALVES = ((0, HALF), (HALF, T))
+LAST_PIECES = ((0, BANK), (BANK, T))
 SCALE_CHUNKS = ((0, 6), (6, 12))
-WORD_CHUNKS = ((0, 4), (4, 8), (8, 11), (11, 12))
+GROUPS = ((0, 4), (4, 8), (8, 12))
 QUANT = ((0, 4), (4, 8), (8, 10), (10, 12))
-WQ_LOADS = ((0, 4), (4, 8), (8, 12))
-EARLY = 8
-WV_LOADS = ((0, 2), (2, 4), (4, 6), (6, 8), (8, 10), (10, 11), (11, 12))
-WK_LOADS = ((0, 6), (6, 10), (10, 12))
-LAST_PIECES = ((0, 512), (512, T))
+PAIRS = tuple((e, e + 2) for e in range(0, E, 2))
 Q_ROWS, K_ROWS, V_ROWS = 0, 1, 2
-COPY = mybir.ActivationFunctionType.Copy
 
 
 def tile_moe_qkv_kernel(
@@ -60,13 +58,13 @@ def tile_moe_qkv_kernel(
         slot_words = {}
         slot_scales = tile([P, SLOTS], U8, "slot_scales")
         slot_scales_low = tile([P, SLOTS], U8, "slot_scales_low")
-        wq_word_sb = {e0: tile([P, PASSES * (e1 - e0), 2 * N], U8, "wq_word_sb%d" % e0) for e0, e1 in WQ_LOADS}
-        wk_word_sb = {e0: tile([P, PASSES * (e1 - e0), N], I32, "wk_word_sb%d" % e0) for e0, e1 in WK_LOADS}
+        wq_word_sb = {e0: tile([P, PASSES * (e1 - e0), 2 * N], U8, "wq_word_sb%d" % e0) for e0, e1 in GROUPS}
+        wk_word_sb = {e0: tile([P, PASSES * (e1 - e0), N], I32, "wk_word_sb%d" % e0) for e0, e1 in GROUPS}
         wv_word_sb = {e0: tile([P, PASSES * (e1 - e0), N], U32, "wv_word_sb%d" % e0) for e0, e1 in QUANT}
         wq_scale_sb = tile([P, E * PASSES, N], U8, "wq_scale_sb")
         wk_scale_sb = tile([P, E * PASSES, N], U8, "wk_scale_sb")
         wv_scale_sb = {e0: tile([P, PASSES * (e1 - e0), N], U8, "wv_scale_sb%d" % e0) for e0, e1 in QUANT}
-        raw = {e0: tile([P, (e1 - e0) * W_ROW], F32, "raw%d" % e0) for e0, e1 in WV_LOADS}
+        raw = {e0: tile([P, (e1 - e0) * W_ROW], F32, "raw%d" % e0) for e0, e1 in PAIRS}
         rounded = {e0: tile([P, (e1 - e0) * W_ROW], BF16, "rounded%d" % e0) for e0, e1 in QUANT}
         gate_cols = tile([P, GATE_COLS], F32, "gate_cols")
         gates = tile([P, TOP * T], F32, "gates")
@@ -76,9 +74,9 @@ def tile_moe_qkv_kernel(
         nc.gpsimd.memset(x_scale_sb[:, 0:T].bitcast(I32), 0)
         make_identity(nc, ident[:])
         nc.vector.memset(x_scale_sb[:, T:].bitcast(I32), 0)
-        nc.vector.memset(wq_scale_sb[:].rearrange("p g n -> p (g n)").bitcast(I32), 0)
         nc.vector.memset(x_word_sb[:, PASSES * T :], 0)
         nc.vector.memset(slot_scales_low[:].bitcast(I32), 0)
+        nc.gpsimd.memset(wq_scale_sb[:].rearrange("p g n -> p (g n)").bitcast(I32), 0)
         nc.gpsimd.memset(wk_scale_sb[:].rearrange("p g n -> p (g n)").bitcast(I32), 0)
 
         def load_wv(e0, e1):
@@ -93,21 +91,32 @@ def tile_moe_qkv_kernel(
             for j in range(4):
                 nc.sync.dma_start(out=plane[j:P:32].bitcast(I32), in_=rows[j].bitcast(I32))
 
+        def load_wq(e0, e1):
+            rows = wq_words.rearrange("e s p b -> p (e s) b").bitcast(I32)
+            nc.sync.dma_start(out=wq_word_sb[e0][:].bitcast(I32), in_=rows[:, PASSES * e0 : PASSES * e1])
+
+        def load_wk(e0, e1):
+            rows = wk_words.rearrange("e s p n d -> p (e s) (n d)").bitcast(I32)
+            nc.sync.dma_start(out=wk_word_sb[e0][:], in_=rows[:, PASSES * e0 : PASSES * e1])
+
+        def load_pos(r):
+            nc.sync.dma_start(pos_sb[r][:], (pos1, pos2, pos3, pos4)[r])
+
         nc.sync.dma_start(offs_sb[:], offs)
         for q in range(4):
             nc.sync.dma_start(
                 out=x_scale_sb[32 * q : 32 * q + 8, 0:T].bitcast(I32), in_=x_scales[:, 4 * q : 4 * q + 4].bitcast(I32)
             )
-        nc.sync.dma_start(out=gate_cols[:], in_=gate[:, 0].rearrange("r (c i) -> r c i", i=GATE_COLS))
-        load_wv(*WV_LOADS[0])
+        nc.sync.dma_start(out=gate_cols[:], in_=gate[:, 0].rearrange("r (c i) -> c r i", i=GATE_COLS))
+        load_wv(*PAIRS[0])
         nc.sync.dma_start(
             out=x_word_sb[:, 0 : PASSES * T].rearrange("p (s t) -> p s t", s=PASSES),
             in_=x_words.rearrange("s p t d -> p s (t d)").bitcast(I32),
         )
-        for e0, e1 in WV_LOADS[1:-1]:
+        nc.sync.dma_start(out=bias_sb[:], in_=bias.rearrange("(j p) e -> p j e", p=P))
+        for e0, e1 in PAIRS[1:]:
             load_wv(e0, e1)
         load_weight_scales(wq_scale_sb, wq_scales)
-        nc.sync.dma_start(out=bias_sb[:], in_=bias.rearrange("(j p) e -> p j e", p=P))
 
         def entries(list_tile, first, last):
             return list_tile[:, first // LIST_ROWS : last // LIST_ROWS]
@@ -117,38 +126,32 @@ def tile_moe_qkv_kernel(
                 slot_scales[:, e0 * C : e1 * C], x_scale_sb[:].indirect(entries(offs_sb, e0 * C, e1 * C))
             )
 
-        def words_at(e0, e1, s):
-            first = max(g for g in slot_words if g <= e0)
+        def words_at(e, s):
+            first = max(g for g in slot_words if g <= e)
             width = slot_words[first].shape[1] // PASSES
-            return slot_words[first][:, s * width + (e0 - first) * C : s * width + (e1 - first) * C]
+            return slot_words[first][:, s * width + (e - first) * C : s * width + (e - first + 1) * C]
 
-        def gather_words(e0, e1, s):
-            window = x_word_sb[:, s * T : s * T + WORD_WINDOW].bitcast(U32)
-            nc.vector.tensor_copy(words_at(e0, e1, s), window.indirect(entries(offs_sb, e0 * C, e1 * C)))
+        def gather_words(e0, e1, tag=None):
+            width = (e1 - e0) * C
+            slot_words[e0] = tile([P, PASSES * width], U32, "slot_words%d" % e0, tag)
+            for s in range(PASSES):
+                window = x_word_sb[:, s * T : s * T + WORD_WINDOW].bitcast(U32)
+                nc.vector.tensor_copy(
+                    slot_words[e0][:, s * width : (s + 1) * width], window.indirect(entries(offs_sb, e0 * C, e1 * C))
+                )
 
-        def gather_group(first, chunks, tag=None):
-            slot_words[first] = tile([P, PASSES * 4 * C], U32, "slot_words%d" % first, tag)
-            for e0, e1 in chunks:
-                for s in range(PASSES):
-                    gather_words(e0, e1, s)
-
-        gather_group(0, WORD_CHUNKS[:1])
+        gather_words(0, 4)
         for j in range(4):
             nc.sync.dma_start(out=slot_scales_low[j:P:32].bitcast(I32), in_=slot_scales[4 + j : P : 32].bitcast(I32))
-
-        def load_wq(e0, e1):
-            rows = wq_words.rearrange("e s p b -> p (e s) b").bitcast(I32)
-            nc.sync.dma_start(out=wq_word_sb[e0][:].bitcast(I32), in_=rows[:, PASSES * e0 : PASSES * e1])
-
-        for e0, e1 in WQ_LOADS:
-            load_wq(e0, e1)
-        for r in range(TOP):
-            nc.sync.dma_start(pos_sb[r][:], (pos1, pos2, pos3, pos4)[r])
-        load_wv(*WV_LOADS[-1])
+        load_pos(0)
+        load_wq(*GROUPS[0])
+        load_wq(*GROUPS[1])
+        load_wq(*GROUPS[2])
+        for r in range(1, TOP):
+            load_pos(r)
         load_weight_scales(wk_scale_sb, wk_scales)
-        for e0, e1 in WK_LOADS:
-            rows = wk_words.rearrange("e s p n d -> p (e s) (n d)").bitcast(I32)
-            nc.sync.dma_start(out=wk_word_sb[e0][:], in_=rows[:, PASSES * e0 : PASSES * e1])
+        for e0, e1 in GROUPS:
+            load_wk(e0, e1)
 
         def bank(b, width):
             return psum.tile([P, width], F32, name="bank%d" % (b % BANKS))
@@ -160,14 +163,14 @@ def tile_moe_qkv_kernel(
                 column = gate_cols[:, i0 + i : i0 + i + 1].to_broadcast([P, P])
                 nc.tensor.transpose(spread[:, i * P : (i + 1) * P], column, ident[:])
             nc.scalar.copy(
-                gates[:].rearrange("p (m i) -> p m i", i=GATE_COLS)[:, :, i0 : i0 + per_bank],
-                spread[:].rearrange("p (i m) -> p m i", i=per_bank),
+                gates[:].rearrange("p (r c i) -> p r c i", r=TOP, i=GATE_COLS)[:, :, :, i0 : i0 + per_bank],
+                spread[:].rearrange("p (i c r) -> p r c i", i=per_bank, r=TOP),
             )
 
-        def round_wv(e0, e1, copy):
+        def round_wv(e0, e1):
             g0 = max(g for g, g1 in QUANT if g <= e0)
             part = rounded[g0][:, (e0 - g0) * W_ROW : (e1 - g0) * W_ROW]
-            copy(
+            nc.scalar.copy(
                 part.rearrange("p (g c i j) -> p g c j i", c=N // 4, i=4, j=PACK),
                 raw[e0][:].rearrange("p (g j c i) -> p g c j i", c=N // 4, i=4, j=PACK),
             )
@@ -179,7 +182,13 @@ def tile_moe_qkv_kernel(
                 in_=rounded[e0][:],
             )
 
-        def project(results, j, experts, b, words, scales, dtype, token_scales):
+        def empty_on_scalar(result, acc, column):
+            nc.scalar.activation(result, acc, IDENTITY, bias=column)
+
+        def empty_on_vector(result, acc, column):
+            nc.vector.tensor_scalar(result, acc, column, None, ADD)
+
+        def project(results, j, experts, b, words, scales, dtype, token_scales, empty=empty_on_scalar):
             acc = bank(b, len(experts) * C)
             for i, e in enumerate(experts):
                 slots = slice(e * C, (e + 1) * C)
@@ -188,15 +197,13 @@ def tile_moe_qkv_kernel(
                         out=acc[:, i * C : (i + 1) * C],
                         lhsT=words(e)[:, s].bitcast(dtype),
                         lhsT_scale=scales(e)[:, s],
-                        rhs=words_at(e, e + 1, s).bitcast(FP8X4),
+                        rhs=words_at(e, s).bitcast(FP8X4),
                         rhs_scale=token_scales[s][:, slots],
                         start=(s == 0),
                         stop=(s == PASSES - 1),
                     )
             for i, e in enumerate(experts):
-                nc.scalar.activation(
-                    results[:, e * C : (e + 1) * C], acc[:, i * C : (i + 1) * C], IDENTITY, bias=bias_sb[:, j, e : e + 1]
-                )
+                empty(results[:, e * C : (e + 1) * C], acc[:, i * C : (i + 1) * C], bias_sb[:, j, e : e + 1])
 
         def words_of(pieces):
             def words(e):
@@ -211,9 +218,19 @@ def tile_moe_qkv_kernel(
         packed_planes = (slot_scales[:], slot_scales[4:P])
         low_planes = (slot_scales[:], slot_scales_low[:])
 
-        def term_tiles(name, tags):
-            pairs = [tile([P, 2 * T], F32, "%s_terms%d" % (name, h), tags[h]) for h in range(2)]
-            return [pairs[r // 2][:, (r % 2) * T : (r % 2 + 1) * T] for r in range(TOP)]
+        def project_q(experts, b):
+            project(q_slots, Q_ROWS, experts, b, words_of(wq_word_sb), scales_of(wq_scale_sb), FP4X4, low_planes)
+
+        def project_k(experts, b):
+            project(k_slots, K_ROWS, experts, b, words_of(wk_word_sb), scales_of(wk_scale_sb), FP8X4, packed_planes)
+
+        def project_v(experts, b, empty):
+            words, scales = words_of(wv_word_sb), words_of(wv_scale_sb)
+            project(v_slots, V_ROWS, experts, b, words, scales, FP8X4, packed_planes, empty)
+
+        def term_tiles(name, count, tag):
+            terms = tile([P, count * T], F32, name, tag)
+            return [terms[:, i * T : (i + 1) * T] for i in range(count)]
 
         def fetch_gated(results, r, term, t0=0, t1=T):
             nc.vector.tensor_tensor(
@@ -223,9 +240,8 @@ def tile_moe_qkv_kernel(
         def fetch_plain(results, r, term, t0=0, t1=T):
             nc.scalar.activation(term[:, t0:t1], results[:].indirect(entries(pos_sb[r], t0, t1)), COPY)
 
-        def gate_term(r, term, t0=0, t1=T, plain=None):
-            source = term if plain is None else plain
-            nc.vector.tensor_tensor(term[:, t0:t1], source[:, t0:t1], gates[:, r * T + t0 : r * T + t1], MULT)
+        def gate_term(r, term, plain, t0=0, t1=T):
+            nc.vector.tensor_tensor(term[:, t0:t1], plain[:, t0:t1], gates[:, r * T + t0 : r * T + t1], MULT)
 
         def turn_into(turned, source, first, last):
             width = source.shape[1]
@@ -239,21 +255,23 @@ def tile_moe_qkv_kernel(
                     is_transpose=True,
                 )
 
-        def turn_terms(turned, terms, opens, closes):
+        def turn_terms(terms, b, pieces):
+            turned = [bank(b + h, t1 - t0) for h, (t0, t1) in enumerate(pieces)]
             for i, term in enumerate(terms):
-                for h in range(2):
-                    half = term[:, h * HALF : (h + 1) * HALF]
-                    turn_into(turned[h], half, opens and i == 0, closes and i == len(terms) - 1)
+                for h, (t0, t1) in enumerate(pieces):
+                    turn_into(turned[h], term[:, t0:t1], i == 0, i == len(terms) - 1)
+            return turned
 
-        def turn_back(name, turned, b, tag=None):
-            totals = []
-            summed = tile([P, T], F32, "%s_summed" % name, tag)
-            for h in range(2):
-                half = summed[:, h * HALF : (h + 1) * HALF]
-                nc.scalar.copy(half, turned[h][:])
-                total = bank(b + h, HALF)
-                turn_into(total, half, True, True)
-                totals.append(total)
+        def empty_turned(name, turned, pieces):
+            summed = tile([P, T], F32, "%s_summed" % name)
+            for h, (t0, t1) in enumerate(pieces):
+                nc.scalar.copy(summed[:, t0:t1], turned[h][:])
+            return [summed[:, t0:t1] for t0, t1 in pieces]
+
+        def turn_back(summed, banks):
+            totals = [bank(b, piece.shape[1]) for b, piece in zip(banks, summed)]
+            for total, piece in zip(totals, summed):
+                turn_into(total, piece, True, True)
             return totals
 
         def store(j, t0, t1, result):
@@ -265,76 +283,64 @@ def tile_moe_qkv_kernel(
                 nc.scalar.copy(result[:], totals[h][:])
                 store(j, h * HALF, (h + 1) * HALF, result[:])
 
-        def project_q(e0, e1, b):
-            for e in range(e0, e1):
-                project(q_slots, Q_ROWS, [e], b + e - e0, words_of(wq_word_sb), scales_of(wq_scale_sb), FP4X4, low_planes)
-
-        def project_v(e0, e1, b):
-            for e in range(e0, e1, 2):
-                words, scales = words_of(wv_word_sb), words_of(wv_scale_sb)
-                project(v_slots, V_ROWS, [e, e + 1], b + (e - e0) // 2, words, scales, FP8X4, packed_planes)
-
-        q_slots = tile([P, SLOTS], F32, "q_slots")
-        for e0, e1 in WV_LOADS[:-1]:
-            round_wv(e0, e1, nc.scalar.copy)
-        quantize_wv(0)
-        gather_group(4, WORD_CHUNKS[1:2], "rounded0")
-        quantize_wv(4)
-        gather_group(8, WORD_CHUNKS[2:], "rounded4")
-        v_slots = tile([P, SLOTS], F32, "v_slots", "raw10")
-        project_v(0, EARLY, 0)
-        project_q(*WQ_LOADS[0], 4)
-        project_q(*WQ_LOADS[1], 0)
-        project_q(*WQ_LOADS[2], 4)
-        quantize_wv(QUANT[2][0])
-        round_wv(*WV_LOADS[-1], nc.vector.tensor_copy)
-        quantize_wv(QUANT[3][0])
-        q_plain = [tile([P, T], F32, "q_plain0", "raw2")[:], None]
-        q_gated = tile([P, 2 * T], F32, "q_gated", "rounded10")
-        q_terms = [None, None, q_gated[:, 0:T], q_gated[:, T:]]
-        fetch_plain(q_slots, 0, q_plain[0])
-        for r in (2, 3):
-            fetch_gated(q_slots, r, q_terms[r])
-        project_v(EARLY, E, 4)
-        q_plain[1] = tile([P, T], F32, "q_plain1", "wv_word_sb%d" % QUANT[-1][0])[:]
-        fetch_plain(q_slots, 1, q_plain[1])
-        v_terms = term_tiles("v", ("raw4", "raw6"))
-        fetch_plain(v_slots, 0, v_terms[0])
-        for r in (1, 2, 3):
-            fetch_gated(v_slots, r, v_terms[r])
-        gate_term(0, v_terms[0])
-        q_turned = [bank(6 + h, HALF) for h in range(2)]
-        turn_terms(q_turned, q_terms[2:], True, False)
-        k_slots = tile([P, SLOTS], F32, "k_slots")
-        for e in range(0, E, 2):
-            project(k_slots, K_ROWS, [e, e + 1], e // 2, words_of(wk_word_sb), scales_of(wk_scale_sb), FP8X4, packed_planes)
-        q_late = tile([P, 2 * T], F32, "q_late", "wk_word_sb%d" % WK_LOADS[-1][0])
-        q_terms[:2] = [q_late[:, 0:T], q_late[:, T:]]
-        for r in (0, 1):
-            gate_term(r, q_terms[r], plain=q_plain[r])
-        turn_terms(q_turned, q_terms[:2], False, True)
-        k_terms = term_tiles("k", ("raw0", "raw8"))
-        fetch_plain(k_slots, 0, k_terms[0])
-        fetch_plain(k_slots, 2, k_terms[2], 0, HALF)
-        fetch_plain(k_slots, 1, k_terms[1])
-        fetch_gated(k_slots, 3, k_terms[3])
-        fetch_gated(k_slots, 2, k_terms[2], HALF, T)
-        v_turned = [bank(4 + h, HALF) for h in range(2)]
-        turn_terms(v_turned, [v_terms[r] for r in (1, 2, 3, 0)], True, True)
-        q_totals = turn_back("q", q_turned, 6)
-        v_totals = turn_back("v", v_turned, 0)
-        finish(Q_ROWS, "q", q_totals)
-        finish(V_ROWS, "v", v_totals)
-
         def add_into(total, term):
             nc.vector.tensor_tensor(total, total, term, ADD)
 
-        gate_term(0, k_terms[0])
-        gate_term(2, k_terms[2], 0, HALF)
-        add_into(k_terms[0], k_terms[3])
-        gate_term(1, k_terms[1], *LAST_PIECES[0])
-        add_into(k_terms[0], k_terms[2])
-        gate_term(1, k_terms[1], *LAST_PIECES[1])
+        for e0, e1 in PAIRS:
+            round_wv(e0, e1)
+        quantize_wv(0)
+        gather_words(4, 8, "raw2")
+        quantize_wv(4)
+        quantize_wv(8)
+        gather_words(8, 11, "raw8")
+        quantize_wv(10)
+        gather_words(11, 12, "raw10")
+        v_slots = tile([P, SLOTS], F32, "v_slots", "raw6")
+        for e in range(0, 8, 2):
+            project_v([e, e + 1], e // 2, empty_on_scalar)
+        q_slots = tile([P, SLOTS], F32, "q_slots")
+        for e in range(0, 8, 2):
+            project_q([e, e + 1], 4 + e // 2)
+        project_v([8, 9], 4, empty_on_scalar)
+        project_v([10], 5, empty_on_vector)
+        project_q([8, 9], 0)
+        project_q([10], 1)
+        project_v([11], 6, empty_on_vector)
+        v_terms = term_tiles("v_plain", 1, "raw0") + term_tiles("v_terms", 2, "raw4") + term_tiles("v_last", 1, "rounded0")
+        fetch_plain(v_slots, 0, v_terms[0])
+        for r in (1, 2, 3):
+            fetch_gated(v_slots, r, v_terms[r])
+        gate_term(0, v_terms[0], v_terms[0])
+        project_q([11], 5)
+        k_slots = tile([P, SLOTS], F32, "k_slots")
+        q_terms = [None, None] + term_tiles("q_terms", 2, "rounded4")
+        for r in (2, 3):
+            fetch_gated(q_slots, r, q_terms[r])
+        for g, (e0, e1) in enumerate(GROUPS):
+            for e in range(e0, e1, 2):
+                project_k([e, e + 1], 6 + e // 2)
+            if g < 2:
+                q_terms[g] = term_tiles("q_plain%d" % g, 1, "wk_word_sb%d" % e0)[0]
+                fetch_plain(q_slots, g, q_terms[g])
+        for r in (0, 1):
+            gate_term(r, q_terms[r], q_terms[r])
+        v_turned = turn_terms([v_terms[r] for r in (1, 2, 3, 0)], 6, HALVES)
+        v_totals = turn_back(empty_turned("v", v_turned, HALVES), (4, 5))
+        q_turned = turn_terms([q_terms[r] for r in (2, 3, 0, 1)], 0, HALVES)
+        k_terms = term_tiles("k_plain", 2, "raw0") + term_tiles("k_gated", 1, "raw8") + term_tiles("k_last", 1, "wk_word_sb4")
+        fetch_plain(k_slots, 0, k_terms[0])
+        fetch_plain(k_slots, 1, k_terms[1])
+        fetch_gated(k_slots, 2, k_terms[2])
+        gate_term(0, k_terms[0], k_terms[0])
         for t0, t1 in LAST_PIECES:
-            add_into(k_terms[1][:, t0:t1], k_terms[0][:, t0:t1])
-            store(K_ROWS, t0, t1, k_terms[1][:, t0:t1])
+            gate_term(1, k_terms[1], k_terms[1], t0, t1)
+        k_turned = turn_terms([k_terms[r] for r in (2, 0, 1)], 2, LAST_PIECES)
+        q_summed = empty_turned("q", q_turned, HALVES)
+        finish(V_ROWS, "v", v_totals)
+        finish(Q_ROWS, "q", turn_back(q_summed, (6, 7)))
+        k_totals = turn_back(empty_turned("k", k_turned, LAST_PIECES), (0, 1))
+        for t0, t1 in LAST_PIECES:
+            fetch_gated(k_slots, 3, k_terms[3], t0, t1)
+        for h, (t0, t1) in enumerate(LAST_PIECES):
+            add_into(k_terms[3][:, t0:t1], k_totals[h][:])
+            store(K_ROWS, t0, t1, k_terms[3][:, t0:t1])

@@ -35,8 +35,7 @@ HALVES = ((0, HALF), (HALF, T))
 LAST_PIECES = ((0, BANK), (BANK, T))
 SCALE_CHUNKS = ((0, 6), (6, 12))
 GROUPS = ((0, 4), (4, 8), (8, 12))
-QUANT = ((0, 4), (4, 8), (8, 10), (10, 12))
-PAIRS = tuple((e, e + 2) for e in range(0, E, 2))
+WV_LOADS = ((0, 2),) + tuple((e, e + 1) for e in range(2, E))
 Q_ROWS, K_ROWS, V_ROWS = 0, 1, 2
 
 
@@ -60,12 +59,12 @@ def tile_moe_qkv_kernel(
         slot_scales_low = tile([P, SLOTS], U8, "slot_scales_low")
         wq_word_sb = {e0: tile([P, PASSES * (e1 - e0), 2 * N], U8, "wq_word_sb%d" % e0) for e0, e1 in GROUPS}
         wk_word_sb = {e0: tile([P, PASSES * (e1 - e0), N], I32, "wk_word_sb%d" % e0) for e0, e1 in GROUPS}
-        wv_word_sb = {e0: tile([P, PASSES * (e1 - e0), N], U32, "wv_word_sb%d" % e0) for e0, e1 in QUANT}
+        wv_word_sb = {e0: tile([P, PASSES * (e1 - e0), N], U32, "wv_word_sb%d" % e0) for e0, e1 in GROUPS}
         wq_scale_sb = tile([P, E * PASSES, N], U8, "wq_scale_sb")
         wk_scale_sb = tile([P, E * PASSES, N], U8, "wk_scale_sb")
-        wv_scale_sb = {e0: tile([P, PASSES * (e1 - e0), N], U8, "wv_scale_sb%d" % e0) for e0, e1 in QUANT}
-        raw = {e0: tile([P, (e1 - e0) * W_ROW], F32, "raw%d" % e0) for e0, e1 in PAIRS}
-        rounded = {e0: tile([P, (e1 - e0) * W_ROW], BF16, "rounded%d" % e0) for e0, e1 in QUANT}
+        wv_scale_sb = {e0: tile([P, PASSES * (e1 - e0), N], U8, "wv_scale_sb%d" % e0) for e0, e1 in GROUPS}
+        raw = {e0: tile([P, (e1 - e0) * W_ROW], F32, "raw%d" % e0) for e0, e1 in WV_LOADS}
+        rounded = {e0: tile([P, (e1 - e0) * W_ROW], BF16, "rounded%d" % e0) for e0, e1 in GROUPS}
         gate_cols = tile([P, GATE_COLS], F32, "gate_cols")
         gates = tile([P, TOP * T], F32, "gates")
         bias_sb = tile([P, 3, E], F32, "bias_sb")
@@ -102,19 +101,19 @@ def tile_moe_qkv_kernel(
         def load_pos(r):
             nc.sync.dma_start(pos_sb[r][:], (pos1, pos2, pos3, pos4)[r])
 
+        nc.scalar.dma_start(out=gate_cols[:], in_=gate[:, 0].rearrange("r (c i) -> c r i", i=GATE_COLS))
         nc.sync.dma_start(offs_sb[:], offs)
         for q in range(4):
             nc.sync.dma_start(
                 out=x_scale_sb[32 * q : 32 * q + 8, 0:T].bitcast(I32), in_=x_scales[:, 4 * q : 4 * q + 4].bitcast(I32)
             )
-        nc.sync.dma_start(out=gate_cols[:], in_=gate[:, 0].rearrange("r (c i) -> c r i", i=GATE_COLS))
-        load_wv(*PAIRS[0])
+        load_wv(*WV_LOADS[0])
         nc.sync.dma_start(
             out=x_word_sb[:, 0 : PASSES * T].rearrange("p (s t) -> p s t", s=PASSES),
             in_=x_words.rearrange("s p t d -> p s (t d)").bitcast(I32),
         )
         nc.sync.dma_start(out=bias_sb[:], in_=bias.rearrange("(j p) e -> p j e", p=P))
-        for e0, e1 in PAIRS[1:]:
+        for e0, e1 in WV_LOADS[1:]:
             load_wv(e0, e1)
         load_weight_scales(wq_scale_sb, wq_scales)
 
@@ -127,20 +126,19 @@ def tile_moe_qkv_kernel(
             )
 
         def words_at(e, s):
-            first = max(g for g in slot_words if g <= e)
-            width = slot_words[first].shape[1] // PASSES
-            return slot_words[first][:, s * width + (e - first) * C : s * width + (e - first + 1) * C]
+            return slot_words[e, s]
 
-        def gather_words(e0, e1, tag=None):
-            width = (e1 - e0) * C
-            slot_words[e0] = tile([P, PASSES * width], U32, "slot_words%d" % e0, tag)
-            for s in range(PASSES):
+        def gather_words(name, steps, tag=None):
+            words = tile([P, sum(e1 - e0 for e0, e1, s in steps) * C], U32, name, tag)
+            c0 = 0
+            for e0, e1, s in steps:
                 window = x_word_sb[:, s * T : s * T + WORD_WINDOW].bitcast(U32)
-                nc.vector.tensor_copy(
-                    slot_words[e0][:, s * width : (s + 1) * width], window.indirect(entries(offs_sb, e0 * C, e1 * C))
-                )
+                c1 = c0 + (e1 - e0) * C
+                nc.vector.tensor_copy(words[:, c0:c1], window.indirect(entries(offs_sb, e0 * C, e1 * C)))
+                slot_words.update({(e, s): words[:, c0 + (e - e0) * C : c0 + (e - e0 + 1) * C] for e in range(e0, e1)})
+                c0 = c1
 
-        gather_words(0, 4)
+        gather_words("first_words", ((0, 4, 0), (0, 4, 1)))
         for j in range(4):
             nc.sync.dma_start(out=slot_scales_low[j:P:32].bitcast(I32), in_=slot_scales[4 + j : P : 32].bitcast(I32))
         load_pos(0)
@@ -168,7 +166,7 @@ def tile_moe_qkv_kernel(
             )
 
         def round_wv(e0, e1):
-            g0 = max(g for g, g1 in QUANT if g <= e0)
+            g0 = max(g for g, g1 in GROUPS if g <= e0)
             part = rounded[g0][:, (e0 - g0) * W_ROW : (e1 - g0) * W_ROW]
             nc.scalar.copy(
                 part.rearrange("p (g c i j) -> p g c j i", c=N // 4, i=4, j=PACK),
@@ -182,28 +180,27 @@ def tile_moe_qkv_kernel(
                 in_=rounded[e0][:],
             )
 
-        def empty_on_scalar(result, acc, column):
-            nc.scalar.activation(result, acc, IDENTITY, bias=column)
-
-        def empty_on_vector(result, acc, column):
-            nc.vector.tensor_scalar(result, acc, column, None, ADD)
-
-        def project(results, j, experts, b, words, scales, dtype, token_scales, empty=empty_on_scalar):
-            acc = bank(b, len(experts) * C)
-            for i, e in enumerate(experts):
-                slots = slice(e * C, (e + 1) * C)
-                for s in range(PASSES):
-                    nc.tensor.matmul_mx(
-                        out=acc[:, i * C : (i + 1) * C],
-                        lhsT=words(e)[:, s].bitcast(dtype),
-                        lhsT_scale=scales(e)[:, s],
-                        rhs=words_at(e, s).bitcast(FP8X4),
-                        rhs_scale=token_scales[s][:, slots],
-                        start=(s == 0),
-                        stop=(s == PASSES - 1),
-                    )
-            for i, e in enumerate(experts):
-                empty(results[:, e * C : (e + 1) * C], acc[:, i * C : (i + 1) * C], bias_sb[:, j, e : e + 1])
+        def project(results, j, experts, banks, words, scales, dtype, token_scales):
+            if len(banks) == 1:
+                shared = bank(banks[0], len(experts) * C)
+                accs = [shared[:, i * C : (i + 1) * C] for i in range(len(experts))]
+                steps = [(i, s) for i in range(len(experts)) for s in range(PASSES)]
+            else:
+                accs = [bank(b, C)[:] for b in banks]
+                steps = [(i, s) for s in range(PASSES) for i in range(len(experts))]
+            for i, s in steps:
+                e = experts[i]
+                nc.tensor.matmul_mx(
+                    out=accs[i],
+                    lhsT=words(e)[:, s].bitcast(dtype),
+                    lhsT_scale=scales(e)[:, s],
+                    rhs=words_at(e, s).bitcast(FP8X4),
+                    rhs_scale=token_scales[s][:, e * C : (e + 1) * C],
+                    start=(s == 0),
+                    stop=(s == PASSES - 1),
+                )
+            for acc, e in zip(accs, experts):
+                nc.scalar.activation(results[:, e * C : (e + 1) * C], acc, IDENTITY, bias=bias_sb[:, j, e : e + 1])
 
         def words_of(pieces):
             def words(e):
@@ -218,15 +215,15 @@ def tile_moe_qkv_kernel(
         packed_planes = (slot_scales[:], slot_scales[4:P])
         low_planes = (slot_scales[:], slot_scales_low[:])
 
-        def project_q(experts, b):
+        def project_q(experts, *b):
             project(q_slots, Q_ROWS, experts, b, words_of(wq_word_sb), scales_of(wq_scale_sb), FP4X4, low_planes)
 
-        def project_k(experts, b):
+        def project_k(experts, *b):
             project(k_slots, K_ROWS, experts, b, words_of(wk_word_sb), scales_of(wk_scale_sb), FP8X4, packed_planes)
 
-        def project_v(experts, b, empty):
+        def project_v(experts, *b):
             words, scales = words_of(wv_word_sb), words_of(wv_scale_sb)
-            project(v_slots, V_ROWS, experts, b, words, scales, FP8X4, packed_planes, empty)
+            project(v_slots, V_ROWS, experts, b, words, scales, FP8X4, packed_planes)
 
         def term_tiles(name, count, tag):
             terms = tile([P, count * T], F32, name, tag)
@@ -255,8 +252,8 @@ def tile_moe_qkv_kernel(
                     is_transpose=True,
                 )
 
-        def turn_terms(terms, b, pieces):
-            turned = [bank(b + h, t1 - t0) for h, (t0, t1) in enumerate(pieces)]
+        def turn_terms(terms, banks, pieces):
+            turned = [bank(b, t1 - t0) for b, (t0, t1) in zip(banks, pieces)]
             for i, term in enumerate(terms):
                 for h, (t0, t1) in enumerate(pieces):
                     turn_into(turned[h], term[:, t0:t1], i == 0, i == len(terms) - 1)
@@ -286,58 +283,55 @@ def tile_moe_qkv_kernel(
         def add_into(total, term):
             nc.vector.tensor_tensor(total, total, term, ADD)
 
-        for e0, e1 in PAIRS:
+        for e0, e1 in WV_LOADS:
             round_wv(e0, e1)
         quantize_wv(0)
-        gather_words(4, 8, "raw2")
+        gather_words("second_words", ((4, 8, 0),), "raw3")
         quantize_wv(4)
+        gather_words("third_words", ((4, 8, 1), (8, 11, 0), (8, 11, 1), (11, 12, 0), (11, 12, 1)), "raw7")
         quantize_wv(8)
-        gather_words(8, 11, "raw8")
-        quantize_wv(10)
-        gather_words(11, 12, "raw10")
-        v_slots = tile([P, SLOTS], F32, "v_slots", "raw6")
-        for e in range(0, 8, 2):
-            project_v([e, e + 1], e // 2, empty_on_scalar)
+        v_slots = tile([P, SLOTS], F32, "v_slots", "raw8")
+        project_v([0, 1], 0)
+        project_v([2, 3], 1)
+        project_v([4, 5, 6, 7], 2, 3, 4, 5)
         q_slots = tile([P, SLOTS], F32, "q_slots")
         for e in range(0, 8, 2):
-            project_q([e, e + 1], 4 + e // 2)
-        project_v([8, 9], 4, empty_on_scalar)
-        project_v([10], 5, empty_on_vector)
-        project_q([8, 9], 0)
-        project_q([10], 1)
-        project_v([11], 6, empty_on_vector)
-        v_terms = term_tiles("v_plain", 1, "raw0") + term_tiles("v_terms", 2, "raw4") + term_tiles("v_last", 1, "rounded0")
-        fetch_plain(v_slots, 0, v_terms[0])
-        for r in (1, 2, 3):
-            fetch_gated(v_slots, r, v_terms[r])
-        gate_term(0, v_terms[0], v_terms[0])
+            project_q([e, e + 1], 6 + e // 2)
+        project_q([8, 9, 10], 2, 3, 4)
         project_q([11], 5)
-        k_slots = tile([P, SLOTS], F32, "k_slots")
-        q_terms = [None, None] + term_tiles("q_terms", 2, "rounded4")
-        for r in (2, 3):
+        q_terms = term_tiles("q_plain", 1, "raw0") + term_tiles("q_terms", 2, "raw4") + term_tiles("q_last", 1, "rounded0")
+        fetch_plain(q_slots, 0, q_terms[0])
+        for r in (1, 2, 3):
             fetch_gated(q_slots, r, q_terms[r])
+        gate_term(0, q_terms[0], q_terms[0])
+        project_v([8, 9], 5)
+        project_v([10, 11], 4)
+        k_slots = tile([P, SLOTS], F32, "k_slots")
+        v_terms = [None, None] + term_tiles("v_terms", 2, "rounded4")
+        for r in (2, 3):
+            fetch_gated(v_slots, r, v_terms[r])
         for g, (e0, e1) in enumerate(GROUPS):
             for e in range(e0, e1, 2):
                 project_k([e, e + 1], 6 + e // 2)
             if g < 2:
-                q_terms[g] = term_tiles("q_plain%d" % g, 1, "wk_word_sb%d" % e0)[0]
-                fetch_plain(q_slots, g, q_terms[g])
+                v_terms[g] = term_tiles("v_plain%d" % g, 1, "wk_word_sb%d" % e0)[0]
+                fetch_plain(v_slots, g, v_terms[g])
         for r in (0, 1):
-            gate_term(r, q_terms[r], q_terms[r])
-        v_turned = turn_terms([v_terms[r] for r in (1, 2, 3, 0)], 6, HALVES)
-        v_totals = turn_back(empty_turned("v", v_turned, HALVES), (4, 5))
-        q_turned = turn_terms([q_terms[r] for r in (2, 3, 0, 1)], 0, HALVES)
-        k_terms = term_tiles("k_plain", 2, "raw0") + term_tiles("k_gated", 1, "raw8") + term_tiles("k_last", 1, "wk_word_sb4")
+            gate_term(r, v_terms[r], v_terms[r])
+        q_turned = turn_terms([q_terms[r] for r in (1, 2, 3, 0)], (6, 7), HALVES)
+        q_totals = turn_back(empty_turned("q", q_turned, HALVES), (4, 5))
+        v_turned = turn_terms([v_terms[r] for r in (2, 3, 0, 1)], (0, 1), HALVES)
+        k_terms = term_tiles("k_plain", 2, "raw0") + term_tiles("k_gated", 1, "raw9") + term_tiles("k_last", 1, "wk_word_sb4")
         fetch_plain(k_slots, 0, k_terms[0])
         fetch_plain(k_slots, 1, k_terms[1])
         fetch_gated(k_slots, 2, k_terms[2])
         gate_term(0, k_terms[0], k_terms[0])
         for t0, t1 in LAST_PIECES:
             gate_term(1, k_terms[1], k_terms[1], t0, t1)
-        k_turned = turn_terms([k_terms[r] for r in (2, 0, 1)], 2, LAST_PIECES)
-        q_summed = empty_turned("q", q_turned, HALVES)
-        finish(V_ROWS, "v", v_totals)
-        finish(Q_ROWS, "q", turn_back(q_summed, (6, 7)))
+        k_turned = turn_terms([k_terms[r] for r in (2, 0, 1)], (2, 3), LAST_PIECES)
+        v_summed = empty_turned("v", v_turned, HALVES)
+        finish(Q_ROWS, "q", q_totals)
+        finish(V_ROWS, "v", turn_back(v_summed, (6, 7)))
         k_totals = turn_back(empty_turned("k", k_turned, LAST_PIECES), (0, 1))
         for t0, t1 in LAST_PIECES:
             fetch_gated(k_slots, 3, k_terms[3], t0, t1)

@@ -48,7 +48,7 @@ def tile_moe_qkv_kernel(
         psum = ctx.enter_context(tc.psum_pool(name="psum", bufs=1))
 
         def tile(shape, dtype, name, tag=None):
-            return keep.tile(shape, dtype, name=name, tag=tag or name, align_bytes=64)
+            return keep.tile(shape, dtype, name=name, tag=tag or name, align_bytes=256)
 
         offs_sb = keep.tile([P, SLOTS // LIST_ROWS], U16, name="offs_sb")
         pos_sb = [keep.tile([P, T // LIST_ROWS], U16, name="pos_sb%d" % r) for r in range(TOP)]

@@ -101,7 +101,7 @@ def tile_moe_qkv_kernel(
         def load_pos(r):
             nc.sync.dma_start(pos_sb[r][:], (pos1, pos2, pos3, pos4)[r])
 
-        nc.scalar.dma_start(out=gate_cols[:], in_=gate[:, 0].rearrange("r (c i) -> c r i", i=GATE_COLS))
+        nc.sync.dma_start(out=gate_cols[:], in_=gate[:, 0].rearrange("r (c i) -> c r i", i=GATE_COLS))
         nc.sync.dma_start(offs_sb[:], offs)
         for q in range(4):
             nc.sync.dma_start(

@@ -319,8 +319,9 @@ def tile_moe_qkv_kernel(
         for r in (0, 1):
             gate_term(r, v_terms[r], v_terms[r])
         q_turned = turn_terms([q_terms[r] for r in (1, 2, 3, 0)], (6, 7), HALVES)
-        q_totals = turn_back(empty_turned("q", q_turned, HALVES), (4, 5))
+        q_summed = empty_turned("q", q_turned, HALVES)
         v_turned = turn_terms([v_terms[r] for r in (2, 3, 0, 1)], (0, 1), HALVES)
+        q_totals = turn_back(q_summed, (4, 5))
         k_terms = term_tiles("k_plain", 2, "raw0") + term_tiles("k_gated", 1, "raw9") + term_tiles("k_last", 1, "wk_word_sb4")
         fetch_plain(k_slots, 0, k_terms[0])
         fetch_plain(k_slots, 1, k_terms[1])

@@ -31,6 +31,7 @@ BANK = 512
 W_ROW = PASSES * PACK * N
 GATE_COLS = TOP * T // P
 HALF = T // 2
+SHARE = 320
 HALVES = ((0, HALF), (HALF, T))
 LAST_PIECES = ((0, BANK), (BANK, T))
 SCALE_CHUNKS = ((0, 6), (6, 12))
@@ -252,11 +253,14 @@ def tile_moe_qkv_kernel(
                     is_transpose=True,
                 )
 
+        def turn_term(turned, term, pieces, opens, closes):
+            for piece, (t0, t1) in zip(turned, pieces):
+                turn_into(piece, term[:, t0:t1], opens, closes)
+
         def turn_terms(terms, banks, pieces):
             turned = [bank(b, t1 - t0) for b, (t0, t1) in zip(banks, pieces)]
             for i, term in enumerate(terms):
-                for h, (t0, t1) in enumerate(pieces):
-                    turn_into(turned[h], term[:, t0:t1], i == 0, i == len(terms) - 1)
+                turn_term(turned, term, pieces, i == 0, i == len(terms) - 1)
             return turned
 
         def empty_turned(name, turned, pieces):
@@ -274,11 +278,10 @@ def tile_moe_qkv_kernel(
         def store(j, t0, t1, result):
             nc.sync.dma_start(out=out[j * N : (j + 1) * N, t0:t1], in_=result)
 
-        def finish(j, name, totals):
-            for h in range(2):
-                result = tile([P, HALF], F32, "%s_result%d" % (name, h))
-                nc.scalar.copy(result[:], totals[h][:])
-                store(j, h * HALF, (h + 1) * HALF, result[:])
+        def finish(j, results, totals):
+            for result, total, (t0, t1) in zip(results, totals, HALVES):
+                nc.scalar.copy(result, total[:])
+                store(j, t0, t1, result)
 
         def add_into(total, term):
             nc.vector.tensor_tensor(total, total, term, ADD)
@@ -310,32 +313,47 @@ def tile_moe_qkv_kernel(
         v_terms = [None, None] + term_tiles("v_terms", 2, "rounded4")
         for r in (2, 3):
             fetch_gated(v_slots, r, v_terms[r])
-        for g, (e0, e1) in enumerate(GROUPS):
-            for e in range(e0, e1, 2):
-                project_k([e, e + 1], 6 + e // 2)
-            if g < 2:
-                v_terms[g] = term_tiles("v_plain%d" % g, 1, "wk_word_sb%d" % e0)[0]
-                fetch_plain(v_slots, g, v_terms[g])
-        for r in (0, 1):
-            gate_term(r, v_terms[r], v_terms[r])
+        for e in range(0, 4, 2):
+            project_k([e, e + 1], 6 + e // 2)
+        v_terms[0] = term_tiles("v_plain0", 1, "wk_word_sb0")[0]
+        fetch_plain(v_slots, 0, v_terms[0])
+        for e in range(4, 8, 2):
+            project_k([e, e + 1], 6 + e // 2)
         q_turned = turn_terms([q_terms[r] for r in (1, 2, 3, 0)], (6, 7), HALVES)
         q_summed = empty_turned("q", q_turned, HALVES)
-        v_turned = turn_terms([v_terms[r] for r in (2, 3, 0, 1)], (0, 1), HALVES)
+        v_terms[1] = term_tiles("v_plain1", 1, "raw0")[0]
+        fetch_plain(v_slots, 1, v_terms[1])
+        for e in range(8, E, 2):
+            project_k([e, e + 1], 6 + e // 2)
+        for r in (0, 1):
+            gate_term(r, v_terms[r], v_terms[r])
         q_totals = turn_back(q_summed, (4, 5))
-        k_terms = term_tiles("k_plain", 2, "raw0") + term_tiles("k_gated", 1, "raw9") + term_tiles("k_last", 1, "wk_word_sb4")
+        v_turned = turn_terms([v_terms[r] for r in (2, 3, 0, 1)], (0, 1), HALVES)
+        k_terms = [term_tiles("k_term%d" % r, 1, tag)[0] for r, tag in enumerate(("raw2", "raw0", "raw9"))]
+        v_summed = [tile([P, HALF], F32, "v_summed%d" % h) for h in range(2)]
         fetch_plain(k_slots, 0, k_terms[0])
-        fetch_plain(k_slots, 1, k_terms[1])
+        nc.scalar.copy(v_summed[0][:], v_turned[0][:])
+        fetch_plain(k_slots, 1, k_terms[1], SHARE, T)
+        nc.scalar.copy(v_summed[1][:], v_turned[1][:])
         fetch_gated(k_slots, 2, k_terms[2])
         gate_term(0, k_terms[0], k_terms[0])
-        for t0, t1 in LAST_PIECES:
-            gate_term(1, k_terms[1], k_terms[1], t0, t1)
-        k_turned = turn_terms([k_terms[r] for r in (2, 0, 1)], (2, 3), LAST_PIECES)
-        v_summed = empty_turned("v", v_turned, HALVES)
-        finish(Q_ROWS, "q", q_totals)
-        finish(V_ROWS, "v", turn_back(v_summed, (6, 7)))
+        fetch_gated(k_slots, 1, k_terms[1], 0, SHARE)
+        gate_term(1, k_terms[1], k_terms[1], SHARE, BANK)
+        gate_term(1, k_terms[1], k_terms[1], BANK, T)
+        k_turned = [bank(2 + h, t1 - t0) for h, (t0, t1) in enumerate(LAST_PIECES)]
+        turn_term(k_turned, k_terms[2], LAST_PIECES, True, False)
+        v_totals = turn_back([v_summed[0][:]], (6,))
+        turn_term(k_turned, k_terms[0], LAST_PIECES, False, False)
+        turn_term(k_turned, k_terms[1], LAST_PIECES, False, True)
+        v_totals = v_totals + turn_back([v_summed[1][:]], (7,))
+        q_result = tile([P, T], F32, "q_result", "raw9")
+        finish(Q_ROWS, [q_result[:, t0:t1] for t0, t1 in HALVES], q_totals)
         k_totals = turn_back(empty_turned("k", k_turned, LAST_PIECES), (0, 1))
+        v_results = [tile([P, HALF], F32, "v_result%d" % h, tag)[:] for h, tag in enumerate((None, "raw0"))]
+        finish(V_ROWS, v_results, v_totals)
+        k_last = term_tiles("k_last", 1, "v_summed0")[0]
         for t0, t1 in LAST_PIECES:
-            fetch_gated(k_slots, 3, k_terms[3], t0, t1)
+            fetch_gated(k_slots, 3, k_last, t0, t1)
         for h, (t0, t1) in enumerate(LAST_PIECES):
-            add_into(k_terms[3][:, t0:t1], k_totals[h][:])
-            store(K_ROWS, t0, t1, k_terms[3][:, t0:t1])
+            add_into(k_last[:, t0:t1], k_totals[h][:])
+            store(K_ROWS, t0, t1, k_last[:, t0:t1])

from contextlib import ExitStack

import concourse.mybir as mybir
from concourse.masks import make_identity

K, T, E, C, N, TOP = 1024, 768, 12, 256, 128, 4
FLOPS = 2 * E * C * K * 3 * N

F32 = mybir.dt.float32
BF16 = mybir.dt.bfloat16
I32 = mybir.dt.int32
U32 = mybir.dt.uint32
U16 = mybir.dt.uint16
U8 = mybir.dt.uint8
FP8X4 = mybir.dt.float8_e4m3fn_x4
FP4X4 = mybir.dt.float4_e2m1fn_x4
MULT = mybir.AluOpType.mult
ADD = mybir.AluOpType.add
IDENTITY = mybir.ActivationFunctionType.Identity
COPY = mybir.ActivationFunctionType.Copy

P = 128
PACK = 4
PASSES = K // (P * PACK)
SLOTS = E * C
LIST_ROWS = 16
SCALE_WINDOW = 2048
WORD_WINDOW = 1408
BANKS = 8
BANK = 512
W_ROW = PASSES * PACK * N
GATE_COLS = TOP * T // P
HALF = T // 2
SHARE = 320
HALVES = ((0, HALF), (HALF, T))
LAST_PIECES = ((0, BANK), (BANK, T))
SCALE_CHUNKS = ((0, 6), (6, 12))
GROUPS = ((0, 4), (4, 8), (8, 12))
WV_LOADS = ((0, 2),) + tuple((e, e + 1) for e in range(2, E))
Q_ROWS, K_ROWS, V_ROWS = 0, 1, 2


def tile_moe_qkv_kernel(
    tc, x_words, x_scales, wq_words, wq_scales, wk_words, wk_scales, wv, bias, gate, offs, pos1, pos2, pos3, pos4, out
):
    nc = tc.nc
    with ExitStack() as ctx:
        keep = ctx.enter_context(tc.tile_pool(name="keep", bufs=1))
        psum = ctx.enter_context(tc.psum_pool(name="psum", bufs=1))

        def tile(shape, dtype, name, tag=None):
            return keep.tile(shape, dtype, name=name, tag=tag or name, align_bytes=256)

        offs_sb = keep.tile([P, SLOTS // LIST_ROWS], U16, name="offs_sb")
        pos_sb = [keep.tile([P, T // LIST_ROWS], U16, name="pos_sb%d" % r) for r in range(TOP)]
        x_scale_sb = tile([P, SCALE_WINDOW], U8, "x_scale_sb")
        x_word_sb = tile([P, T + WORD_WINDOW], I32, "x_word_sb")
        slot_words = {}
        slot_scales = tile([P, SLOTS], U8, "slot_scales")
        slot_scales_low = tile([P, SLOTS], U8, "slot_scales_low")
        wq_word_sb = {e0: tile([P, PASSES * (e1 - e0), 2 * N], U8, "wq_word_sb%d" % e0) for e0, e1 in GROUPS}
        wk_word_sb = {e0: tile([P, PASSES * (e1 - e0), N], I32, "wk_word_sb%d" % e0) for e0, e1 in GROUPS}
        wv_word_sb = {e0: tile([P, PASSES * (e1 - e0), N], U32, "wv_word_sb%d" % e0) for e0, e1 in GROUPS}
        wq_scale_sb = tile([P, E * PASSES, N], U8, "wq_scale_sb")
        wk_scale_sb = tile([P, E * PASSES, N], U8, "wk_scale_sb")
        wv_scale_sb = {e0: tile([P, PASSES * (e1 - e0), N], U8, "wv_scale_sb%d" % e0) for e0, e1 in GROUPS}
        raw = {e0: tile([P, (e1 - e0) * W_ROW], F32, "raw%d" % e0) for e0, e1 in WV_LOADS}
        rounded = {e0: tile([P, (e1 - e0) * W_ROW], BF16, "rounded%d" % e0) for e0, e1 in GROUPS}
        gate_cols = tile([P, GATE_COLS], F32, "gate_cols")
        gates = tile([P, TOP * T], F32, "gates")
        bias_sb = tile([P, 3, E], F32, "bias_sb")
        ident = tile([P, P], F32, "ident")

        nc.gpsimd.memset(x_scale_sb[:, 0:T].bitcast(I32), 0)
        make_identity(nc, ident[:])
        nc.vector.memset(x_scale_sb[:, T:].bitcast(I32), 0)
        nc.vector.memset(x_word_sb[:, PASSES * T :], 0)
        nc.vector.memset(slot_scales_low[:].bitcast(I32), 0)
        nc.gpsimd.memset(wq_scale_sb[:].rearrange("p g n -> p (g n)").bitcast(I32), 0)
        nc.gpsimd.memset(wk_scale_sb[:].rearrange("p g n -> p (g n)").bitcast(I32), 0)

        def load_wv(e0, e1):
            rows = wv.rearrange("e (s p j) n -> p (e s) (j n)", s=PASSES, j=PACK)
            nc.sync.dma_start(
                out=raw[e0][:].rearrange("p (g c) -> p g c", c=PACK * N),
                in_=rows[:, PASSES * e0 : PASSES * e1],
            )

        def load_weight_scales(plane, scales):
            rows = scales.rearrange("e s (q j) n -> j q (e s) n", j=4)
            for j in range(4):
                nc.sync.dma_start(out=plane[j:P:32].bitcast(I32), in_=rows[j].bitcast(I32))

        def load_wq(e0, e1):
            rows = wq_words.rearrange("e s p b -> p (e s) b").bitcast(I32)
            nc.sync.dma_start(out=wq_word_sb[e0][:].bitcast(I32), in_=rows[:, PASSES * e0 : PASSES * e1])

        def load_wk(e0, e1):
            rows = wk_words.rearrange("e s p n d -> p (e s) (n d)").bitcast(I32)
            nc.sync.dma_start(out=wk_word_sb[e0][:], in_=rows[:, PASSES * e0 : PASSES * e1])

        def load_pos(r):
            nc.sync.dma_start(pos_sb[r][:], (pos1, pos2, pos3, pos4)[r])

        nc.sync.dma_start(out=gate_cols[:], in_=gate[:, 0].rearrange("r (c i) -> c r i", i=GATE_COLS))
        nc.sync.dma_start(offs_sb[:], offs)
        for q in range(4):
            nc.sync.dma_start(
                out=x_scale_sb[32 * q : 32 * q + 8, 0:T].bitcast(I32), in_=x_scales[:, 4 * q : 4 * q + 4].bitcast(I32)
            )
        load_wv(*WV_LOADS[0])
        nc.sync.dma_start(
            out=x_word_sb[:, 0 : PASSES * T].rearrange("p (s t) -> p s t", s=PASSES),
            in_=x_words.rearrange("s p t d -> p s (t d)").bitcast(I32),
        )
        nc.sync.dma_start(out=bias_sb[:], in_=bias.rearrange("(j p) e -> p j e", p=P))
        for e0, e1 in WV_LOADS[1:]:
            load_wv(e0, e1)
        load_weight_scales(wq_scale_sb, wq_scales)

        def entries(list_tile, first, last):
            return list_tile[:, first // LIST_ROWS : last // LIST_ROWS]

        for e0, e1 in SCALE_CHUNKS:
            nc.vector.tensor_copy(
                slot_scales[:, e0 * C : e1 * C], x_scale_sb[:].indirect(entries(offs_sb, e0 * C, e1 * C))
            )

        def words_at(e, s):
            return slot_words[e, s]

        def gather_words(name, steps, tag=None):
            words = tile([P, sum(e1 - e0 for e0, e1, s in steps) * C], U32, name, tag)
            c0 = 0
            for e0, e1, s in steps:
                window = x_word_sb[:, s * T : s * T + WORD_WINDOW].bitcast(U32)
                c1 = c0 + (e1 - e0) * C
                nc.vector.tensor_copy(words[:, c0:c1], window.indirect(entries(offs_sb, e0 * C, e1 * C)))
                slot_words.update({(e, s): words[:, c0 + (e - e0) * C : c0 + (e - e0 + 1) * C] for e in range(e0, e1)})
                c0 = c1

        gather_words("first_words", ((0, 4, 0), (0, 4, 1)))
        for j in range(4):
            nc.sync.dma_start(out=slot_scales_low[j:P:32].bitcast(I32), in_=slot_scales[4 + j : P : 32].bitcast(I32))
        load_pos(0)
        load_wq(*GROUPS[0])
        load_wq(*GROUPS[1])
        load_wq(*GROUPS[2])
        for r in range(1, TOP):
            load_pos(r)
        load_weight_scales(wk_scale_sb, wk_scales)
        for e0, e1 in GROUPS:
            load_wk(e0, e1)

        def bank(b, width):
            return psum.tile([P, width], F32, name="bank%d" % (b % BANKS))

        per_bank = BANK // P
        for i0 in range(0, GATE_COLS, per_bank):
            spread = bank(i0 // per_bank, BANK)
            for i in range(per_bank):
                column = gate_cols[:, i0 + i : i0 + i + 1].to_broadcast([P, P])
                nc.tensor.transpose(spread[:, i * P : (i + 1) * P], column, ident[:])
            nc.scalar.copy(
                gates[:].rearrange("p (r c i) -> p r c i", r=TOP, i=GATE_COLS)[:, :, :, i0 : i0 + per_bank],
                spread[:].rearrange("p (i c r) -> p r c i", i=per_bank, r=TOP),
            )

        def round_wv(e0, e1):
            g0 = max(g for g, g1 in GROUPS if g <= e0)
            part = rounded[g0][:, (e0 - g0) * W_ROW : (e1 - g0) * W_ROW]
            nc.scalar.copy(
                part.rearrange("p (g c i j) -> p g c j i", c=N // 4, i=4, j=PACK),
                raw[e0][:].rearrange("p (g j c i) -> p g c j i", c=N // 4, i=4, j=PACK),
            )

        def quantize_wv(e0):
            nc.vector.quantize_mx(
                out=wv_word_sb[e0][:].rearrange("p g n -> p (g n)").bitcast(FP8X4),
                scales=wv_scale_sb[e0][:].rearrange("p g n -> p (g n)"),
                in_=rounded[e0][:],
            )

        def project(results, j, experts, banks, words, scales, dtype, token_scales):
            if len(banks) == 1:
                shared = bank(banks[0], len(experts) * C)
                accs = [shared[:, i * C : (i + 1) * C] for i in range(len(experts))]
                steps = [(i, s) for i in range(len(experts)) for s in range(PASSES)]
            else:
                accs = [bank(b, C)[:] for b in banks]
                steps = [(i, s) for s in range(PASSES) for i in range(len(experts))]
            for i, s in steps:
                e = experts[i]
                nc.tensor.matmul_mx(
                    out=accs[i],
                    lhsT=words(e)[:, s].bitcast(dtype),
                    lhsT_scale=scales(e)[:, s],
                    rhs=words_at(e, s).bitcast(FP8X4),
                    rhs_scale=token_scales[s][:, e * C : (e + 1) * C],
                    start=(s == 0),
                    stop=(s == PASSES - 1),
                )
            for acc, e in zip(accs, experts):
                nc.scalar.activation(results[:, e * C : (e + 1) * C], acc, IDENTITY, bias=bias_sb[:, j, e : e + 1])

        def words_of(pieces):
            def words(e):
                e0 = max(g for g in pieces if g <= e)
                return pieces[e0][:, PASSES * (e - e0) : PASSES * (e - e0 + 1)]

            return words

        def scales_of(plane):
            return words_of({0: plane})

        packed_planes = (slot_scales[:], slot_scales[4:P])
        low_planes = (slot_scales[:], slot_scales_low[:])

        def project_q(experts, *b):
            project(q_slots, Q_ROWS, experts, b, words_of(wq_word_sb), scales_of(wq_scale_sb), FP4X4, low_planes)

        def project_k(experts, *b):
            project(k_slots, K_ROWS, experts, b, words_of(wk_word_sb), scales_of(wk_scale_sb), FP8X4, packed_planes)

        def project_v(experts, *b):
            words, scales = words_of(wv_word_sb), words_of(wv_scale_sb)
            project(v_slots, V_ROWS, experts, b, words, scales, FP8X4, packed_planes)

        def term_tiles(name, count, tag):
            terms = tile([P, count * T], F32, name, tag)
            return [terms[:, i * T : (i + 1) * T] for i in range(count)]

        def fetch_gated(results, r, term, t0=0, t1=T):
            nc.vector.tensor_tensor(
                term[:, t0:t1], results[:].indirect(entries(pos_sb[r], t0, t1)), gates[:, r * T + t0 : r * T + t1], MULT
            )

        def fetch_plain(results, r, term, t0=0, t1=T):
            nc.scalar.activation(term[:, t0:t1], results[:].indirect(entries(pos_sb[r], t0, t1)), COPY)

        def gate_term(r, term, plain, t0=0, t1=T):
            nc.vector.tensor_tensor(term[:, t0:t1], plain[:, t0:t1], gates[:, r * T + t0 : r * T + t1], MULT)

        def turn_into(turned, source, first, last):
            width = source.shape[1]
            for c0 in range(0, width, P):
                nc.tensor.matmul(
                    turned[:, c0 : c0 + P],
                    source[:, c0 : c0 + P],
                    ident[:],
                    start=(first and c0 == 0),
                    stop=(last and c0 == width - P),
                    is_transpose=True,
                )

        def turn_term(turned, term, pieces, opens, closes):
            for piece, (t0, t1) in zip(turned, pieces):
                turn_into(piece, term[:, t0:t1], opens, closes)

        def turn_terms(terms, banks, pieces):
            turned = [bank(b, t1 - t0) for b, (t0, t1) in zip(banks, pieces)]
            for i, term in enumerate(terms):
                turn_term(turned, term, pieces, i == 0, i == len(terms) - 1)
            return turned

        def empty_turned(name, turned, pieces):
            summed = tile([P, T], F32, "%s_summed" % name)
            for h, (t0, t1) in enumerate(pieces):
                nc.scalar.copy(summed[:, t0:t1], turned[h][:])
            return [summed[:, t0:t1] for t0, t1 in pieces]

        def turn_back(summed, banks):
            totals = [bank(b, piece.shape[1]) for b, piece in zip(banks, summed)]
            for total, piece in zip(totals, summed):
                turn_into(total, piece, True, True)
            return totals

        def store(j, t0, t1, result):
            nc.sync.dma_start(out=out[j * N : (j + 1) * N, t0:t1], in_=result)

        def finish(j, results, totals):
            for result, total, (t0, t1) in zip(results, totals, HALVES):
                nc.scalar.copy(result, total[:])
                store(j, t0, t1, result)

        def add_into(total, term):
            nc.vector.tensor_tensor(total, total, term, ADD)

        for e0, e1 in WV_LOADS:
            round_wv(e0, e1)
        quantize_wv(0)
        gather_words("second_words", ((4, 8, 0),), "raw3")
        quantize_wv(4)
        gather_words("third_words", ((4, 8, 1), (8, 11, 0), (8, 11, 1), (11, 12, 0), (11, 12, 1)), "raw7")
        quantize_wv(8)
        v_slots = tile([P, SLOTS], F32, "v_slots", "raw8")
        project_v([0, 1], 0)
        project_v([2, 3], 1)
        project_v([4, 5, 6, 7], 2, 3, 4, 5)
        q_slots = tile([P, SLOTS], F32, "q_slots")
        for e in range(0, 8, 2):
            project_q([e, e + 1], 6 + e // 2)
        project_q([8, 9, 10], 2, 3, 4)
        project_q([11], 5)
        q_terms = term_tiles("q_plain", 1, "raw0") + term_tiles("q_terms", 2, "raw4") + term_tiles("q_last", 1, "rounded0")
        fetch_plain(q_slots, 0, q_terms[0])
        for r in (1, 2, 3):
            fetch_gated(q_slots, r, q_terms[r])
        gate_term(0, q_terms[0], q_terms[0])
        project_v([8, 9], 5)
        project_v([10, 11], 4)
        k_slots = tile([P, SLOTS], F32, "k_slots")
        v_terms = [None, None] + term_tiles("v_terms", 2, "rounded4")
        for r in (2, 3):
            fetch_gated(v_slots, r, v_terms[r])
        for e in range(0, 4, 2):
            project_k([e, e + 1], 6 + e // 2)
        v_terms[0] = term_tiles("v_plain0", 1, "wk_word_sb0")[0]
        fetch_plain(v_slots, 0, v_terms[0])
        for e in range(4, 8, 2):
            project_k([e, e + 1], 6 + e // 2)
        q_turned = turn_terms([q_terms[r] for r in (1, 2, 3, 0)], (6, 7), HALVES)
        q_summed = empty_turned("q", q_turned, HALVES)
        v_terms[1] = term_tiles("v_plain1", 1, "raw0")[0]
        fetch_plain(v_slots, 1, v_terms[1])
        for e in range(8, E, 2):
            project_k([e, e + 1], 6 + e // 2)
        for r in (0, 1):
            gate_term(r, v_terms[r], v_terms[r])
        q_totals = turn_back(q_summed, (4, 5))
        v_turned = turn_terms([v_terms[r] for r in (2, 3, 0, 1)], (0, 1), HALVES)
        k_terms = [term_tiles("k_term%d" % r, 1, tag)[0] for r, tag in enumerate(("raw2", "raw0", "raw9"))]
        v_summed = [tile([P, HALF], F32, "v_summed%d" % h) for h in range(2)]
        fetch_plain(k_slots, 0, k_terms[0])
        nc.scalar.copy(v_summed[0][:], v_turned[0][:])
        fetch_plain(k_slots, 1, k_terms[1], SHARE, T)
        nc.scalar.copy(v_summed[1][:], v_turned[1][:])
        fetch_gated(k_slots, 2, k_terms[2])
        gate_term(0, k_terms[0], k_terms[0])
        fetch_gated(k_slots, 1, k_terms[1], 0, SHARE)
        gate_term(1, k_terms[1], k_terms[1], SHARE, BANK)
        gate_term(1, k_terms[1], k_terms[1], BANK, T)
        k_turned = [bank(2 + h, t1 - t0) for h, (t0, t1) in enumerate(LAST_PIECES)]
        turn_term(k_turned, k_terms[2], LAST_PIECES, True, False)
        v_totals = turn_back([v_summed[0][:]], (6,))
        turn_term(k_turned, k_terms[0], LAST_PIECES, False, False)
        turn_term(k_turned, k_terms[1], LAST_PIECES, False, True)
        v_totals = v_totals + turn_back([v_summed[1][:]], (7,))
        q_result = tile([P, T], F32, "q_result", "raw9")
        finish(Q_ROWS, [q_result[:, t0:t1] for t0, t1 in HALVES], q_totals)
        k_totals = turn_back(empty_turned("k", k_turned, LAST_PIECES), (0, 1))
        v_results = [tile([P, HALF], F32, "v_result%d" % h, tag)[:] for h, tag in enumerate((None, "raw0"))]
        finish(V_ROWS, v_results, v_totals)
        k_last = term_tiles("k_last", 1, "v_summed0")[0]
        for t0, t1 in LAST_PIECES:
            fetch_gated(k_slots, 3, k_last, t0, t1)
        for h, (t0, t1) in enumerate(LAST_PIECES):
            add_into(k_last[:, t0:t1], k_totals[h][:])
            store(K_ROWS, t0, t1, k_last[:, t0:t1])
